import numpy as np
import ml_dtypes


def mxq(x, axis, fmt="e4m3"):
    dtype, down = {"e4m3": (ml_dtypes.float8_e4m3fn, 7), "e5m2": (ml_dtypes.float8_e5m2, 14)}[fmt]
    v = np.moveaxis(np.asarray(x, np.float32).astype(ml_dtypes.bfloat16).astype(np.float64), axis, -1)
    blocks = v.reshape(v.shape[:-1] + (-1, 32))
    amax = np.abs(blocks).max(-1, keepdims=True)
    byte = np.maximum(np.where(amax > 0, np.frexp(amax)[1] - 1 + 127, 0) - down, 1)
    scale = np.exp2(byte - 127.0)
    codes = (blocks / scale).astype(np.float32).astype(dtype).astype(np.float64)
    return np.moveaxis((codes * scale).reshape(v.shape), -1, axis)


WIDE = False


def mx_kscale(k):
    if not WIDE:
        return np.ones(k)
    levels = np.array([24, -24, 12, -12, 0])
    if k % 512:
        return np.exp2(np.random.permutation(np.resize(levels, k // 32))).repeat(32)
    a = np.empty((k // 512, 16))
    for p in range(k // 512):
        a[p, :8] = np.random.permutation(np.resize(levels, 8))
        for g in range(8):
            far = levels[np.abs(levels - a[p, g]) >= 10]
            a[p, g + 8] = far[np.random.randint(len(far))]
    return np.exp2(a.ravel()).repeat(32)


def f64(x):
    return np.asarray(x).astype(np.float64)


def striped(idx):
    return np.tile(idx.reshape(-1, 16).T, (8, 1)).astype(np.uint16)


def unstriped(offs):
    return offs[:16].T.reshape(-1).astype(np.int64)


E2M1 = np.array([0.0, 0.5, 1.0, 1.5, 2.0, 3.0, 4.0, 6.0, -0.0, -0.5, -1.0, -1.5, -2.0, -3.0, -4.0, -6.0])


def pack_weight(w, fmt):
    k, n = w.shape
    w = f64(np.asarray(w, np.float32).astype(ml_dtypes.bfloat16)).reshape(k // 32, 32, n)
    amax = np.abs(w).max(1)
    if fmt == "e4m3":
        byte = np.frexp(amax)[1] - 1 + 127 - 7
    else:
        mant, ex = np.frexp(amax / 6.0)
        byte = np.where(mant > 0.5, ex, ex - 1) + 127
    byte = np.clip(np.where(amax > 0, byte, 1), 1, 254)
    scaled = (w * np.exp2(127.0 - byte)[:, None, :]).reshape(k, n).astype(np.float32)
    by_word = np.ascontiguousarray(scaled.reshape(k // 512, 128, 4, n).transpose(0, 1, 3, 2))
    if fmt == "e4m3":
        words = by_word.astype(ml_dtypes.float8_e4m3fn).view(np.uint8)
    else:
        c = by_word.astype(ml_dtypes.float4_e2m1fn).view(np.uint8) & 0xF
        words = (c[..., 0::2] | (c[..., 1::2] << 4)).reshape(k // 512, 128, 2 * n)
    return np.ascontiguousarray(words), np.ascontiguousarray(byte.astype(np.uint8).reshape(k // 512, 16, n))


def unpack_weight(words, scales, fmt):
    g, _, n = scales.shape
    words = np.ascontiguousarray(words).reshape(g, 128, n, -1)
    if fmt == "e4m3":
        vals = words.view(ml_dtypes.float8_e4m3fn).astype(np.float64)
    else:
        nib = np.empty((g, 128, n, 4), np.uint8)
        nib[..., 0::2] = words & 0xF
        nib[..., 1::2] = words >> 4
        vals = E2M1[nib]
    vals = vals * np.repeat(np.exp2(scales.astype(np.float64) - 127.0), 8, axis=1)[..., None]
    return vals.transpose(0, 1, 3, 2).reshape(g * 512, n)


def pack_table4(v):
    words, scales = pack_weight(v, "e2m1")
    g, t = words.shape[0] // 2, v.shape[1]
    return np.ascontiguousarray(words.reshape(g, 2, 128, t, 2).transpose(0, 2, 3, 1, 4).reshape(g, 128, t, 4)), scales


def unpack_table4(words, scales):
    g, _, t, _ = words.shape
    return unpack_weight(words.reshape(g, 128, t, 2, 2).transpose(0, 3, 1, 2, 4).reshape(2 * g, 128, 2 * t), scales, "e2m1")


K, N, T, J = 1024, 512, 4096, 2048


def setup_inputs():
    n = np.random.standard_normal
    s = mx_kscale(K)[:, None]
    p_tab = pack_table4(n((K, T)) * s)
    p_tab2 = pack_table4(n((K, T)) * s)
    return {
        "tab_words": p_tab[0],
        "tab_scales": p_tab[1],
        "tab2_words": p_tab2[0],
        "tab2_scales": p_tab2[1],
        "wr": (n((K, N)) / np.sqrt(2 * K) / s).astype(np.float32),
        "wi": (n((K, N)) / np.sqrt(2 * K) / s).astype(np.float32),
        "gT": (n((N, T))).astype(np.float32),
        "offs": striped(np.random.permutation(T)[:J]),
    }


def reference(tab_words, tab_scales, tab2_words, tab2_scales, wr, wi, gT, offs):
    idx = unstriped(offs)
    tab_ = unpack_table4(tab_words, tab_scales)[:, idx]
    tab2_ = unpack_table4(tab2_words, tab2_scales)[:, idx]
    wr_ = mxq(f64(wr), 0, "e4m3")
    wi_ = mxq(f64(wi), 0, "e4m3")
    rr = wr_.T @ tab_
    ii = wi_.T @ tab2_
    zr = rr - ii
    ri = wr_.T @ tab2_ + wi_.T @ tab_
    zi = ri
    return zr * f64(gT)[:, idx], zi * f64(gT)[:, idx]

@@ -1,0 +1,212 @@
+from contextlib import ExitStack
+
+import concourse.mybir as mybir
+
+K, N, T, J = 1024, 512, 4096, 2048
+FLOPS = 4 * 2 * K * N * J
+
+F32 = mybir.dt.float32
+BF16 = mybir.dt.bfloat16
+I32 = mybir.dt.int32
+U32 = mybir.dt.uint32
+U16 = mybir.dt.uint16
+U8 = mybir.dt.uint8
+FP8X4 = mybir.dt.float8_e4m3fn_x4
+FP4X4 = mybir.dt.float4_e2m1fn_x4
+COPY = mybir.ActivationFunctionType.Copy
+MULT = mybir.AluOpType.mult
+
+P = 128
+PASSES = 2
+JC = 512
+CHUNKS = J // JC
+ROW_TILES = N // P
+EARLY = 2
+
+
+def tile_list_cpxtab_gate_kernel(
+    tc, tab_words, tab_scales, tab2_words, tab2_scales, wr, wi, gT, offs, out_0, out_1
+):
+    nc = tc.nc
+    outs = (out_0, out_1)
+    with ExitStack() as ctx:
+        held = ctx.enter_context(tc.tile_pool(name="held", bufs=1))
+        stage = ctx.enter_context(tc.tile_pool(name="stage", bufs=6))
+        ring = ctx.enter_context(tc.tile_pool(name="ring", bufs=3))
+        gate_ring = ctx.enter_context(tc.tile_pool(name="gate_ring", bufs=8))
+        late_ring = ctx.enter_context(tc.tile_pool(name="late_ring", bufs=3))
+        psum = ctx.enter_context(tc.psum_pool(name="psum", bufs=8))
+
+        offsets = held.tile([P, J // 16], U16, name="offsets")
+        nc.sync.dma_start(offsets[:], offs)
+
+        def listed(c):
+            return offsets[:, c * (JC // 16) : (c + 1) * (JC // 16)]
+
+        scale_base = (0, 64)
+        scale_window = []
+        for t, scales in enumerate((tab_scales, tab2_scales)):
+            window = held.tile([P, T // 4], I32, name="scale_window%d" % t, align_bytes=64)
+            base = scale_base[t]
+            nc.sync.dma_start(window[base : base + 32, :], scales.rearrange("a q t -> (a q) t").bitcast(I32))
+            nc.vector.memset(window[base + 32 : base + 64, :], 0)
+            nc.vector.memset(window[64 - base : 128 - base, :], 0)
+            scale_window.append(window)
+
+        warm = held.tile([P, 8], F32, name="warm")
+        nc.gpsimd.memset(warm[:], 0.0)
+        nc.scalar.activation(warm[:, 0:1], warm[:, 1:2], COPY)
+
+        planes = []
+        for t in range(2):
+            plane = held.tile([P, PASSES, J // 4], I32, name="planes%d" % t, align_bytes=64)
+            nc.gpsimd.memset(plane[:], 0)
+            planes.append(plane)
+
+        word_window = [held.tile([P, T], I32, name="word_window%d" % t, align_bytes=64) for t in range(2)]
+
+        def load_words(t, words):
+            nc.sync.dma_start(word_window[t][:], words[0].rearrange("p t b -> p (t b)").bitcast(I32))
+
+        raw = {}
+
+        def load_weight(name, w, a):
+            tile = stage.tile([P, 4, N], F32, name="raw_%s%d" % (name, a), tag="stage", align_bytes=64)
+            nc.sync.dma_start(tile[:], w[512 * a : 512 * (a + 1), :].rearrange("(p i) n -> p i n", i=4))
+            raw[name, a] = tile
+
+        load_words(0, tab_words)
+        for name, w in (("wr", wr), ("wi", wi)):
+            for a in range(PASSES):
+                load_weight(name, w, a)
+        load_words(1, tab2_words)
+        gate_window = []
+        for n in range(ROW_TILES):
+            window = held.tile([P, T], F32, name="gate_window%d" % n, align_bytes=64)
+            nc.sync.dma_start(window[:], gT[n * P : (n + 1) * P, :])
+            gate_window.append(window)
+
+        for t in range(2):
+            picked = held.tile([P, J], U8, name="picked_scales%d" % t, align_bytes=64)
+            nc.vector.tensor_copy(picked[:], scale_window[t][:].bitcast(U8).indirect(offsets[:]))
+            for a in range(PASSES):
+                for q in range(4):
+                    row = scale_base[t] + 16 * a + 4 * q
+                    nc.gpsimd.dma_start(planes[t][32 * q : 32 * q + 4, a, :], picked[row : row + 4, :].bitcast(I32))
+
+        codes, code_scales = {}, {}
+
+        def cast(name, source, a, sign):
+            grouped = ring.tile([P, N, 4], BF16, name="grouped", align_bytes=64)
+            nc.scalar.activation(
+                grouped[:].rearrange("p (c m) i -> p c i m", m=4),
+                raw[source, a][:].rearrange("p i (c m) -> p c i m", m=4),
+                COPY,
+                scale=sign,
+            )
+            return grouped
+
+        def quantise(name, a, grouped):
+            codes[name, a] = held.tile([P, N], U32, name="codes_%s%d" % (name, a), align_bytes=64)
+            code_scales[name, a] = held.tile([P, N], U8, name="code_scales_%s%d" % (name, a), align_bytes=64)
+            nc.vector.quantize_mx(
+                out=codes[name, a][:].bitcast(FP8X4),
+                scales=code_scales[name, a][:],
+                in_=grouped[:].rearrange("p n i -> p (n i)"),
+            )
+
+        parted = [held.tile([P, PASSES, 2 * J], U8, name="parted%d" % t, align_bytes=64) for t in range(2)]
+
+        def gather_words(t, c):
+            picked = ring.tile([P, JC], U32, name="picked_words", align_bytes=64)
+            nc.vector.tensor_copy(picked[:], word_window[t][:].bitcast(U32).indirect(listed(c)))
+            return picked
+
+        def part_words(t, c, picked):
+            nc.vector.tensor_copy(
+                parted[t][:, :, 2 * JC * c : 2 * JC * (c + 1)].bitcast(U16),
+                picked[:].bitcast(U16).rearrange("p (j d) -> p d j", d=2),
+            )
+
+        def table_words(t, between):
+            picked = [gather_words(t, 0)]
+            for c in range(CHUNKS):
+                if c + 1 < CHUNKS:
+                    picked.append(gather_words(t, c + 1))
+                for name, source, a, sign in between.get(c, ()):
+                    quantise(name, a, cast(name, source, a, sign))
+                part_words(t, c, picked[c])
+
+        table_words(0, {1: [("wr", "wr", 0, 1.0)], 2: [("wr", "wr", 1, 1.0)], 3: [("wi", "wi", 0, 1.0), ("wi", "wi", 1, 1.0)]})
+        table_words(1, {0: [("neg", "wi", 0, -1.0)], 1: [("neg", "wi", 1, -1.0)]})
+
+        terms = ((("wr", 0), ("neg", 1)), (("wi", 0), ("wr", 1)))
+
+        banks = {}
+
+        def half_product(n, c, o, half):
+            if half == 0:
+                banks[n, c, o] = psum.tile([P, JC], F32, name="acc")
+            name, t = terms[o][half]
+            for a in range(PASSES):
+                nc.tensor.matmul_mx(
+                    out=banks[n, c, o][:],
+                    lhsT=codes[name, a][:, n * P : (n + 1) * P].bitcast(FP8X4),
+                    lhsT_scale=code_scales[name, a][:, n * P : (n + 1) * P],
+                    rhs=parted[t][:, a, 2 * JC * c : 2 * JC * (c + 1)].bitcast(FP4X4),
+                    rhs_scale=planes[t][:, a, (JC // 4) * c : (JC // 4) * (c + 1)].bitcast(U8),
+                    start=(half == 0 and a == 0),
+                    stop=(half == 1 and a == PASSES - 1),
+                )
+
+        def product(n, c, o):
+            if (n, c, o) not in banks:
+                half_product(n, c, o, 0)
+            half_product(n, c, o, 1)
+            return banks[n, c, o]
+
+        staged = {}
+
+        def result(n, c, o):
+            if (n, c // 2) not in staged:
+                staged[n, c // 2] = stage.tile(
+                    [P, 2, 2 * JC], F32, name="staged%d_%d" % (n, c // 2), tag="stage", align_bytes=64
+                )
+            return staged[n, c // 2][:, o, (c % 2) * JC : (c % 2 + 1) * JC]
+
+        def gather_gate(n, c):
+            gate = (gate_ring if n < EARLY else late_ring).tile([P, JC], F32, name="gate", align_bytes=64)
+            nc.vector.tensor_copy(gate[:], gate_window[n][:].indirect(listed(c)))
+            return gate
+
+        def store(n, c, o):
+            rows = slice(n * P, (n + 1) * P)
+            queue = nc.sync if n < EARLY else nc.scalar
+            if n == ROW_TILES - 1 and c >= 2:
+                queue.dma_start(outs[o][rows, c * JC : (c + 1) * JC], result(n, c, o))
+            elif c % 2 == 1:
+                queue.dma_start(outs[o][rows, (c - 1) * JC : (c + 1) * JC], staged[n, c // 2][:, o, :])
+
+        for o in range(2):
+            for c in range(2):
+                for n in range(2):
+                    half_product(n, c, o, 0)
+        for c in range(CHUNKS):
+            for n in range(EARLY):
+                for o in (1, 0):
+                    nc.scalar.activation(result(n, c, o), product(n, c, o)[:], COPY)
+        for n in range(EARLY):
+            for c in range(CHUNKS):
+                gate = gather_gate(n, c)
+                for o in range(2):
+                    nc.gpsimd.tensor_tensor(result(n, c, o), result(n, c, o), gate[:], MULT)
+                    store(n, c, o)
+
+        late = [(n, c) for n in range(EARLY, ROW_TILES) for c in range(CHUNKS)]
+        gates = [gather_gate(*late[0])]
+        for u, (n, c) in enumerate(late):
+            if u + 1 < len(late):
+                gates.append(gather_gate(*late[u + 1]))
+            for o in range(2):
+                nc.vector.tensor_tensor(result(n, c, o), product(n, c, o)[:], gates[u][:], MULT)
+                store(n, c, o)

@@ -20,8 +20,10 @@ P = 128
 PASSES = 2
 JC = 512
 CHUNKS = J // JC
+JH = 1024
+HALVES = J // JH
 ROW_TILES = N // P
-EARLY = 2
+SCALE_ROWS = 96
 
 
 def tile_list_cpxtab_gate_kernel(
@@ -31,114 +33,113 @@ def tile_list_cpxtab_gate_kernel(
     outs = (out_0, out_1)
     with ExitStack() as ctx:
         held = ctx.enter_context(tc.tile_pool(name="held", bufs=1))
-        stage = ctx.enter_context(tc.tile_pool(name="stage", bufs=6))
         ring = ctx.enter_context(tc.tile_pool(name="ring", bufs=3))
-        gate_ring = ctx.enter_context(tc.tile_pool(name="gate_ring", bufs=8))
-        late_ring = ctx.enter_context(tc.tile_pool(name="late_ring", bufs=3))
         psum = ctx.enter_context(tc.psum_pool(name="psum", bufs=8))
 
         offsets = held.tile([P, J // 16], U16, name="offsets")
         nc.sync.dma_start(offsets[:], offs)
 
-        def listed(c):
-            return offsets[:, c * (JC // 16) : (c + 1) * (JC // 16)]
+        def listed(first, count):
+            return offsets[:, first // 16 : (first + count) // 16]
 
-        scale_base = (0, 64)
         scale_window = []
         for t, scales in enumerate((tab_scales, tab2_scales)):
-            window = held.tile([P, T // 4], I32, name="scale_window%d" % t, align_bytes=64)
-            base = scale_base[t]
-            nc.sync.dma_start(window[base : base + 32, :], scales.rearrange("a q t -> (a q) t").bitcast(I32))
-            nc.vector.memset(window[base + 32 : base + 64, :], 0)
-            nc.vector.memset(window[64 - base : 128 - base, :], 0)
+            window = held.tile([P, T // 4], I32, name="scale_window%d" % t, tag="slot%d" % t, align_bytes=64)
+            nc.sync.dma_start(window[SCALE_ROWS:P, :], scales.rearrange("a q t -> (a q) t").bitcast(I32))
+            nc.vector.memset(window[0:SCALE_ROWS, :], 0)
             scale_window.append(window)
-
-        warm = held.tile([P, 8], F32, name="warm")
-        nc.gpsimd.memset(warm[:], 0.0)
-        nc.scalar.activation(warm[:, 0:1], warm[:, 1:2], COPY)
 
         planes = []
         for t in range(2):
             plane = held.tile([P, PASSES, J // 4], I32, name="planes%d" % t, align_bytes=64)
-            nc.gpsimd.memset(plane[:], 0)
+            nc.vector.memset(plane[:], 0)
             planes.append(plane)
 
-        word_window = [held.tile([P, T], I32, name="word_window%d" % t, align_bytes=64) for t in range(2)]
+        def load_words(t, words, slot):
+            window = held.tile([P, T], I32, name="word_window%d" % t, tag=slot, align_bytes=64)
+            nc.sync.dma_start(window[:], words[0].rearrange("p t b -> p (t b)").bitcast(I32))
+            return window
 
-        def load_words(t, words):
-            nc.sync.dma_start(word_window[t][:], words[0].rearrange("p t b -> p (t b)").bitcast(I32))
-
-        raw = {}
-
-        def load_weight(name, w, a):
-            tile = stage.tile([P, 4, N], F32, name="raw_%s%d" % (name, a), tag="stage", align_bytes=64)
-            nc.sync.dma_start(tile[:], w[512 * a : 512 * (a + 1), :].rearrange("(p i) n -> p i n", i=4))
-            raw[name, a] = tile
-
-        load_words(0, tab_words)
-        for name, w in (("wr", wr), ("wi", wi)):
+        def load_weight(name, w, slot):
+            raw = held.tile([P, PASSES, 4, N], F32, name="raw_" + name, tag=slot, align_bytes=64)
             for a in range(PASSES):
-                load_weight(name, w, a)
-        load_words(1, tab2_words)
-        gate_window = []
-        for n in range(ROW_TILES):
-            window = held.tile([P, T], F32, name="gate_window%d" % n, align_bytes=64)
-            nc.sync.dma_start(window[:], gT[n * P : (n + 1) * P, :])
-            gate_window.append(window)
+                nc.sync.dma_start(raw[:, a], w[512 * a : 512 * (a + 1), :].rearrange("(p i) n -> p i n", i=4))
+            return raw
 
-        for t in range(2):
+        def load_gates(n, slot):
+            window = held.tile([P, T], F32, name="gate_window%d" % n, tag=slot, align_bytes=64)
+            nc.sync.dma_start(window[:], gT[n * P : (n + 1) * P, :])
+            return window
+
+        def pick_scales(t):
             picked = held.tile([P, J], U8, name="picked_scales%d" % t, align_bytes=64)
             nc.vector.tensor_copy(picked[:], scale_window[t][:].bitcast(U8).indirect(offsets[:]))
             for a in range(PASSES):
                 for q in range(4):
-                    row = scale_base[t] + 16 * a + 4 * q
-                    nc.gpsimd.dma_start(planes[t][32 * q : 32 * q + 4, a, :], picked[row : row + 4, :].bitcast(I32))
+                    row = SCALE_ROWS + 16 * a + 4 * q
+                    nc.sync.dma_start(planes[t][32 * q : 32 * q + 4, a, :], picked[row : row + 4, :].bitcast(I32))
 
-        codes, code_scales = {}, {}
+        raw_wr = load_weight("wr", wr, "slot3")
+        word_window = [load_words(0, tab_words, "slot2")]
+        raw_wi = load_weight("wi", wi, "slot4")
+        pick_scales(0)
+        word_window.append(load_words(1, tab2_words, "slot0"))
+        pick_scales(1)
+        gate_window = [load_gates(0, "slot1")]
 
-        def cast(name, source, a, sign):
-            grouped = ring.tile([P, N, 4], BF16, name="grouped", align_bytes=64)
+        grouped, codes, code_scales = {}, {}, {}
+
+        def cast(name, raw, a):
+            grouped[name, a] = held.tile([P, N, 4], BF16, name="grouped_%s%d" % (name, a), align_bytes=64)
             nc.scalar.activation(
-                grouped[:].rearrange("p (c m) i -> p c i m", m=4),
-                raw[source, a][:].rearrange("p i (c m) -> p c i m", m=4),
+                grouped[name, a][:].rearrange("p (c m) i -> p c i m", m=4),
+                raw[:, a].rearrange("p i (c m) -> p c i m", m=4),
                 COPY,
-                scale=sign,
             )
-            return grouped
 
-        def quantise(name, a, grouped):
+        def negate(a):
+            grouped["neg", a] = held.tile([P, N, 4], BF16, name="grouped_neg%d" % a, align_bytes=64)
+            nc.scalar.activation(grouped["neg", a][:], grouped["wi", a][:], COPY, scale=-1.0)
+
+        def quantise(name, a):
             codes[name, a] = held.tile([P, N], U32, name="codes_%s%d" % (name, a), align_bytes=64)
             code_scales[name, a] = held.tile([P, N], U8, name="code_scales_%s%d" % (name, a), align_bytes=64)
             nc.vector.quantize_mx(
                 out=codes[name, a][:].bitcast(FP8X4),
                 scales=code_scales[name, a][:],
-                in_=grouped[:].rearrange("p n i -> p (n i)"),
+                in_=grouped[name, a][:].rearrange("p n i -> p (n i)"),
             )
 
-        parted = [held.tile([P, PASSES, 2 * J], U8, name="parted%d" % t, align_bytes=64) for t in range(2)]
+        for a in range(PASSES):
+            cast("wr", raw_wr, a)
+        for a in range(PASSES):
+            cast("wi", raw_wi, a)
+        for a in range(PASSES):
+            negate(a)
 
-        def gather_words(t, c):
-            picked = ring.tile([P, JC], U32, name="picked_words", align_bytes=64)
-            nc.vector.tensor_copy(picked[:], word_window[t][:].bitcast(U32).indirect(listed(c)))
+        parted = {}
+
+        def gather_words(t, h):
+            picked = ring.tile([P, JH], U32, name="picked_words", align_bytes=64)
+            nc.vector.tensor_copy(picked[:], word_window[t][:].bitcast(U32).indirect(listed(h * JH, JH)))
             return picked
 
-        def part_words(t, c, picked):
-            nc.vector.tensor_copy(
-                parted[t][:, :, 2 * JC * c : 2 * JC * (c + 1)].bitcast(U16),
-                picked[:].bitcast(U16).rearrange("p (j d) -> p d j", d=2),
-            )
+        def part_words(t, h, picked):
+            parted[t, h] = held.tile([P, PASSES, JH], U16, name="parted%d_%d" % (t, h), align_bytes=64)
+            nc.vector.tensor_copy(parted[t, h][:], picked[:].bitcast(U16).rearrange("p (j d) -> p d j", d=2))
 
         def table_words(t, between):
-            picked = [gather_words(t, 0)]
-            for c in range(CHUNKS):
-                if c + 1 < CHUNKS:
-                    picked.append(gather_words(t, c + 1))
-                for name, source, a, sign in between.get(c, ()):
-                    quantise(name, a, cast(name, source, a, sign))
-                part_words(t, c, picked[c])
+            picked = [gather_words(t, h) for h in range(HALVES)]
+            for h in range(HALVES):
+                part_words(t, h, picked[h])
+                for name, a in between[h]:
+                    quantise(name, a)
 
-        table_words(0, {1: [("wr", "wr", 0, 1.0)], 2: [("wr", "wr", 1, 1.0)], 3: [("wi", "wi", 0, 1.0), ("wi", "wi", 1, 1.0)]})
-        table_words(1, {0: [("neg", "wi", 0, -1.0)], 1: [("neg", "wi", 1, -1.0)]})
+        table_words(0, ([("wr", 0), ("wr", 1)], [("wi", 0), ("wi", 1)]))
+        gate_window.append(load_gates(1, "slot2"))
+        gate_window.append(load_gates(2, "slot4"))
+        table_words(1, ([("neg", 0), ("neg", 1)], []))
+        gate_window.append(load_gates(3, "slot0"))
 
         terms = ((("wr", 0), ("neg", 1)), (("wi", 0), ("wr", 1)))
 
@@ -148,65 +149,48 @@ def tile_list_cpxtab_gate_kernel(
             if half == 0:
                 banks[n, c, o] = psum.tile([P, JC], F32, name="acc")
             name, t = terms[o][half]
+            first = (c % 2) * JC
             for a in range(PASSES):
                 nc.tensor.matmul_mx(
                     out=banks[n, c, o][:],
                     lhsT=codes[name, a][:, n * P : (n + 1) * P].bitcast(FP8X4),
                     lhsT_scale=code_scales[name, a][:, n * P : (n + 1) * P],
-                    rhs=parted[t][:, a, 2 * JC * c : 2 * JC * (c + 1)].bitcast(FP4X4),
+                    rhs=parted[t, c // 2][:, a, first : first + JC].bitcast(FP4X4),
                     rhs_scale=planes[t][:, a, (JC // 4) * c : (JC // 4) * (c + 1)].bitcast(U8),
                     start=(half == 0 and a == 0),
                     stop=(half == 1 and a == PASSES - 1),
                 )
 
-        def product(n, c, o):
-            if (n, c, o) not in banks:
-                half_product(n, c, o, 0)
-            half_product(n, c, o, 1)
-            return banks[n, c, o]
+        sums = {}
 
-        staged = {}
-
-        def result(n, c, o):
-            if (n, c // 2) not in staged:
-                staged[n, c // 2] = stage.tile(
-                    [P, 2, 2 * JC], F32, name="staged%d_%d" % (n, c // 2), tag="stage", align_bytes=64
-                )
-            return staged[n, c // 2][:, o, (c % 2) * JC : (c % 2 + 1) * JC]
-
-        def gather_gate(n, c):
-            gate = (gate_ring if n < EARLY else late_ring).tile([P, JC], F32, name="gate", align_bytes=64)
-            nc.vector.tensor_copy(gate[:], gate_window[n][:].indirect(listed(c)))
-            return gate
-
-        def store(n, c, o):
-            rows = slice(n * P, (n + 1) * P)
-            queue = nc.sync if n < EARLY else nc.scalar
-            if n == ROW_TILES - 1 and c >= 2:
-                queue.dma_start(outs[o][rows, c * JC : (c + 1) * JC], result(n, c, o))
-            elif c % 2 == 1:
-                queue.dma_start(outs[o][rows, (c - 1) * JC : (c + 1) * JC], staged[n, c // 2][:, o, :])
+        def products(n):
+            tag = "slot3" if n == 0 else "sums%d" % n
+            sums[n] = held.tile([P, 2, J], F32, name="sums%d" % n, tag=tag, align_bytes=64)
+            for c in range(CHUNKS):
+                for o in (1, 0):
+                    if (n, c, o) not in banks:
+                        half_product(n, c, o, 0)
+                    half_product(n, c, o, 1)
+                    nc.scalar.activation(sums[n][:, o, c * JC : (c + 1) * JC], banks[n, c, o][:], COPY)
 
         for o in range(2):
-            for c in range(2):
-                for n in range(2):
-                    half_product(n, c, o, 0)
-        for c in range(CHUNKS):
-            for n in range(EARLY):
-                for o in (1, 0):
-                    nc.scalar.activation(result(n, c, o), product(n, c, o)[:], COPY)
-        for n in range(EARLY):
             for c in range(CHUNKS):
-                gate = gather_gate(n, c)
-                for o in range(2):
-                    nc.gpsimd.tensor_tensor(result(n, c, o), result(n, c, o), gate[:], MULT)
-                    store(n, c, o)
+                half_product(0, c, o, 0)
+        for n in range(ROW_TILES):
+            products(n)
 
-        late = [(n, c) for n in range(EARLY, ROW_TILES) for c in range(CHUNKS)]
-        gates = [gather_gate(*late[0])]
-        for u, (n, c) in enumerate(late):
-            if u + 1 < len(late):
-                gates.append(gather_gate(*late[u + 1]))
-            for o in range(2):
-                nc.vector.tensor_tensor(result(n, c, o), product(n, c, o)[:], gates[u][:], MULT)
-                store(n, c, o)
+        def gather_gate(n, first, count):
+            gate = ring.tile([P, JH], F32, name="gate", align_bytes=64)
+            nc.vector.tensor_copy(gate[:, 0:count], gate_window[n][:].indirect(listed(first, count)))
+            return gate
+
+        pieces = [(n, h * JH, JH) for n in range(ROW_TILES - 1) for h in range(HALVES)]
+        pieces = pieces + [(ROW_TILES - 1, c * JC, JC) for c in range(CHUNKS)]
+        gates = [gather_gate(*pieces[0])]
+        for u, (n, first, count) in enumerate(pieces):
+            if u + 1 < len(pieces):
+                gates.append(gather_gate(*pieces[u + 1]))
+            for o in (1, 0):
+                piece = sums[n][:, o, first : first + count]
+                nc.vector.tensor_tensor(piece, piece, gates[u][:, 0:count], MULT)
+                nc.sync.dma_start(outs[o][n * P : (n + 1) * P, first : first + count], piece)

@@ -23,6 +23,7 @@ CHUNKS = J // JC
 JH = 1024
 HALVES = J // JH
 ROW_TILES = N // P
+AHEAD = 1
 SCALE_ROWS = 96
 
 
@@ -34,7 +35,10 @@ def tile_list_cpxtab_gate_kernel(
     with ExitStack() as ctx:
         held = ctx.enter_context(tc.tile_pool(name="held", bufs=1))
         ring = ctx.enter_context(tc.tile_pool(name="ring", bufs=3))
-        psum = ctx.enter_context(tc.psum_pool(name="psum", bufs=8))
+        gate_ring = ctx.enter_context(tc.tile_pool(name="gate_ring", bufs=2))
+        result_ring = ctx.enter_context(tc.tile_pool(name="result_ring", bufs=4))
+        psum_held = ctx.enter_context(tc.psum_pool(name="psum_held", bufs=6))
+        psum_quick = ctx.enter_context(tc.psum_pool(name="psum_quick", bufs=2))
 
         offsets = held.tile([P, J // 16], U16, name="offsets")
         nc.sync.dma_start(offsets[:], offs)
@@ -52,7 +56,7 @@ def tile_list_cpxtab_gate_kernel(
         planes = []
         for t in range(2):
             plane = held.tile([P, PASSES, J // 4], I32, name="planes%d" % t, align_bytes=64)
-            nc.vector.memset(plane[:], 0)
+            nc.gpsimd.memset(plane[:], 0)
             planes.append(plane)
 
         def load_words(t, words, slot):
@@ -60,11 +64,11 @@ def tile_list_cpxtab_gate_kernel(
             nc.sync.dma_start(window[:], words[0].rearrange("p t b -> p (t b)").bitcast(I32))
             return window
 
-        def load_weight(name, w, slot):
-            raw = held.tile([P, PASSES, 4, N], F32, name="raw_" + name, tag=slot, align_bytes=64)
-            for a in range(PASSES):
-                nc.sync.dma_start(raw[:, a], w[512 * a : 512 * (a + 1), :].rearrange("(p i) n -> p i n", i=4))
-            return raw
+        raw = {}
+
+        def load_weight(name, w, a, slot):
+            raw[name, a] = held.tile([P, 4, N], F32, name="raw_%s%d" % (name, a), tag=slot, align_bytes=64)
+            nc.sync.dma_start(raw[name, a][:], w[512 * a : 512 * (a + 1), :].rearrange("(p i) n -> p i n", i=4))
 
         def load_gates(n, slot):
             window = held.tile([P, T], F32, name="gate_window%d" % n, tag=slot, align_bytes=64)
@@ -77,23 +81,25 @@ def tile_list_cpxtab_gate_kernel(
             for a in range(PASSES):
                 for q in range(4):
                     row = SCALE_ROWS + 16 * a + 4 * q
-                    nc.sync.dma_start(planes[t][32 * q : 32 * q + 4, a, :], picked[row : row + 4, :].bitcast(I32))
+                    queue = nc.gpsimd if q == 3 else nc.sync
+                    queue.dma_start(planes[t][32 * q : 32 * q + 4, a, :], picked[row : row + 4, :].bitcast(I32))
 
-        raw_wr = load_weight("wr", wr, "slot3")
+        load_weight("wi", wi, 0, "slot3")
+        load_weight("wi", wi, 1, "slot4")
         word_window = [load_words(0, tab_words, "slot2")]
-        raw_wi = load_weight("wi", wi, "slot4")
+        load_weight("wr", wr, 0, "slot5")
         pick_scales(0)
-        word_window.append(load_words(1, tab2_words, "slot0"))
+        load_weight("wr", wr, 1, "slot0")
+        word_window.append(load_words(1, tab2_words, "slot1"))
         pick_scales(1)
-        gate_window = [load_gates(0, "slot1")]
 
         grouped, codes, code_scales = {}, {}, {}
 
-        def cast(name, raw, a):
+        def cast(name, a):
             grouped[name, a] = held.tile([P, N, 4], BF16, name="grouped_%s%d" % (name, a), align_bytes=64)
             nc.scalar.activation(
-                grouped[name, a][:].rearrange("p (c m) i -> p c i m", m=4),
-                raw[:, a].rearrange("p i (c m) -> p c i m", m=4),
+                grouped[name, a][:],
+                raw[name, a][:].rearrange("p i n -> p n i"),
                 COPY,
             )
 
@@ -111,86 +117,112 @@ def tile_list_cpxtab_gate_kernel(
             )
 
         for a in range(PASSES):
-            cast("wr", raw_wr, a)
-        for a in range(PASSES):
-            cast("wi", raw_wi, a)
+            cast("wi", a)
         for a in range(PASSES):
             negate(a)
+        for a in range(PASSES):
+            cast("wr", a)
 
         parted = {}
 
-        def gather_words(t, h):
-            picked = ring.tile([P, JH], U32, name="picked_words", align_bytes=64)
-            nc.vector.tensor_copy(picked[:], word_window[t][:].bitcast(U32).indirect(listed(h * JH, JH)))
+        def gather_words(t, first, count):
+            if t == 1:
+                picked = held.tile([P, count], U32, name="picked_first", tag="grouped_wr%d" % (first // count % PASSES), align_bytes=64)
+            else:
+                picked = ring.tile([P, count], U32, name="picked_words", align_bytes=64)
+            nc.vector.tensor_copy(picked[:, 0:count], word_window[t][:].bitcast(U32).indirect(listed(first, count)))
             return picked
 
-        def part_words(t, h, picked):
-            parted[t, h] = held.tile([P, PASSES, JH], U16, name="parted%d_%d" % (t, h), align_bytes=64)
-            nc.vector.tensor_copy(parted[t, h][:], picked[:].bitcast(U16).rearrange("p (j d) -> p d j", d=2))
+        def part_words(t, first, count, picked):
+            tile = held.tile([P, PASSES, count], U16, name="parted%d_%d" % (t, first), align_bytes=64)
+            nc.vector.tensor_copy(tile[:], picked[:, 0:count].bitcast(U16).rearrange("p (j d) -> p d j", d=2))
+            for c in range(count // JC):
+                parted[t, first // JC + c] = tile[:, :, c * JC : (c + 1) * JC]
 
-        def table_words(t, between):
-            picked = [gather_words(t, h) for h in range(HALVES)]
-            for h in range(HALVES):
-                part_words(t, h, picked[h])
-                for name, a in between[h]:
+        def table_words(t, count, between):
+            picked = [gather_words(t, 0, count)]
+            for u in range(J // count):
+                if (u + 1) * count < J:
+                    picked.append(gather_words(t, (u + 1) * count, count))
+                part_words(t, u * count, count, picked[u])
+                for name, a in between.get(u, ()):
                     quantise(name, a)
 
-        table_words(0, ([("wr", 0), ("wr", 1)], [("wi", 0), ("wi", 1)]))
-        gate_window.append(load_gates(1, "slot2"))
-        gate_window.append(load_gates(2, "slot4"))
-        table_words(1, ([("neg", 0), ("neg", 1)], []))
-        gate_window.append(load_gates(3, "slot0"))
+        for a in range(PASSES):
+            quantise("wi", a)
+        table_words(0, JC, {1: [("neg", 0), ("neg", 1)], 3: [("wr", 0), ("wr", 1)]})
+        gate_window = [load_gates(0, "slot5"), load_gates(1, "slot0"), load_gates(2, "slot2")]
+        table_words(1, JC, {})
+        gate_window.append(load_gates(3, "slot1"))
 
         terms = ((("wr", 0), ("neg", 1)), (("wi", 0), ("wr", 1)))
+
+        def on_gpsimd(c, o):
+            return o == 0 and c % 2 == 0
 
         banks = {}
 
         def half_product(n, c, o, half):
             if half == 0:
-                banks[n, c, o] = psum.tile([P, JC], F32, name="acc")
+                pool = psum_quick if on_gpsimd(c, o) else psum_held
+                banks[n, c, o] = pool.tile([P, JC], F32, name="acc")
             name, t = terms[o][half]
-            first = (c % 2) * JC
             for a in range(PASSES):
                 nc.tensor.matmul_mx(
                     out=banks[n, c, o][:],
                     lhsT=codes[name, a][:, n * P : (n + 1) * P].bitcast(FP8X4),
                     lhsT_scale=code_scales[name, a][:, n * P : (n + 1) * P],
-                    rhs=parted[t, c // 2][:, a, first : first + JC].bitcast(FP4X4),
+                    rhs=parted[t, c][:, a, :].bitcast(FP4X4),
                     rhs_scale=planes[t][:, a, (JC // 4) * c : (JC // 4) * (c + 1)].bitcast(U8),
                     start=(half == 0 and a == 0),
                     stop=(half == 1 and a == PASSES - 1),
                 )
 
-        sums = {}
+        copied = {}
 
-        def products(n):
-            tag = "slot3" if n == 0 else "sums%d" % n
-            sums[n] = held.tile([P, 2, J], F32, name="sums%d" % n, tag=tag, align_bytes=64)
+        def product(n, c, o):
+            if (n, c, o) not in banks:
+                half_product(n, c, o, 0)
+            half_product(n, c, o, 1)
+            if on_gpsimd(c, o):
+                copied[n, c] = ring.tile([P, JC], F32, name="copied", align_bytes=64)
+                nc.scalar.activation(copied[n, c][:], banks[n, c, o][:], COPY)
+
+        for o in (1, 0):
             for c in range(CHUNKS):
-                for o in (1, 0):
-                    if (n, c, o) not in banks:
-                        half_product(n, c, o, 0)
-                    half_product(n, c, o, 1)
-                    nc.scalar.activation(sums[n][:, o, c * JC : (c + 1) * JC], banks[n, c, o][:], COPY)
-
-        for o in range(2):
-            for c in range(CHUNKS):
-                half_product(0, c, o, 0)
-        for n in range(ROW_TILES):
-            products(n)
-
-        def gather_gate(n, first, count):
-            gate = ring.tile([P, JH], F32, name="gate", align_bytes=64)
-            nc.vector.tensor_copy(gate[:, 0:count], gate_window[n][:].indirect(listed(first, count)))
-            return gate
-
-        pieces = [(n, h * JH, JH) for n in range(ROW_TILES - 1) for h in range(HALVES)]
-        pieces = pieces + [(ROW_TILES - 1, c * JC, JC) for c in range(CHUNKS)]
-        gates = [gather_gate(*pieces[0])]
-        for u, (n, first, count) in enumerate(pieces):
-            if u + 1 < len(pieces):
-                gates.append(gather_gate(*pieces[u + 1]))
+                if not on_gpsimd(c, o):
+                    half_product(0, c, o, 0)
+        for c in (0, 2):
+            half_product(0, c, 0, 0)
+        for c in range(CHUNKS):
             for o in (1, 0):
-                piece = sums[n][:, o, first : first + count]
-                nc.vector.tensor_tensor(piece, piece, gates[u][:, 0:count], MULT)
-                nc.sync.dma_start(outs[o][n * P : (n + 1) * P, first : first + count], piece)
+                product(0, c, o)
+
+        def gather_gate(n, h):
+            gate = gate_ring.tile([P, JH], F32, name="gate", align_bytes=64)
+            nc.vector.tensor_copy(gate[:], gate_window[n][:].indirect(listed(h * JH, JH)))
+            result = result_ring.tile([P, 2, JH], F32, name="result", align_bytes=64)
+            nc.gpsimd.tensor_tensor(result[:, 0, 0:JC], copied[n, 2 * h][:], gate[:, 0:JC], MULT)
+            return gate, result
+
+        pieces = [(n, h) for n in range(ROW_TILES) for h in range(HALVES)]
+        for n, h in pieces[HALVES : HALVES + AHEAD]:
+            product(n, 2 * h, 0)
+        ready = [gather_gate(*pieces[0])]
+        for u, (n, h) in enumerate(pieces):
+            if u + 1 < len(pieces):
+                ready.append(gather_gate(*pieces[u + 1]))
+            gate, result = ready[u]
+            rows = slice(n * P, (n + 1) * P)
+            for c, o in ((2 * h + 1, 0), (2 * h, 1), (2 * h + 1, 1)):
+                if n > 0:
+                    product(n, c, o)
+                cols = slice((c % 2) * JC, (c % 2 + 1) * JC)
+                nc.vector.tensor_tensor(result[:, o, cols], banks[n, c, o][:], gate[:, cols], MULT)
+                if o == 0 and u + HALVES + AHEAD < len(pieces):
+                    later, half = pieces[u + HALVES + AHEAD]
+                    product(later, 2 * half, 0)
+                if u + 1 == len(pieces) and o == 1:
+                    nc.sync.dma_start(outs[o][rows, c * JC : (c + 1) * JC], result[:, o, cols])
+                elif c % 2 == 1:
+                    nc.sync.dma_start(outs[o][rows, h * JH : (h + 1) * JH], result[:, o, :])

@@ -23,7 +23,7 @@ CHUNKS = J // JC
 JH = 1024
 HALVES = J // JH
 ROW_TILES = N // P
-AHEAD = 1
+AHEAD = 2
 SCALE_ROWS = 96
 
 
@@ -31,14 +31,13 @@ def tile_list_cpxtab_gate_kernel(
     tc, tab_words, tab_scales, tab2_words, tab2_scales, wr, wi, gT, offs, out_0, out_1
 ):
     nc = tc.nc
-    outs = (out_0, out_1)
     with ExitStack() as ctx:
         held = ctx.enter_context(tc.tile_pool(name="held", bufs=1))
         ring = ctx.enter_context(tc.tile_pool(name="ring", bufs=3))
         gate_ring = ctx.enter_context(tc.tile_pool(name="gate_ring", bufs=2))
         result_ring = ctx.enter_context(tc.tile_pool(name="result_ring", bufs=4))
-        psum_held = ctx.enter_context(tc.psum_pool(name="psum_held", bufs=6))
-        psum_quick = ctx.enter_context(tc.psum_pool(name="psum_quick", bufs=2))
+        psum_held = ctx.enter_context(tc.psum_pool(name="psum_held", bufs=4))
+        psum_quick = ctx.enter_context(tc.psum_pool(name="psum_quick", bufs=4))
 
         offsets = held.tile([P, J // 16], U16, name="offsets")
         nc.sync.dma_start(offsets[:], offs)
@@ -125,46 +124,43 @@ def tile_list_cpxtab_gate_kernel(
 
         parted = {}
 
-        def gather_words(t, first, count):
-            if t == 1:
-                picked = held.tile([P, count], U32, name="picked_first", tag="grouped_wr%d" % (first // count % PASSES), align_bytes=64)
+        def gather_words(t, c, slot):
+            if slot is None:
+                picked = ring.tile([P, JC], U32, name="picked_words", align_bytes=64)
             else:
-                picked = ring.tile([P, count], U32, name="picked_words", align_bytes=64)
-            nc.vector.tensor_copy(picked[:, 0:count], word_window[t][:].bitcast(U32).indirect(listed(first, count)))
+                picked = held.tile([P, JC], U32, name="picked_late", tag=slot, align_bytes=64)
+            nc.vector.tensor_copy(picked[:], word_window[t][:].bitcast(U32).indirect(listed(c * JC, JC)))
             return picked
 
-        def part_words(t, first, count, picked):
-            tile = held.tile([P, PASSES, count], U16, name="parted%d_%d" % (t, first), align_bytes=64)
-            nc.vector.tensor_copy(tile[:], picked[:, 0:count].bitcast(U16).rearrange("p (j d) -> p d j", d=2))
-            for c in range(count // JC):
-                parted[t, first // JC + c] = tile[:, :, c * JC : (c + 1) * JC]
-
-        def table_words(t, count, between):
-            picked = [gather_words(t, 0, count)]
-            for u in range(J // count):
-                if (u + 1) * count < J:
-                    picked.append(gather_words(t, (u + 1) * count, count))
-                part_words(t, u * count, count, picked[u])
-                for name, a in between.get(u, ()):
-                    quantise(name, a)
+        def part_words(t, c, picked):
+            parted[t, c] = held.tile([P, PASSES, JC], U16, name="parted%d_%d" % (t, c), align_bytes=64)
+            nc.vector.tensor_copy(parted[t, c][:], picked[:].bitcast(U16).rearrange("p (j d) -> p d j", d=2))
 
         for a in range(PASSES):
             quantise("wi", a)
-        table_words(0, JC, {1: [("neg", 0), ("neg", 1)], 3: [("wr", 0), ("wr", 1)]})
-        gate_window = [load_gates(0, "slot5"), load_gates(1, "slot0"), load_gates(2, "slot2")]
-        table_words(1, JC, {})
-        gate_window.append(load_gates(3, "slot1"))
+        early = [gather_words(0, c, None) for c in range(CHUNKS - 1)]
+        part_words(0, 0, early[0])
+        for a in range(PASSES):
+            quantise("neg", a)
+        part_words(0, 1, early[1])
+        quantise("wr", 0)
+        part_words(0, 2, early[2])
+        late = [(1, 0), (0, 3), (1, 1), (1, 2), (1, 3)]
+        picked = [gather_words(*late[0], "grouped_wr0")]
+        quantise("wr", 1)
+        for u, (t, c) in enumerate(late):
+            part_words(t, c, picked[u])
+            for v in range(len(picked), min(u + 3, len(late))):
+                picked.append(gather_words(*late[v], "grouped_wr%d" % (v % 2)))
+        gate_window = [load_gates(0, "slot5"), load_gates(1, "slot0"), load_gates(2, "slot2"), load_gates(3, "slot1")]
 
         terms = ((("wr", 0), ("neg", 1)), (("wi", 0), ("wr", 1)))
-
-        def on_gpsimd(c, o):
-            return o == 0 and c % 2 == 0
 
         banks = {}
 
         def half_product(n, c, o, half):
             if half == 0:
-                pool = psum_quick if on_gpsimd(c, o) else psum_held
+                pool = psum_quick if o == 0 else psum_held
                 banks[n, c, o] = pool.tile([P, JC], F32, name="acc")
             name, t = terms[o][half]
             for a in range(PASSES):
@@ -184,45 +180,54 @@ def tile_list_cpxtab_gate_kernel(
             if (n, c, o) not in banks:
                 half_product(n, c, o, 0)
             half_product(n, c, o, 1)
-            if on_gpsimd(c, o):
-                copied[n, c] = ring.tile([P, JC], F32, name="copied", align_bytes=64)
-                nc.scalar.activation(copied[n, c][:], banks[n, c, o][:], COPY)
+            if o == 0:
+                if c % 2 == 0:
+                    copied[n, c // 2] = ring.tile([P, JH], F32, name="copied", align_bytes=64)
+                nc.scalar.activation(copied[n, c // 2][:, (c % 2) * JC : (c % 2 + 1) * JC], banks[n, c, o][:], COPY)
 
         for o in (1, 0):
-            for c in range(CHUNKS):
-                if not on_gpsimd(c, o):
-                    half_product(0, c, o, 0)
-        for c in (0, 2):
-            half_product(0, c, 0, 0)
+            for c in range(CHUNKS - 1):
+                half_product(0, c, o, 0)
+        half_product(1, 0, 0, 0)
         for c in range(CHUNKS):
             for o in (1, 0):
                 product(0, c, o)
 
-        def gather_gate(n, h):
+        pieces = [(n, h) for n in range(ROW_TILES) for h in range(HALVES)]
+
+        def gather_gate(u):
+            n, h = pieces[u]
             gate = gate_ring.tile([P, JH], F32, name="gate", align_bytes=64)
             nc.vector.tensor_copy(gate[:], gate_window[n][:].indirect(listed(h * JH, JH)))
-            result = result_ring.tile([P, 2, JH], F32, name="result", align_bytes=64)
-            nc.gpsimd.tensor_tensor(result[:, 0, 0:JC], copied[n, 2 * h][:], gate[:, 0:JC], MULT)
-            return gate, result
+            result = result_ring.tile([P, JH], F32, name="real", align_bytes=64)
+            width = JC if u + 1 == len(pieces) else JH
+            for first in range(0, JH, width):
+                cols = slice(first, first + width)
+                nc.gpsimd.tensor_tensor(result[:, cols], copied[n, h][:, cols], gate[:, cols], MULT)
+                nc.sync.dma_start(out_0[n * P : (n + 1) * P, h * JH + first : h * JH + first + width], result[:, cols])
+            return gate
 
-        pieces = [(n, h) for n in range(ROW_TILES) for h in range(HALVES)]
-        for n, h in pieces[HALVES : HALVES + AHEAD]:
-            product(n, 2 * h, 0)
-        ready = [gather_gate(*pieces[0])]
+        def real_products(u):
+            n, h = pieces[u]
+            for c in (2 * h, 2 * h + 1):
+                product(n, c, 0)
+
+        for u in range(HALVES, HALVES + AHEAD):
+            real_products(u)
+        gates = [gather_gate(0)]
         for u, (n, h) in enumerate(pieces):
             if u + 1 < len(pieces):
-                ready.append(gather_gate(*pieces[u + 1]))
-            gate, result = ready[u]
+                gates.append(gather_gate(u + 1))
+            result = result_ring.tile([P, JH], F32, name="imaginary", align_bytes=64)
             rows = slice(n * P, (n + 1) * P)
-            for c, o in ((2 * h + 1, 0), (2 * h, 1), (2 * h + 1, 1)):
+            for c in (2 * h, 2 * h + 1):
                 if n > 0:
-                    product(n, c, o)
+                    product(n, c, 1)
                 cols = slice((c % 2) * JC, (c % 2 + 1) * JC)
-                nc.vector.tensor_tensor(result[:, o, cols], banks[n, c, o][:], gate[:, cols], MULT)
-                if o == 0 and u + HALVES + AHEAD < len(pieces):
-                    later, half = pieces[u + HALVES + AHEAD]
-                    product(later, 2 * half, 0)
-                if u + 1 == len(pieces) and o == 1:
-                    nc.sync.dma_start(outs[o][rows, c * JC : (c + 1) * JC], result[:, o, cols])
-                elif c % 2 == 1:
-                    nc.sync.dma_start(outs[o][rows, h * JH : (h + 1) * JH], result[:, o, :])
+                nc.vector.tensor_tensor(result[:, cols], banks[n, c, 1][:], gates[u][:, cols], MULT)
+                if u + 1 == len(pieces):
+                    nc.sync.dma_start(out_1[rows, c * JC : (c + 1) * JC], result[:, cols])
+            if u + 1 < len(pieces):
+                nc.sync.dma_start(out_1[rows, h * JH : (h + 1) * JH], result[:])
+            if u + HALVES + AHEAD < len(pieces):
+                real_products(u + HALVES + AHEAD)

@@ -23,7 +23,6 @@ CHUNKS = J // JC
 JH = 1024
 HALVES = J // JH
 ROW_TILES = N // P
-AHEAD = 2
 SCALE_ROWS = 96
 
 
@@ -31,13 +30,13 @@ def tile_list_cpxtab_gate_kernel(
     tc, tab_words, tab_scales, tab2_words, tab2_scales, wr, wi, gT, offs, out_0, out_1
 ):
     nc = tc.nc
+    outs = (out_0, out_1)
     with ExitStack() as ctx:
         held = ctx.enter_context(tc.tile_pool(name="held", bufs=1))
         ring = ctx.enter_context(tc.tile_pool(name="ring", bufs=3))
-        gate_ring = ctx.enter_context(tc.tile_pool(name="gate_ring", bufs=2))
+        gate_ring = ctx.enter_context(tc.tile_pool(name="gate_ring", bufs=3))
         result_ring = ctx.enter_context(tc.tile_pool(name="result_ring", bufs=4))
-        psum_held = ctx.enter_context(tc.psum_pool(name="psum_held", bufs=4))
-        psum_quick = ctx.enter_context(tc.psum_pool(name="psum_quick", bufs=4))
+        psum = ctx.enter_context(tc.psum_pool(name="psum", bufs=1))
 
         offsets = held.tile([P, J // 16], U16, name="offsets")
         nc.sync.dma_start(offsets[:], offs)
@@ -145,23 +144,37 @@ def tile_list_cpxtab_gate_kernel(
         part_words(0, 1, early[1])
         quantise("wr", 0)
         part_words(0, 2, early[2])
-        late = [(1, 0), (0, 3), (1, 1), (1, 2), (1, 3)]
+        late = [(1, 0), (1, 1), (0, 3), (1, 2), (1, 3)]
         picked = [gather_words(*late[0], "grouped_wr0")]
         quantise("wr", 1)
+        picked.append(gather_words(*late[1], "grouped_wr1"))
         for u, (t, c) in enumerate(late):
             part_words(t, c, picked[u])
-            for v in range(len(picked), min(u + 3, len(late))):
-                picked.append(gather_words(*late[v], "grouped_wr%d" % (v % 2)))
+            if u + 2 < len(late):
+                picked.append(gather_words(*late[u + 2], "grouped_wr%d" % (u % 2)))
         gate_window = [load_gates(0, "slot5"), load_gates(1, "slot0"), load_gates(2, "slot2"), load_gates(3, "slot1")]
 
         terms = ((("wr", 0), ("neg", 1)), (("wi", 0), ("wr", 1)))
 
-        banks = {}
+        pieces = [(n, h) for n in range(ROW_TILES) for h in range(HALVES)]
+
+        def on_gpsimd(n, c, o):
+            return o == 1 or (n == 0 and c < 2)
+
+        banks, turns = {}, {True: [], False: []}
+
+        def open_bank(n, c, o):
+            if o == 1 and c < 2:
+                number = 4 * c + n
+            else:
+                turn = turns[on_gpsimd(n, c, o)]
+                number = len(turn) % 2 if on_gpsimd(n, c, o) else 2 + len(turn) % 6
+                turn.append((n, c, o))
+            banks[n, c, o] = psum.tile([P, JC], F32, name="acc", tag="bank%d" % number)
 
         def half_product(n, c, o, half):
             if half == 0:
-                pool = psum_quick if o == 0 else psum_held
-                banks[n, c, o] = pool.tile([P, JC], F32, name="acc")
+                open_bank(n, c, o)
             name, t = terms[o][half]
             for a in range(PASSES):
                 nc.tensor.matmul_mx(
@@ -174,60 +187,53 @@ def tile_list_cpxtab_gate_kernel(
                     stop=(half == 1 and a == PASSES - 1),
                 )
 
-        copied = {}
+        sums = {
+            (n, 1): held.tile([P, J], F32, name="sums%d" % n, tag=("slot3", "slot4", "sums2", "sums3")[n], align_bytes=64)
+            for n in range(ROW_TILES)
+        }
+        sums[0, 0] = held.tile([P, JH], F32, name="first_real_sums", align_bytes=64)
 
         def product(n, c, o):
             if (n, c, o) not in banks:
                 half_product(n, c, o, 0)
             half_product(n, c, o, 1)
-            if o == 0:
-                if c % 2 == 0:
-                    copied[n, c // 2] = ring.tile([P, JH], F32, name="copied", align_bytes=64)
-                nc.scalar.activation(copied[n, c // 2][:, (c % 2) * JC : (c % 2 + 1) * JC], banks[n, c, o][:], COPY)
+            if on_gpsimd(n, c, o):
+                nc.scalar.activation(sums[n, o][:, c * JC : (c + 1) * JC], banks[n, c, o][:], COPY)
 
-        for o in (1, 0):
-            for c in range(CHUNKS - 1):
-                half_product(0, c, o, 0)
-        half_product(1, 0, 0, 0)
-        for c in range(CHUNKS):
-            for o in (1, 0):
-                product(0, c, o)
-
-        pieces = [(n, h) for n in range(ROW_TILES) for h in range(HALVES)]
+        for c in range(2):
+            for n in range(ROW_TILES):
+                half_product(n, c, 1, 0)
+        for c in range(2):
+            for n in range(ROW_TILES):
+                product(n, c, 1)
 
         def gather_gate(u):
             n, h = pieces[u]
             gate = gate_ring.tile([P, JH], F32, name="gate", align_bytes=64)
             nc.vector.tensor_copy(gate[:], gate_window[n][:].indirect(listed(h * JH, JH)))
-            result = result_ring.tile([P, JH], F32, name="real", align_bytes=64)
-            width = JC if u + 1 == len(pieces) else JH
-            for first in range(0, JH, width):
-                cols = slice(first, first + width)
-                nc.gpsimd.tensor_tensor(result[:, cols], copied[n, h][:, cols], gate[:, cols], MULT)
-                nc.sync.dma_start(out_0[n * P : (n + 1) * P, h * JH + first : h * JH + first + width], result[:, cols])
+            for o in (1, 0):
+                if on_gpsimd(n, 2 * h, o):
+                    for c in (2 * h, 2 * h + 1):
+                        if (n, c, o) not in banks:
+                            product(n, c, o)
+                    piece = sums[n, o][:, h * JH : (h + 1) * JH]
+                    nc.gpsimd.tensor_tensor(piece, piece, gate[:], MULT)
+                    nc.sync.dma_start(outs[o][n * P : (n + 1) * P, h * JH : (h + 1) * JH], piece)
             return gate
 
-        def real_products(u):
-            n, h = pieces[u]
-            for c in (2 * h, 2 * h + 1):
-                product(n, c, 0)
-
-        for u in range(HALVES, HALVES + AHEAD):
-            real_products(u)
         gates = [gather_gate(0)]
         for u, (n, h) in enumerate(pieces):
             if u + 1 < len(pieces):
                 gates.append(gather_gate(u + 1))
-            result = result_ring.tile([P, JH], F32, name="imaginary", align_bytes=64)
+            if on_gpsimd(n, 2 * h, 0):
+                continue
+            result = result_ring.tile([P, JH], F32, name="real", align_bytes=64)
             rows = slice(n * P, (n + 1) * P)
             for c in (2 * h, 2 * h + 1):
-                if n > 0:
-                    product(n, c, 1)
+                product(n, c, 0)
                 cols = slice((c % 2) * JC, (c % 2 + 1) * JC)
-                nc.vector.tensor_tensor(result[:, cols], banks[n, c, 1][:], gates[u][:, cols], MULT)
+                nc.vector.tensor_tensor(result[:, cols], banks[n, c, 0][:], gates[u][:, cols], MULT)
                 if u + 1 == len(pieces):
-                    nc.sync.dma_start(out_1[rows, c * JC : (c + 1) * JC], result[:, cols])
+                    nc.sync.dma_start(out_0[rows, c * JC : (c + 1) * JC], result[:, cols])
             if u + 1 < len(pieces):
-                nc.sync.dma_start(out_1[rows, h * JH : (h + 1) * JH], result[:])
-            if u + HALVES + AHEAD < len(pieces):
-                real_products(u + HALVES + AHEAD)
+                nc.sync.dma_start(out_0[rows, h * JH : (h + 1) * JH], result[:])

@@ -18,12 +18,16 @@ MULT = mybir.AluOpType.mult
 
 P = 128
 PASSES = 2
-JC = 512
-CHUNKS = J // JC
-JH = 1024
-HALVES = J // JH
+K_PASS = K // PASSES
+CHUNK = 512
+CHUNKS = J // CHUNK
+HALF = 2 * CHUNK
+HALVES = J // HALF
 ROW_TILES = N // P
 SCALE_ROWS = 96
+REAL_ON_GPSIMD = 2
+QUICK_BANKS = 2
+BANKS = 8
 
 
 def tile_list_cpxtab_gate_kernel(
@@ -33,7 +37,7 @@ def tile_list_cpxtab_gate_kernel(
     outs = (out_0, out_1)
     with ExitStack() as ctx:
         held = ctx.enter_context(tc.tile_pool(name="held", bufs=1))
-        ring = ctx.enter_context(tc.tile_pool(name="ring", bufs=3))
+        word_ring = ctx.enter_context(tc.tile_pool(name="word_ring", bufs=3))
         gate_ring = ctx.enter_context(tc.tile_pool(name="gate_ring", bufs=3))
         result_ring = ctx.enter_context(tc.tile_pool(name="result_ring", bufs=4))
         psum = ctx.enter_context(tc.psum_pool(name="psum", bufs=1))
@@ -66,7 +70,7 @@ def tile_list_cpxtab_gate_kernel(
 
         def load_weight(name, w, a, slot):
             raw[name, a] = held.tile([P, 4, N], F32, name="raw_%s%d" % (name, a), tag=slot, align_bytes=64)
-            nc.sync.dma_start(raw[name, a][:], w[512 * a : 512 * (a + 1), :].rearrange("(p i) n -> p i n", i=4))
+            nc.sync.dma_start(raw[name, a][:], w[K_PASS * a : K_PASS * (a + 1), :].rearrange("(p i) n -> p i n", i=4))
 
         def load_gates(n, slot):
             window = held.tile([P, T], F32, name="gate_window%d" % n, tag=slot, align_bytes=64)
@@ -77,10 +81,12 @@ def tile_list_cpxtab_gate_kernel(
             picked = held.tile([P, J], U8, name="picked_scales%d" % t, align_bytes=64)
             nc.vector.tensor_copy(picked[:], scale_window[t][:].bitcast(U8).indirect(offsets[:]))
             for a in range(PASSES):
-                for q in range(4):
-                    row = SCALE_ROWS + 16 * a + 4 * q
-                    queue = nc.gpsimd if q == 3 else nc.sync
-                    queue.dma_start(planes[t][32 * q : 32 * q + 4, a, :], picked[row : row + 4, :].bitcast(I32))
+                for quadrant in range(4):
+                    row = SCALE_ROWS + 16 * a + 4 * quadrant
+                    queue = nc.gpsimd if quadrant == 3 else nc.sync
+                    queue.dma_start(
+                        planes[t][32 * quadrant : 32 * quadrant + 4, a, :], picked[row : row + 4, :].bitcast(I32)
+                    )
 
         load_weight("wi", wi, 0, "slot3")
         load_weight("wi", wi, 1, "slot4")
@@ -96,8 +102,8 @@ def tile_list_cpxtab_gate_kernel(
         def cast(name, a):
             grouped[name, a] = held.tile([P, N, 4], BF16, name="grouped_%s%d" % (name, a), align_bytes=64)
             nc.scalar.activation(
-                grouped[name, a][:],
-                raw[name, a][:].rearrange("p i n -> p n i"),
+                grouped[name, a][:].rearrange("p (c m) i -> p c i m", m=4),
+                raw[name, a][:].rearrange("p i (c m) -> p c i m", m=4),
                 COPY,
             )
 
@@ -123,102 +129,116 @@ def tile_list_cpxtab_gate_kernel(
 
         parted = {}
 
-        def gather_words(t, c, slot):
-            if slot is None:
-                picked = ring.tile([P, JC], U32, name="picked_words", align_bytes=64)
-            else:
-                picked = held.tile([P, JC], U32, name="picked_late", tag=slot, align_bytes=64)
-            nc.vector.tensor_copy(picked[:], word_window[t][:].bitcast(U32).indirect(listed(c * JC, JC)))
+        def gather_words(t, c, picked):
+            nc.vector.tensor_copy(picked[:], word_window[t][:].bitcast(U32).indirect(listed(c * CHUNK, CHUNK)))
             return picked
 
         def part_words(t, c, picked):
-            parted[t, c] = held.tile([P, PASSES, JC], U16, name="parted%d_%d" % (t, c), align_bytes=64)
-            nc.vector.tensor_copy(parted[t, c][:], picked[:].bitcast(U16).rearrange("p (j d) -> p d j", d=2))
+            parted[t, c] = held.tile([P, PASSES, CHUNK], U16, name="parted%d_%d" % (t, c), align_bytes=64)
+            nc.vector.tensor_copy(
+                parted[t, c][:].rearrange("p d (h j) -> p h d j", h=2),
+                picked[:].bitcast(U16).rearrange("p (h j d) -> p h d j", h=2, d=2),
+            )
+
+        def early_tile():
+            return word_ring.tile([P, CHUNK], U32, name="picked_words", align_bytes=64)
+
+        def late_tile(a):
+            return held.tile([P, CHUNK], U32, name="picked_late", tag="grouped_wr%d" % a, align_bytes=64)
 
         for a in range(PASSES):
             quantise("wi", a)
-        early = [gather_words(0, c, None) for c in range(CHUNKS - 1)]
+        early = [gather_words(0, c, early_tile()) for c in range(CHUNKS - 1)]
         part_words(0, 0, early[0])
         for a in range(PASSES):
             quantise("neg", a)
         part_words(0, 1, early[1])
         quantise("wr", 0)
         part_words(0, 2, early[2])
-        late = [(1, 0), (1, 1), (0, 3), (1, 2), (1, 3)]
-        picked = [gather_words(*late[0], "grouped_wr0")]
+        late = [(1, 0), (1, 1), (0, CHUNKS - 1)] + [(1, c) for c in range(2, CHUNKS)]
+        picked_late = [gather_words(*late[0], late_tile(0))]
         quantise("wr", 1)
-        picked.append(gather_words(*late[1], "grouped_wr1"))
+        picked_late.append(gather_words(*late[1], late_tile(1)))
         for u, (t, c) in enumerate(late):
-            part_words(t, c, picked[u])
+            part_words(t, c, picked_late[u])
             if u + 2 < len(late):
-                picked.append(gather_words(*late[u + 2], "grouped_wr%d" % (u % 2)))
-        gate_window = [load_gates(0, "slot5"), load_gates(1, "slot0"), load_gates(2, "slot2"), load_gates(3, "slot1")]
+                picked_late.append(gather_words(*late[u + 2], late_tile(u % 2)))
+        gate_window = [load_gates(n, slot) for n, slot in enumerate(("slot5", "slot0", "slot2", "slot1"))]
 
         terms = ((("wr", 0), ("neg", 1)), (("wi", 0), ("wr", 1)))
 
         pieces = [(n, h) for n in range(ROW_TILES) for h in range(HALVES)]
 
         def on_gpsimd(n, c, o):
-            return o == 1 or (n == 0 and c < 2)
+            return o == 1 or CHUNKS * n + c < REAL_ON_GPSIMD
 
         banks, turns = {}, {True: [], False: []}
 
         def open_bank(n, c, o):
             if o == 1 and c < 2:
-                number = 4 * c + n
+                number = ROW_TILES * c + n
             else:
-                turn = turns[on_gpsimd(n, c, o)]
-                number = len(turn) % 2 if on_gpsimd(n, c, o) else 2 + len(turn) % 6
-                turn.append((n, c, o))
-            banks[n, c, o] = psum.tile([P, JC], F32, name="acc", tag="bank%d" % number)
+                quick = on_gpsimd(n, c, o)
+                turn = len(turns[quick])
+                number = turn % QUICK_BANKS if quick else QUICK_BANKS + turn % (BANKS - QUICK_BANKS)
+                turns[quick].append((n, c, o))
+            banks[n, c, o] = psum.tile([P, CHUNK], F32, name="acc", tag="bank%d" % number)
 
-        def half_product(n, c, o, half):
-            if half == 0:
+        def term_product(n, c, o, term):
+            if term == 0:
                 open_bank(n, c, o)
-            name, t = terms[o][half]
+            name, t = terms[o][term]
             for a in range(PASSES):
                 nc.tensor.matmul_mx(
                     out=banks[n, c, o][:],
                     lhsT=codes[name, a][:, n * P : (n + 1) * P].bitcast(FP8X4),
                     lhsT_scale=code_scales[name, a][:, n * P : (n + 1) * P],
                     rhs=parted[t, c][:, a, :].bitcast(FP4X4),
-                    rhs_scale=planes[t][:, a, (JC // 4) * c : (JC // 4) * (c + 1)].bitcast(U8),
-                    start=(half == 0 and a == 0),
-                    stop=(half == 1 and a == PASSES - 1),
+                    rhs_scale=planes[t][:, a, (CHUNK // 4) * c : (CHUNK // 4) * (c + 1)].bitcast(U8),
+                    start=(term == 0 and a == 0),
+                    stop=(term == 1 and a == PASSES - 1),
                 )
 
         sums = {
             (n, 1): held.tile([P, J], F32, name="sums%d" % n, tag=("slot3", "slot4", "sums2", "sums3")[n], align_bytes=64)
             for n in range(ROW_TILES)
         }
-        sums[0, 0] = held.tile([P, JH], F32, name="first_real_sums", align_bytes=64)
+        sums[0, 0] = held.tile([P, REAL_ON_GPSIMD * CHUNK], F32, name="first_real_sums", align_bytes=64)
 
         def product(n, c, o):
             if (n, c, o) not in banks:
-                half_product(n, c, o, 0)
-            half_product(n, c, o, 1)
+                term_product(n, c, o, 0)
+            term_product(n, c, o, 1)
             if on_gpsimd(n, c, o):
-                nc.scalar.activation(sums[n, o][:, c * JC : (c + 1) * JC], banks[n, c, o][:], COPY)
+                nc.scalar.activation(sums[n, o][:, c * CHUNK : (c + 1) * CHUNK], banks[n, c, o][:], COPY)
 
         for c in range(2):
             for n in range(ROW_TILES):
-                half_product(n, c, 1, 0)
+                term_product(n, c, 1, 0)
         for c in range(2):
             for n in range(ROW_TILES):
                 product(n, c, 1)
 
         def gather_gate(u):
             n, h = pieces[u]
-            gate = gate_ring.tile([P, JH], F32, name="gate", align_bytes=64)
-            nc.vector.tensor_copy(gate[:], gate_window[n][:].indirect(listed(h * JH, JH)))
+            rows = slice(n * P, (n + 1) * P)
+            gate = gate_ring.tile([P, HALF], F32, name="gate", align_bytes=64)
+            nc.vector.tensor_copy(gate[:], gate_window[n][:].indirect(listed(h * HALF, HALF)))
             for o in (1, 0):
-                if on_gpsimd(n, 2 * h, o):
-                    for c in (2 * h, 2 * h + 1):
-                        if (n, c, o) not in banks:
-                            product(n, c, o)
-                    piece = sums[n, o][:, h * JH : (h + 1) * JH]
-                    nc.gpsimd.tensor_tensor(piece, piece, gate[:], MULT)
-                    nc.sync.dma_start(outs[o][n * P : (n + 1) * P, h * JH : (h + 1) * JH], piece)
+                if not on_gpsimd(n, 2 * h, o):
+                    continue
+                for c in (2 * h, 2 * h + 1):
+                    if (n, c, o) not in banks:
+                        product(n, c, o)
+                for c in (2 * h, 2 * h + 1):
+                    cols = slice(c * CHUNK, (c + 1) * CHUNK)
+                    gate_cols = slice((c % 2) * CHUNK, (c % 2 + 1) * CHUNK)
+                    nc.gpsimd.tensor_tensor(sums[n, o][:, cols], sums[n, o][:, cols], gate[:, gate_cols], MULT)
+                    if u + 1 == len(pieces):
+                        nc.sync.dma_start(outs[o][rows, cols], sums[n, o][:, cols])
+                if u + 1 < len(pieces):
+                    cols = slice(h * HALF, (h + 1) * HALF)
+                    nc.sync.dma_start(outs[o][rows, cols], sums[n, o][:, cols])
             return gate
 
         gates = [gather_gate(0)]
@@ -227,13 +247,13 @@ def tile_list_cpxtab_gate_kernel(
                 gates.append(gather_gate(u + 1))
             if on_gpsimd(n, 2 * h, 0):
                 continue
-            result = result_ring.tile([P, JH], F32, name="real", align_bytes=64)
+            result = result_ring.tile([P, HALF], F32, name="real", align_bytes=64)
             rows = slice(n * P, (n + 1) * P)
             for c in (2 * h, 2 * h + 1):
                 product(n, c, 0)
-                cols = slice((c % 2) * JC, (c % 2 + 1) * JC)
-                nc.vector.tensor_tensor(result[:, cols], banks[n, c, 0][:], gates[u][:, cols], MULT)
+                half_cols = slice((c % 2) * CHUNK, (c % 2 + 1) * CHUNK)
+                nc.vector.tensor_tensor(result[:, half_cols], banks[n, c, 0][:], gates[u][:, half_cols], MULT)
                 if u + 1 == len(pieces):
-                    nc.sync.dma_start(out_0[rows, c * JC : (c + 1) * JC], result[:, cols])
+                    nc.sync.dma_start(out_0[rows, c * CHUNK : (c + 1) * CHUNK], result[:, half_cols])
             if u + 1 < len(pieces):
-                nc.sync.dma_start(out_0[rows, h * JH : (h + 1) * JH], result[:])
+                nc.sync.dma_start(out_0[rows, h * HALF : (h + 1) * HALF], result[:])

@@ -25,9 +25,10 @@ HALF = 2 * CHUNK
 HALVES = J // HALF
 ROW_TILES = N // P
 SCALE_ROWS = 96
-REAL_ON_GPSIMD = 2
+REAL_ON_GPSIMD = 0
 QUICK_BANKS = 2
 BANKS = 8
+KIB = 1024
 
 
 def tile_list_cpxtab_gate_kernel(
@@ -37,10 +38,62 @@ def tile_list_cpxtab_gate_kernel(
     outs = (out_0, out_1)
     with ExitStack() as ctx:
         held = ctx.enter_context(tc.tile_pool(name="held", bufs=1))
-        word_ring = ctx.enter_context(tc.tile_pool(name="word_ring", bufs=3))
-        gate_ring = ctx.enter_context(tc.tile_pool(name="gate_ring", bufs=3))
-        result_ring = ctx.enter_context(tc.tile_pool(name="result_ring", bufs=4))
+        shared = ctx.enter_context(tc.tile_pool(name="shared", bufs=1))
         psum = ctx.enter_context(tc.psum_pool(name="psum", bufs=1))
+
+        place = {
+            "word_window0": 0,
+            "gate_window3": 116,
+            "word_window1": 16,
+            "scale_window0": 16,
+            "raw_wi0": 32,
+            "raw_wi1": 40,
+            "gate_window0": 32,
+            "raw_wr0": 48,
+            "raw_wr1": 56,
+            "scale_window1": 54,
+            "picked1_2": 48,
+            "picked1_3": 48,
+            "parted1_2": 60,
+            "grouped_wi0": 64,
+            "grouped_wi1": 68,
+            "gate_window1": 64,
+            "grouped_neg0": 80,
+            "grouped_neg1": 116,
+            "gate_window2": 80,
+            "grouped_wr0": 96,
+            "picked0_2": 96,
+            "picked0_3": 96,
+            "grouped_wr1": 100,
+            "parted0_2": 100,
+            "picked0_0": 104,
+            "picked1_0": 104,
+            "picked0_1": 108,
+            "picked1_1": 108,
+            "gate0": 48,
+            "gate1": 96,
+            "gate2": 16,
+            "gate3": 20,
+            "gate4": 24,
+            "gate5": 28,
+            "gate6": 20,
+            "gate7": 24,
+            "gate8": 20,
+            "result0": 64,
+            "result1": 68,
+            "result2": 80,
+            "result3": 84,
+            "result4": 32,
+            "result5": 36,
+            "result6": 40,
+            "result7": 44,
+            "result8": 46,
+        }
+
+        def sbuf(name, shape, dtype):
+            if name in place:
+                return shared.tile(shape, dtype, name=name, align_bytes=64, offset=place[name] * KIB)
+            return held.tile(shape, dtype, name=name, align_bytes=64)
 
         offsets = held.tile([P, J // 16], U16, name="offsets")
         nc.sync.dma_start(offsets[:], offs)
@@ -50,57 +103,53 @@ def tile_list_cpxtab_gate_kernel(
 
         scale_window = []
         for t, scales in enumerate((tab_scales, tab2_scales)):
-            window = held.tile([P, T // 4], I32, name="scale_window%d" % t, tag="slot%d" % t, align_bytes=64)
-            nc.sync.dma_start(window[SCALE_ROWS:P, :], scales.rearrange("a q t -> (a q) t").bitcast(I32))
+            window = sbuf("scale_window%d" % t, [P, T // 4], I32)
+            nc.sync.dma_start(window[SCALE_ROWS:P, :], scales.bitcast(I32).rearrange("a q t -> q a t"))
             nc.vector.memset(window[0:SCALE_ROWS, :], 0)
             scale_window.append(window)
 
         planes = []
         for t in range(2):
-            plane = held.tile([P, PASSES, J // 4], I32, name="planes%d" % t, align_bytes=64)
+            plane = sbuf("planes%d" % t, [P, PASSES * J // 4], I32)
             nc.gpsimd.memset(plane[:], 0)
             planes.append(plane)
 
-        def load_words(t, words, slot):
-            window = held.tile([P, T], I32, name="word_window%d" % t, tag=slot, align_bytes=64)
+        def load_words(t, words):
+            window = sbuf("word_window%d" % t, [P, T], I32)
             nc.sync.dma_start(window[:], words[0].rearrange("p t b -> p (t b)").bitcast(I32))
             return window
 
         raw = {}
 
-        def load_weight(name, w, a, slot):
-            raw[name, a] = held.tile([P, 4, N], F32, name="raw_%s%d" % (name, a), tag=slot, align_bytes=64)
+        def load_weight(name, w, a):
+            raw[name, a] = sbuf("raw_%s%d" % (name, a), [P, 4, N], F32)
             nc.sync.dma_start(raw[name, a][:], w[K_PASS * a : K_PASS * (a + 1), :].rearrange("(p i) n -> p i n", i=4))
 
-        def load_gates(n, slot):
-            window = held.tile([P, T], F32, name="gate_window%d" % n, tag=slot, align_bytes=64)
+        def load_gates(n):
+            window = sbuf("gate_window%d" % n, [P, T], F32)
             nc.sync.dma_start(window[:], gT[n * P : (n + 1) * P, :])
             return window
 
         def pick_scales(t):
-            picked = held.tile([P, J], U8, name="picked_scales%d" % t, align_bytes=64)
+            picked = sbuf("picked_scales%d" % t, [P, J], U8)
             nc.vector.tensor_copy(picked[:], scale_window[t][:].bitcast(U8).indirect(offsets[:]))
-            for a in range(PASSES):
-                for quadrant in range(4):
-                    row = SCALE_ROWS + 16 * a + 4 * quadrant
-                    queue = nc.gpsimd if quadrant == 3 else nc.sync
-                    queue.dma_start(
-                        planes[t][32 * quadrant : 32 * quadrant + 4, a, :], picked[row : row + 4, :].bitcast(I32)
-                    )
+            for quadrant in (0, 2, 1, 3):
+                row = SCALE_ROWS + 8 * quadrant
+                nc.sync.dma_start(planes[t][32 * quadrant : 32 * quadrant + 4, :], picked[row : row + 8, :].bitcast(I32))
 
-        load_weight("wi", wi, 0, "slot3")
-        load_weight("wi", wi, 1, "slot4")
-        word_window = [load_words(0, tab_words, "slot2")]
-        load_weight("wr", wr, 0, "slot5")
+        load_weight("wi", wi, 0)
+        load_weight("wi", wi, 1)
+        word_window = [load_words(0, tab_words)]
         pick_scales(0)
-        load_weight("wr", wr, 1, "slot0")
-        word_window.append(load_words(1, tab2_words, "slot1"))
+        word_window.append(load_words(1, tab2_words))
         pick_scales(1)
+        load_weight("wr", wr, 0)
+        load_weight("wr", wr, 1)
 
         grouped, codes, code_scales = {}, {}, {}
 
         def cast(name, a):
-            grouped[name, a] = held.tile([P, N, 4], BF16, name="grouped_%s%d" % (name, a), align_bytes=64)
+            grouped[name, a] = sbuf("grouped_%s%d" % (name, a), [P, N, 4], BF16)
             nc.scalar.activation(
                 grouped[name, a][:].rearrange("p (c m) i -> p c i m", m=4),
                 raw[name, a][:].rearrange("p i (c m) -> p c i m", m=4),
@@ -108,12 +157,12 @@ def tile_list_cpxtab_gate_kernel(
             )
 
         def negate(a):
-            grouped["neg", a] = held.tile([P, N, 4], BF16, name="grouped_neg%d" % a, align_bytes=64)
+            grouped["neg", a] = sbuf("grouped_neg%d" % a, [P, N, 4], BF16)
             nc.scalar.activation(grouped["neg", a][:], grouped["wi", a][:], COPY, scale=-1.0)
 
         def quantise(name, a):
-            codes[name, a] = held.tile([P, N], U32, name="codes_%s%d" % (name, a), align_bytes=64)
-            code_scales[name, a] = held.tile([P, N], U8, name="code_scales_%s%d" % (name, a), align_bytes=64)
+            codes[name, a] = sbuf("codes_%s%d" % (name, a), [P, N], U32)
+            code_scales[name, a] = sbuf("code_scales_%s%d" % (name, a), [P, N], U8)
             nc.vector.quantize_mx(
                 out=codes[name, a][:].bitcast(FP8X4),
                 scales=code_scales[name, a][:],
@@ -127,133 +176,134 @@ def tile_list_cpxtab_gate_kernel(
         for a in range(PASSES):
             cast("wr", a)
 
-        parted = {}
+        picked, parted = {}, {}
 
-        def gather_words(t, c, picked):
-            nc.vector.tensor_copy(picked[:], word_window[t][:].bitcast(U32).indirect(listed(c * CHUNK, CHUNK)))
-            return picked
+        def gather_words(t, c):
+            picked[t, c] = sbuf("picked%d_%d" % (t, c), [P, CHUNK], U32)
+            nc.vector.tensor_copy(picked[t, c][:], word_window[t][:].bitcast(U32).indirect(listed(c * CHUNK, CHUNK)))
 
-        def part_words(t, c, picked):
-            parted[t, c] = held.tile([P, PASSES, CHUNK], U16, name="parted%d_%d" % (t, c), align_bytes=64)
+        def part_words(t, c):
+            parted[t, c] = sbuf("parted%d_%d" % (t, c), [P, PASSES, CHUNK], U16)
             nc.vector.tensor_copy(
                 parted[t, c][:].rearrange("p d (h j) -> p h d j", h=2),
-                picked[:].bitcast(U16).rearrange("p (h j d) -> p h d j", h=2, d=2),
+                picked[t, c][:].bitcast(U16).rearrange("p (h j d) -> p h d j", h=2, d=2),
             )
-
-        def early_tile():
-            return word_ring.tile([P, CHUNK], U32, name="picked_words", align_bytes=64)
-
-        def late_tile(a):
-            return held.tile([P, CHUNK], U32, name="picked_late", tag="grouped_wr%d" % a, align_bytes=64)
 
         for a in range(PASSES):
             quantise("wi", a)
-        early = [gather_words(0, c, early_tile()) for c in range(CHUNKS - 1)]
-        part_words(0, 0, early[0])
-        for a in range(PASSES):
-            quantise("neg", a)
-        part_words(0, 1, early[1])
+        for t in range(2):
+            for c in range(2):
+                gather_words(t, c)
+            for c in range(2):
+                part_words(t, c)
+            if t == 0:
+                for a in range(PASSES):
+                    quantise("neg", a)
+        gate_window = [load_gates(n) for n in range(ROW_TILES)]
         quantise("wr", 0)
-        part_words(0, 2, early[2])
-        late = [(1, 0), (1, 1), (0, CHUNKS - 1)] + [(1, c) for c in range(2, CHUNKS)]
-        picked_late = [gather_words(*late[0], late_tile(0))]
+        for t in (1, 0):
+            gather_words(t, 2)
         quantise("wr", 1)
-        picked_late.append(gather_words(*late[1], late_tile(1)))
-        for u, (t, c) in enumerate(late):
-            part_words(t, c, picked_late[u])
-            if u + 2 < len(late):
-                picked_late.append(gather_words(*late[u + 2], late_tile(u % 2)))
-        gate_window = [load_gates(n, slot) for n, slot in enumerate(("slot5", "slot0", "slot2", "slot1"))]
+        for t in (1, 0):
+            part_words(t, 2)
+        for t in (1, 0):
+            gather_words(t, 3)
+        for t in (1, 0):
+            part_words(t, 3)
 
         terms = ((("wr", 0), ("neg", 1)), (("wi", 0), ("wr", 1)))
-
-        pieces = [(n, h) for n in range(ROW_TILES) for h in range(HALVES)]
+        pieces = [(n, (2 * h, 2 * h + 1)) for n in range(ROW_TILES) for h in range(HALVES)]
+        pieces[-1:] = [(ROW_TILES - 1, (c,)) for c in pieces[-1][1]]
 
         def on_gpsimd(n, c, o):
             return o == 1 or CHUNKS * n + c < REAL_ON_GPSIMD
 
-        banks, turns = {}, {True: [], False: []}
+        banks = {}
 
         def open_bank(n, c, o):
-            if o == 1 and c < 2:
-                number = ROW_TILES * c + n
-            else:
-                quick = on_gpsimd(n, c, o)
-                turn = len(turns[quick])
-                number = turn % QUICK_BANKS if quick else QUICK_BANKS + turn % (BANKS - QUICK_BANKS)
-                turns[quick].append((n, c, o))
-            banks[n, c, o] = psum.tile([P, CHUNK], F32, name="acc", tag="bank%d" % number)
+            banks[n, c, o] = psum.tile([P, CHUNK], F32, name="acc", tag="bank%d" % (len(banks) % BANKS))
 
-        def term_product(n, c, o, term):
-            if term == 0:
+        def mx_pass(n, c, o, step):
+            if step == 0:
                 open_bank(n, c, o)
-            name, t = terms[o][term]
-            for a in range(PASSES):
-                nc.tensor.matmul_mx(
-                    out=banks[n, c, o][:],
-                    lhsT=codes[name, a][:, n * P : (n + 1) * P].bitcast(FP8X4),
-                    lhsT_scale=code_scales[name, a][:, n * P : (n + 1) * P],
-                    rhs=parted[t, c][:, a, :].bitcast(FP4X4),
-                    rhs_scale=planes[t][:, a, (CHUNK // 4) * c : (CHUNK // 4) * (c + 1)].bitcast(U8),
-                    start=(term == 0 and a == 0),
-                    stop=(term == 1 and a == PASSES - 1),
-                )
+            name, t = terms[o][step // PASSES]
+            a = step % PASSES
+            first = (J * a + CHUNK * c) // 4
+            nc.tensor.matmul_mx(
+                out=banks[n, c, o][:],
+                lhsT=codes[name, a][:, n * P : (n + 1) * P].bitcast(FP8X4),
+                lhsT_scale=code_scales[name, a][:, n * P : (n + 1) * P],
+                rhs=parted[t, c][:, a, :].bitcast(FP4X4),
+                rhs_scale=planes[t][:, first : first + CHUNK // 4].bitcast(U8),
+                start=(step == 0),
+                stop=(step == 2 * PASSES - 1),
+            )
 
-        sums = {
-            (n, 1): held.tile([P, J], F32, name="sums%d" % n, tag=("slot3", "slot4", "sums2", "sums3")[n], align_bytes=64)
-            for n in range(ROW_TILES)
-        }
-        sums[0, 0] = held.tile([P, REAL_ON_GPSIMD * CHUNK], F32, name="first_real_sums", align_bytes=64)
+        sums = {}
+
+        def empty(n, c, o):
+            if (n, c // 2, o) not in sums:
+                sums[n, c // 2, o] = sbuf("sums%d_%d_%d" % (n, c // 2, o), [P, HALF], F32)
+            nc.scalar.activation(sums[n, c // 2, o][:, (c % 2) * CHUNK : (c % 2 + 1) * CHUNK], banks[n, c, o][:], COPY)
 
         def product(n, c, o):
-            if (n, c, o) not in banks:
-                term_product(n, c, o, 0)
-            term_product(n, c, o, 1)
+            for step in range(2 * PASSES):
+                mx_pass(n, c, o, step)
             if on_gpsimd(n, c, o):
-                nc.scalar.activation(sums[n, o][:, c * CHUNK : (c + 1) * CHUNK], banks[n, c, o][:], COPY)
+                empty(n, c, o)
 
-        for c in range(2):
-            for n in range(ROW_TILES):
-                term_product(n, c, 1, 0)
-        for c in range(2):
+        opening = [(n, c) for c in range(2) for n in range(ROW_TILES)]
+        for n, c in opening:
+            for step in range(PASSES):
+                mx_pass(n, c, 1, step)
+        for n, c in opening:
+            mx_pass(n, c, 1, 2)
+        for n, c in opening:
+            mx_pass(n, c, 1, 3)
+            empty(n, c, 1)
+
+        for c in range(2, CHUNKS):
             for n in range(ROW_TILES):
                 product(n, c, 1)
+        for c in range(REAL_ON_GPSIMD):
+            product(0, c, 0)
 
         def gather_gate(u):
-            n, h = pieces[u]
+            n, chunks = pieces[u]
             rows = slice(n * P, (n + 1) * P)
-            gate = gate_ring.tile([P, HALF], F32, name="gate", align_bytes=64)
-            nc.vector.tensor_copy(gate[:], gate_window[n][:].indirect(listed(h * HALF, HALF)))
+            gate = sbuf("gate%d" % u, [P, len(chunks) * CHUNK], F32)
+            nc.vector.tensor_copy(gate[:], gate_window[n][:].indirect(listed(chunks[0] * CHUNK, len(chunks) * CHUNK)))
             for o in (1, 0):
-                if not on_gpsimd(n, 2 * h, o):
+                mine = [c for c in chunks if on_gpsimd(n, c, o)]
+                if not mine:
                     continue
-                for c in (2 * h, 2 * h + 1):
-                    if (n, c, o) not in banks:
-                        product(n, c, o)
-                for c in (2 * h, 2 * h + 1):
-                    cols = slice(c * CHUNK, (c + 1) * CHUNK)
-                    gate_cols = slice((c % 2) * CHUNK, (c % 2 + 1) * CHUNK)
-                    nc.gpsimd.tensor_tensor(sums[n, o][:, cols], sums[n, o][:, cols], gate[:, gate_cols], MULT)
-                    if u + 1 == len(pieces):
-                        nc.sync.dma_start(outs[o][rows, cols], sums[n, o][:, cols])
-                if u + 1 < len(pieces):
-                    cols = slice(h * HALF, (h + 1) * HALF)
-                    nc.sync.dma_start(outs[o][rows, cols], sums[n, o][:, cols])
+                tile = sums[n, chunks[0] // 2, o]
+                for c in mine:
+                    cols = slice((c % 2) * CHUNK, (c % 2 + 1) * CHUNK)
+                    gate_cols = slice((c - chunks[0]) * CHUNK, (c - chunks[0] + 1) * CHUNK)
+                    nc.gpsimd.tensor_tensor(tile[:, cols], tile[:, cols], gate[:, gate_cols], MULT)
+                nc.scalar.dma_start(
+                    outs[o][rows, mine[0] * CHUNK : (mine[-1] + 1) * CHUNK],
+                    tile[:, (mine[0] % 2) * CHUNK : (mine[-1] % 2 + 1) * CHUNK],
+                )
             return gate
 
-        gates = [gather_gate(0)]
-        for u, (n, h) in enumerate(pieces):
-            if u + 1 < len(pieces):
-                gates.append(gather_gate(u + 1))
-            if on_gpsimd(n, 2 * h, 0):
-                continue
-            result = result_ring.tile([P, HALF], F32, name="real", align_bytes=64)
-            rows = slice(n * P, (n + 1) * P)
-            for c in (2 * h, 2 * h + 1):
+        def multiply(u):
+            n, chunks = pieces[u]
+            mine = [c for c in chunks if not on_gpsimd(n, c, 0)]
+            if not mine:
+                return
+            result = sbuf("result%d" % u, [P, len(mine) * CHUNK], F32)
+            for c in mine:
                 product(n, c, 0)
-                half_cols = slice((c % 2) * CHUNK, (c % 2 + 1) * CHUNK)
-                nc.vector.tensor_tensor(result[:, half_cols], banks[n, c, 0][:], gates[u][:, half_cols], MULT)
-                if u + 1 == len(pieces):
-                    nc.sync.dma_start(out_0[rows, c * CHUNK : (c + 1) * CHUNK], result[:, half_cols])
-            if u + 1 < len(pieces):
-                nc.sync.dma_start(out_0[rows, h * HALF : (h + 1) * HALF], result[:])
+                cols = slice((c - mine[0]) * CHUNK, (c - mine[0] + 1) * CHUNK)
+                gate_cols = slice((c - chunks[0]) * CHUNK, (c - chunks[0] + 1) * CHUNK)
+                nc.vector.tensor_tensor(result[:, cols], banks[n, c, 0][:], gates[u][:, gate_cols], MULT)
+            nc.sync.dma_start(out_0[n * P : (n + 1) * P, mine[0] * CHUNK : (mine[-1] + 1) * CHUNK], result[:])
+
+        gates = {}
+        for gathers, products in (((0, 1, 2, 3), (0, 1)), ((4, 5), (2, 3)), ((6,), (4,)), ((7,), (5, 6)), ((8,), (7, 8))):
+            for u in gathers:
+                gates[u] = gather_gate(u)
+            for u in products:
+                multiply(u)

@@ -25,7 +25,7 @@ HALF = 2 * CHUNK
 HALVES = J // HALF
 ROW_TILES = N // P
 SCALE_ROWS = 96
-REAL_ON_GPSIMD = 0
+REAL_ON_GPSIMD = 4
 QUICK_BANKS = 2
 BANKS = 8
 KIB = 1024
@@ -76,18 +76,14 @@ def tile_list_cpxtab_gate_kernel(
             "gate3": 20,
             "gate4": 24,
             "gate5": 28,
-            "gate6": 20,
-            "gate7": 24,
-            "gate8": 20,
-            "result0": 64,
-            "result1": 68,
+            "gate6": 16,
+            "gate7": 20,
             "result2": 80,
             "result3": 84,
-            "result4": 32,
-            "result5": 36,
-            "result6": 40,
-            "result7": 44,
-            "result8": 46,
+            "result4": 88,
+            "result5": 32,
+            "result6": 36,
+            "result7": 40,
         }
 
         def sbuf(name, shape, dtype):
@@ -213,7 +209,6 @@ def tile_list_cpxtab_gate_kernel(
 
         terms = ((("wr", 0), ("neg", 1)), (("wi", 0), ("wr", 1)))
         pieces = [(n, (2 * h, 2 * h + 1)) for n in range(ROW_TILES) for h in range(HALVES)]
-        pieces[-1:] = [(ROW_TILES - 1, (c,)) for c in pieces[-1][1]]
 
         def on_gpsimd(n, c, o):
             return o == 1 or CHUNKS * n + c < REAL_ON_GPSIMD
@@ -262,11 +257,11 @@ def tile_list_cpxtab_gate_kernel(
             mx_pass(n, c, 1, 3)
             empty(n, c, 1)
 
-        for c in range(2, CHUNKS):
-            for n in range(ROW_TILES):
-                product(n, c, 1)
-        for c in range(REAL_ON_GPSIMD):
-            product(0, c, 0)
+        for n, chunks in pieces:
+            for c in chunks:
+                for o in (1, 0):
+                    if on_gpsimd(n, c, o) and (n, c, o) not in banks:
+                        product(n, c, o)
 
         def gather_gate(u):
             n, chunks = pieces[u]
@@ -282,10 +277,13 @@ def tile_list_cpxtab_gate_kernel(
                     cols = slice((c % 2) * CHUNK, (c % 2 + 1) * CHUNK)
                     gate_cols = slice((c - chunks[0]) * CHUNK, (c - chunks[0] + 1) * CHUNK)
                     nc.gpsimd.tensor_tensor(tile[:, cols], tile[:, cols], gate[:, gate_cols], MULT)
-                nc.scalar.dma_start(
-                    outs[o][rows, mine[0] * CHUNK : (mine[-1] + 1) * CHUNK],
-                    tile[:, (mine[0] % 2) * CHUNK : (mine[-1] % 2 + 1) * CHUNK],
-                )
+                    if u + 1 == len(pieces):
+                        nc.sync.dma_start(outs[o][rows, c * CHUNK : (c + 1) * CHUNK], tile[:, cols])
+                if u + 1 < len(pieces):
+                    nc.sync.dma_start(
+                        outs[o][rows, mine[0] * CHUNK : (mine[-1] + 1) * CHUNK],
+                        tile[:, (mine[0] % 2) * CHUNK : (mine[-1] % 2 + 1) * CHUNK],
+                    )
             return gate
 
         def multiply(u):
@@ -299,11 +297,13 @@ def tile_list_cpxtab_gate_kernel(
                 cols = slice((c - mine[0]) * CHUNK, (c - mine[0] + 1) * CHUNK)
                 gate_cols = slice((c - chunks[0]) * CHUNK, (c - chunks[0] + 1) * CHUNK)
                 nc.vector.tensor_tensor(result[:, cols], banks[n, c, 0][:], gates[u][:, gate_cols], MULT)
-            nc.sync.dma_start(out_0[n * P : (n + 1) * P, mine[0] * CHUNK : (mine[-1] + 1) * CHUNK], result[:])
+                if u + 1 == len(pieces):
+                    nc.scalar.dma_start(out_0[n * P : (n + 1) * P, c * CHUNK : (c + 1) * CHUNK], result[:, cols])
+            if u + 1 < len(pieces):
+                nc.scalar.dma_start(out_0[n * P : (n + 1) * P, mine[0] * CHUNK : (mine[-1] + 1) * CHUNK], result[:])
 
-        gates = {}
-        for gathers, products in (((0, 1, 2, 3), (0, 1)), ((4, 5), (2, 3)), ((6,), (4,)), ((7,), (5, 6)), ((8,), (7, 8))):
-            for u in gathers:
-                gates[u] = gather_gate(u)
-            for u in products:
-                multiply(u)
+        gates = [gather_gate(0)]
+        for u in range(len(pieces)):
+            if u + 1 < len(pieces):
+                gates.append(gather_gate(u + 1))
+            multiply(u)

@@ -25,7 +25,7 @@ HALF = 2 * CHUNK
 HALVES = J // HALF
 ROW_TILES = N // P
 SCALE_ROWS = 96
-REAL_ON_GPSIMD = 4
+REAL_ON_GPSIMD = 2
 QUICK_BANKS = 2
 BANKS = 8
 KIB = 1024
@@ -43,47 +43,49 @@ def tile_list_cpxtab_gate_kernel(
 
         place = {
             "word_window0": 0,
-            "gate_window3": 116,
             "word_window1": 16,
-            "scale_window0": 16,
-            "raw_wi0": 32,
-            "raw_wi1": 40,
-            "gate_window0": 32,
-            "raw_wr0": 48,
-            "raw_wr1": 56,
-            "scale_window1": 54,
-            "picked1_2": 48,
-            "picked1_3": 48,
-            "parted1_2": 60,
-            "grouped_wi0": 64,
-            "grouped_wi1": 68,
-            "gate_window1": 64,
-            "grouped_neg0": 80,
-            "grouped_neg1": 116,
-            "gate_window2": 80,
-            "grouped_wr0": 96,
-            "picked0_2": 96,
-            "picked0_3": 96,
-            "grouped_wr1": 100,
-            "parted0_2": 100,
-            "picked0_0": 104,
-            "picked1_0": 104,
-            "picked0_1": 108,
-            "picked1_1": 108,
-            "gate0": 48,
-            "gate1": 96,
             "gate2": 16,
             "gate3": 20,
             "gate4": 24,
             "gate5": 28,
             "gate6": 16,
-            "gate7": 20,
-            "result2": 80,
-            "result3": 84,
-            "result4": 88,
-            "result5": 32,
-            "result6": 36,
-            "result7": 40,
+            "gate7": 24,
+            "gate8": 16,
+            "scale_window0": 30,
+            "raw_wr0": 32,
+            "picked0_3": 32,
+            "raw_wr1": 40,
+            "picked1_2": 40,
+            "gate0": 40,
+            "raw_wi0": 48,
+            "raw_wi1": 56,
+            "gate_window0": 48,
+            "result4_0": 48,
+            "result5_0": 52,
+            "result6_0": 56,
+            "result7_0": 60,
+            "result8_0": 62,
+            "grouped_wi0": 64,
+            "grouped_wi1": 68,
+            "scale_window1": 72,
+            "gate_window1": 64,
+            "grouped_neg0": 80,
+            "gate_window2": 80,
+            "result1_0": 80,
+            "result2_0": 84,
+            "result3_0": 88,
+            "result8_1": 92,
+            "grouped_wr0": 96,
+            "parted0_2": 96,
+            "grouped_wr1": 100,
+            "picked1_3": 100,
+            "gate1": 100,
+            "picked0_0": 104,
+            "picked1_0": 104,
+            "picked0_1": 108,
+            "picked1_1": 108,
+            "grouped_neg1": 116,
+            "gate_window3": 116,
         }
 
         def sbuf(name, shape, dtype):
@@ -99,9 +101,9 @@ def tile_list_cpxtab_gate_kernel(
 
         scale_window = []
         for t, scales in enumerate((tab_scales, tab2_scales)):
-            window = sbuf("scale_window%d" % t, [P, T // 4], I32)
+            window = sbuf("scale_window%d" % t, [P, (3 - 2 * t) * T // 4], I32)[:, 0 : T // 4]
             nc.sync.dma_start(window[SCALE_ROWS:P, :], scales.bitcast(I32).rearrange("a q t -> q a t"))
-            nc.vector.memset(window[0:SCALE_ROWS, :], 0)
+            nc.gpsimd.memset(window[0:SCALE_ROWS, :], 0)
             scale_window.append(window)
 
         planes = []
@@ -138,9 +140,9 @@ def tile_list_cpxtab_gate_kernel(
         word_window = [load_words(0, tab_words)]
         pick_scales(0)
         word_window.append(load_words(1, tab2_words))
-        pick_scales(1)
         load_weight("wr", wr, 0)
         load_weight("wr", wr, 1)
+        pick_scales(1)
 
         grouped, codes, code_scales = {}, {}, {}
 
@@ -195,23 +197,26 @@ def tile_list_cpxtab_gate_kernel(
             if t == 0:
                 for a in range(PASSES):
                     quantise("neg", a)
+                gather_words(0, 2)
         gate_window = [load_gates(n) for n in range(ROW_TILES)]
         quantise("wr", 0)
-        for t in (1, 0):
-            gather_words(t, 2)
+        gather_words(0, 3)
+        for c in (2, 3):
+            part_words(0, c)
         quantise("wr", 1)
-        for t in (1, 0):
-            part_words(t, 2)
-        for t in (1, 0):
-            gather_words(t, 3)
-        for t in (1, 0):
-            part_words(t, 3)
+        for c in (2, 3):
+            gather_words(1, c)
+        for c in (2, 3):
+            part_words(1, c)
 
         terms = ((("wr", 0), ("neg", 1)), (("wi", 0), ("wr", 1)))
         pieces = [(n, (2 * h, 2 * h + 1)) for n in range(ROW_TILES) for h in range(HALVES)]
+        pieces[-1:] = [(ROW_TILES - 1, (c,)) for c in pieces[-1][1]]
 
         def on_gpsimd(n, c, o):
-            return o == 1 or CHUNKS * n + c < REAL_ON_GPSIMD
+            if o == 1:
+                return (n, c) != (ROW_TILES - 1, CHUNKS - 1)
+            return CHUNKS * n + c < REAL_ON_GPSIMD or (n, c) == (ROW_TILES - 1, CHUNKS - 2)
 
         banks = {}
 
@@ -277,30 +282,27 @@ def tile_list_cpxtab_gate_kernel(
                     cols = slice((c % 2) * CHUNK, (c % 2 + 1) * CHUNK)
                     gate_cols = slice((c - chunks[0]) * CHUNK, (c - chunks[0] + 1) * CHUNK)
                     nc.gpsimd.tensor_tensor(tile[:, cols], tile[:, cols], gate[:, gate_cols], MULT)
-                    if u + 1 == len(pieces):
-                        nc.sync.dma_start(outs[o][rows, c * CHUNK : (c + 1) * CHUNK], tile[:, cols])
-                if u + 1 < len(pieces):
-                    nc.sync.dma_start(
-                        outs[o][rows, mine[0] * CHUNK : (mine[-1] + 1) * CHUNK],
-                        tile[:, (mine[0] % 2) * CHUNK : (mine[-1] % 2 + 1) * CHUNK],
-                    )
+                nc.sync.dma_start(
+                    outs[o][rows, mine[0] * CHUNK : (mine[-1] + 1) * CHUNK],
+                    tile[:, (mine[0] % 2) * CHUNK : (mine[-1] % 2 + 1) * CHUNK],
+                )
             return gate
 
         def multiply(u):
             n, chunks = pieces[u]
-            mine = [c for c in chunks if not on_gpsimd(n, c, 0)]
-            if not mine:
-                return
-            result = sbuf("result%d" % u, [P, len(mine) * CHUNK], F32)
-            for c in mine:
-                product(n, c, 0)
-                cols = slice((c - mine[0]) * CHUNK, (c - mine[0] + 1) * CHUNK)
-                gate_cols = slice((c - chunks[0]) * CHUNK, (c - chunks[0] + 1) * CHUNK)
-                nc.vector.tensor_tensor(result[:, cols], banks[n, c, 0][:], gates[u][:, gate_cols], MULT)
-                if u + 1 == len(pieces):
-                    nc.scalar.dma_start(out_0[n * P : (n + 1) * P, c * CHUNK : (c + 1) * CHUNK], result[:, cols])
-            if u + 1 < len(pieces):
-                nc.scalar.dma_start(out_0[n * P : (n + 1) * P, mine[0] * CHUNK : (mine[-1] + 1) * CHUNK], result[:])
+            for o in range(2):
+                mine = [c for c in chunks if not on_gpsimd(n, c, o)]
+                if not mine:
+                    continue
+                result = sbuf("result%d_%d" % (u, o), [P, len(mine) * CHUNK], F32)
+                for c in mine:
+                    product(n, c, o)
+                    cols = slice((c - mine[0]) * CHUNK, (c - mine[0] + 1) * CHUNK)
+                    gate_cols = slice((c - chunks[0]) * CHUNK, (c - chunks[0] + 1) * CHUNK)
+                    nc.vector.tensor_tensor(result[:, cols], banks[n, c, o][:], gates[u][:, gate_cols], MULT)
+                nc.scalar.dma_start(
+                    outs[o][n * P : (n + 1) * P, mine[0] * CHUNK : (mine[-1] + 1) * CHUNK], result[:]
+                )
 
         gates = [gather_gate(0)]
         for u in range(len(pieces)):

@@ -25,7 +25,7 @@ HALF = 2 * CHUNK
 HALVES = J // HALF
 ROW_TILES = N // P
 SCALE_ROWS = 96
-REAL_ON_GPSIMD = 2
+REAL_ON_GPSIMD = 3
 QUICK_BANKS = 2
 BANKS = 8
 KIB = 1024
@@ -48,9 +48,6 @@ def tile_list_cpxtab_gate_kernel(
             "gate3": 20,
             "gate4": 24,
             "gate5": 28,
-            "gate6": 16,
-            "gate7": 24,
-            "gate8": 16,
             "scale_window0": 30,
             "raw_wr0": 32,
             "picked0_3": 32,
@@ -60,37 +57,45 @@ def tile_list_cpxtab_gate_kernel(
             "raw_wi0": 48,
             "raw_wi1": 56,
             "gate_window0": 48,
-            "result4_0": 48,
-            "result5_0": 52,
-            "result6_0": 56,
-            "result7_0": 60,
-            "result8_0": 62,
-            "grouped_wi0": 64,
-            "grouped_wi1": 68,
+            "result2_0": 48,
+            "result3_0": 50,
+            "result4_0": 54,
+            "result5_0": 58,
+            "result9_0": 62,
+            "grouped_wi0_0": 64,
+            "grouped_wi1_0": 68,
             "scale_window1": 72,
             "gate_window1": 64,
-            "grouped_neg0": 80,
+            "result6_0": 64,
+            "result7_0": 68,
+            "result9_1": 72,
+            "result8_0": 74,
+            "grouped_neg0_0": 80,
             "gate_window2": 80,
-            "result1_0": 80,
-            "result2_0": 84,
-            "result3_0": 88,
-            "result8_1": 92,
-            "grouped_wr0": 96,
+            "grouped_wr0_0": 96,
             "parted0_2": 96,
-            "grouped_wr1": 100,
-            "picked1_3": 100,
-            "gate1": 100,
+            "grouped_wr1_0": 100,
+            "grouped_wr1_2": 102,
+            "picked1_3": 102,
+            "gate1": 102,
             "picked0_0": 104,
             "picked1_0": 104,
             "picked0_1": 108,
             "picked1_1": 108,
-            "grouped_neg1": 116,
+            "parted0_1": 112,
+            "gate9": 112,
+            "gate6": 132,
+            "codes_wr1_0": 135.5,
+            "gate7": 136,
+            "codes_wr1_2": 140,
+            "gate8": 140,
+            "grouped_neg1_0": 116,
             "gate_window3": 116,
         }
 
         def sbuf(name, shape, dtype):
             if name in place:
-                return shared.tile(shape, dtype, name=name, align_bytes=64, offset=place[name] * KIB)
+                return shared.tile(shape, dtype, name=name, align_bytes=64, offset=int(place[name] * KIB))
             return held.tile(shape, dtype, name=name, align_bytes=64)
 
         offsets = held.tile([P, J // 16], U16, name="offsets")
@@ -146,33 +151,38 @@ def tile_list_cpxtab_gate_kernel(
 
         grouped, codes, code_scales = {}, {}, {}
 
-        def cast(name, a):
-            grouped[name, a] = sbuf("grouped_%s%d" % (name, a), [P, N, 4], BF16)
+        def cast(name, a, first=0, count=ROW_TILES):
+            key = name, a, first
+            grouped[key] = sbuf("grouped_%s%d_%d" % key, [P, count * P, 4], BF16)
             nc.scalar.activation(
-                grouped[name, a][:].rearrange("p (c m) i -> p c i m", m=4),
-                raw[name, a][:].rearrange("p i (c m) -> p c i m", m=4),
+                grouped[key][:].rearrange("p (c m) i -> p c i m", m=4),
+                raw[name, a][:, :, first * P : (first + count) * P].rearrange("p i (c m) -> p c i m", m=4),
                 COPY,
             )
 
         def negate(a):
-            grouped["neg", a] = sbuf("grouped_neg%d" % a, [P, N, 4], BF16)
-            nc.scalar.activation(grouped["neg", a][:], grouped["wi", a][:], COPY, scale=-1.0)
+            grouped["neg", a, 0] = sbuf("grouped_neg%d_0" % a, [P, N, 4], BF16)
+            nc.scalar.activation(grouped["neg", a, 0][:], grouped["wi", a, 0][:], COPY, scale=-1.0)
 
-        def quantise(name, a):
-            codes[name, a] = sbuf("codes_%s%d" % (name, a), [P, N], U32)
-            code_scales[name, a] = sbuf("code_scales_%s%d" % (name, a), [P, N], U8)
+        def quantise(name, a, first=0, count=ROW_TILES, source=0):
+            key = name, a, first
+            values = grouped[name, a, source][:, (first - source) * P : (first - source + count) * P, :]
+            words = sbuf("codes_%s%d_%d" % key, [P, count * P], U32)
+            scales = sbuf("code_scales_%s%d_%d" % key, [P, count * P], U8)
             nc.vector.quantize_mx(
-                out=codes[name, a][:].bitcast(FP8X4),
-                scales=code_scales[name, a][:],
-                in_=grouped[name, a][:].rearrange("p n i -> p (n i)"),
+                out=words[:].bitcast(FP8X4), scales=scales[:], in_=values.rearrange("p n i -> p (n i)")
             )
+            for n in range(count):
+                codes[name, a, first + n] = words[:, n * P : (n + 1) * P]
+                code_scales[name, a, first + n] = scales[:, n * P : (n + 1) * P]
 
         for a in range(PASSES):
             cast("wi", a)
         for a in range(PASSES):
             negate(a)
-        for a in range(PASSES):
-            cast("wr", a)
+        cast("wr", 0)
+        for first in (0, 2):
+            cast("wr", 1, first, 2)
 
         picked, parted = {}, {}
 
@@ -201,27 +211,31 @@ def tile_list_cpxtab_gate_kernel(
         gate_window = [load_gates(n) for n in range(ROW_TILES)]
         quantise("wr", 0)
         gather_words(0, 3)
-        for c in (2, 3):
-            part_words(0, c)
-        quantise("wr", 1)
+        quantise("wr", 1, 0, 2)
+        part_words(0, 2)
+        quantise("wr", 1, 2, 1, 2)
+        quantise("wr", 1, 3, 1, 2)
+        part_words(0, 3)
         for c in (2, 3):
             gather_words(1, c)
         for c in (2, 3):
             part_words(1, c)
 
-        terms = ((("wr", 0), ("neg", 1)), (("wi", 0), ("wr", 1)))
+        terms = ((("neg", 1), ("wr", 0)), (("wi", 0), ("wr", 1)))
         pieces = [(n, (2 * h, 2 * h + 1)) for n in range(ROW_TILES) for h in range(HALVES)]
+        pieces[:1] = [(0, (c,)) for c in pieces[0][1]]
         pieces[-1:] = [(ROW_TILES - 1, (c,)) for c in pieces[-1][1]]
 
         def on_gpsimd(n, c, o):
             if o == 1:
                 return (n, c) != (ROW_TILES - 1, CHUNKS - 1)
-            return CHUNKS * n + c < REAL_ON_GPSIMD or (n, c) == (ROW_TILES - 1, CHUNKS - 2)
+            return CHUNKS * n + c < REAL_ON_GPSIMD
 
         banks = {}
 
         def open_bank(n, c, o):
-            banks[n, c, o] = psum.tile([P, CHUNK], F32, name="acc", tag="bank%d" % (len(banks) % BANKS))
+            number = 2 * n + c if len(banks) < BANKS else len(banks) % BANKS
+            banks[n, c, o] = psum.tile([P, CHUNK], F32, name="acc", tag="bank%d" % number)
 
         def mx_pass(n, c, o, step):
             if step == 0:
@@ -231,8 +245,8 @@ def tile_list_cpxtab_gate_kernel(
             first = (J * a + CHUNK * c) // 4
             nc.tensor.matmul_mx(
                 out=banks[n, c, o][:],
-                lhsT=codes[name, a][:, n * P : (n + 1) * P].bitcast(FP8X4),
-                lhsT_scale=code_scales[name, a][:, n * P : (n + 1) * P],
+                lhsT=codes[name, a, n].bitcast(FP8X4),
+                lhsT_scale=code_scales[name, a, n],
                 rhs=parted[t, c][:, a, :].bitcast(FP4X4),
                 rhs_scale=planes[t][:, first : first + CHUNK // 4].bitcast(U8),
                 start=(step == 0),
@@ -258,15 +272,9 @@ def tile_list_cpxtab_gate_kernel(
                 mx_pass(n, c, 1, step)
         for n, c in opening:
             mx_pass(n, c, 1, 2)
-        for n, c in opening:
+        for n, c in sorted(opening):
             mx_pass(n, c, 1, 3)
             empty(n, c, 1)
-
-        for n, chunks in pieces:
-            for c in chunks:
-                for o in (1, 0):
-                    if on_gpsimd(n, c, o) and (n, c, o) not in banks:
-                        product(n, c, o)
 
         def gather_gate(u):
             n, chunks = pieces[u]
@@ -282,10 +290,12 @@ def tile_list_cpxtab_gate_kernel(
                     cols = slice((c % 2) * CHUNK, (c % 2 + 1) * CHUNK)
                     gate_cols = slice((c - chunks[0]) * CHUNK, (c - chunks[0] + 1) * CHUNK)
                     nc.gpsimd.tensor_tensor(tile[:, cols], tile[:, cols], gate[:, gate_cols], MULT)
-                nc.sync.dma_start(
-                    outs[o][rows, mine[0] * CHUNK : (mine[-1] + 1) * CHUNK],
-                    tile[:, (mine[0] % 2) * CHUNK : (mine[-1] % 2 + 1) * CHUNK],
-                )
+                last = mine[-1]
+                if last % 2 == 1 or not on_gpsimd(n, last + 1, o):
+                    nc.sync.dma_start(
+                        outs[o][rows, (last - last % 2) * CHUNK : (last + 1) * CHUNK],
+                        tile[:, 0 : (last % 2 + 1) * CHUNK],
+                    )
             return gate
 
         def multiply(u):
@@ -300,12 +310,20 @@ def tile_list_cpxtab_gate_kernel(
                     cols = slice((c - mine[0]) * CHUNK, (c - mine[0] + 1) * CHUNK)
                     gate_cols = slice((c - chunks[0]) * CHUNK, (c - chunks[0] + 1) * CHUNK)
                     nc.vector.tensor_tensor(result[:, cols], banks[n, c, o][:], gates[u][:, gate_cols], MULT)
-                nc.scalar.dma_start(
-                    outs[o][n * P : (n + 1) * P, mine[0] * CHUNK : (mine[-1] + 1) * CHUNK], result[:]
-                )
+                    if n == ROW_TILES - 1:
+                        nc.scalar.dma_start(outs[o][n * P : (n + 1) * P, c * CHUNK : (c + 1) * CHUNK], result[:, cols])
+                if n < ROW_TILES - 1:
+                    nc.scalar.dma_start(
+                        outs[o][n * P : (n + 1) * P, mine[0] * CHUNK : (mine[-1] + 1) * CHUNK], result[:]
+                    )
 
-        gates = [gather_gate(0)]
-        for u in range(len(pieces)):
-            if u + 1 < len(pieces):
-                gates.append(gather_gate(u + 1))
-            multiply(u)
+        gates = {}
+        for n in range(ROW_TILES):
+            for c in range(CHUNKS):
+                for o in (1, 0):
+                    if on_gpsimd(n, c, o) and (n, c, o) not in banks:
+                        product(n, c, o)
+            for u in range(len(pieces)):
+                if pieces[u][0] == n:
+                    gates[u] = gather_gate(u)
+                    multiply(u)

@@ -51,6 +51,8 @@ def tile_list_cpxtab_gate_kernel(
             "scale_window0": 30,
             "raw_wr0": 32,
             "picked0_3": 32,
+            "parted1_1": 36,
+            "scale_window1": 40,
             "raw_wr1": 40,
             "picked1_2": 40,
             "gate0": 40,
@@ -58,19 +60,17 @@ def tile_list_cpxtab_gate_kernel(
             "raw_wi1": 56,
             "gate_window0": 48,
             "result2_0": 48,
-            "result3_0": 50,
+            "result3_0": 52,
             "result4_0": 54,
             "result5_0": 58,
             "result9_0": 62,
-            "grouped_wi0_0": 64,
-            "grouped_wi1_0": 68,
-            "scale_window1": 72,
+            "grouped_wi": 64,
             "gate_window1": 64,
             "result6_0": 64,
             "result7_0": 68,
             "result9_1": 72,
             "result8_0": 74,
-            "grouped_neg0_0": 80,
+            "grouped_neg": 80,
             "gate_window2": 80,
             "grouped_wr0_0": 96,
             "parted0_2": 96,
@@ -89,7 +89,7 @@ def tile_list_cpxtab_gate_kernel(
             "gate7": 136,
             "codes_wr1_2": 140,
             "gate8": 140,
-            "grouped_neg1_0": 116,
+            "picked0_2": 116,
             "gate_window3": 116,
         }
 
@@ -106,7 +106,7 @@ def tile_list_cpxtab_gate_kernel(
 
         scale_window = []
         for t, scales in enumerate((tab_scales, tab2_scales)):
-            window = sbuf("scale_window%d" % t, [P, (3 - 2 * t) * T // 4], I32)[:, 0 : T // 4]
+            window = sbuf("scale_window%d" % t, [P, T // 4], I32)
             nc.sync.dma_start(window[SCALE_ROWS:P, :], scales.bitcast(I32).rearrange("a q t -> q a t"))
             nc.gpsimd.memset(window[0:SCALE_ROWS, :], 0)
             scale_window.append(window)
@@ -146,43 +146,38 @@ def tile_list_cpxtab_gate_kernel(
         pick_scales(0)
         word_window.append(load_words(1, tab2_words))
         load_weight("wr", wr, 0)
-        load_weight("wr", wr, 1)
         pick_scales(1)
+        load_weight("wr", wr, 1)
 
-        grouped, codes, code_scales = {}, {}, {}
+        codes, code_scales = {}, {}
 
-        def cast(name, a, first=0, count=ROW_TILES):
-            key = name, a, first
-            grouped[key] = sbuf("grouped_%s%d_%d" % key, [P, count * P, 4], BF16)
+        def cast(target, source):
             nc.scalar.activation(
-                grouped[key][:].rearrange("p (c m) i -> p c i m", m=4),
-                raw[name, a][:, :, first * P : (first + count) * P].rearrange("p i (c m) -> p c i m", m=4),
-                COPY,
+                target.rearrange("p (c m i) -> p c i m", m=4, i=4), source.rearrange("p i (c m) -> p c i m", m=4), COPY
             )
 
-        def negate(a):
-            grouped["neg", a, 0] = sbuf("grouped_neg%d_0" % a, [P, N, 4], BF16)
-            nc.scalar.activation(grouped["neg", a, 0][:], grouped["wi", a, 0][:], COPY, scale=-1.0)
+        def quantise(name, values, parts):
+            width = len(parts) * P
+            label = "%s%d_%d" % (name, *parts[0])
+            words = sbuf("codes_" + label, [P, width], U32)
+            scales = sbuf("code_scales_" + label, [P, width], U8)
+            nc.vector.quantize_mx(out=words[:].bitcast(FP8X4), scales=scales[:], in_=values)
+            for k, (a, n) in enumerate(parts):
+                codes[name, a, n] = words[:, k * P : (k + 1) * P]
+                code_scales[name, a, n] = scales[:, k * P : (k + 1) * P]
 
-        def quantise(name, a, first=0, count=ROW_TILES, source=0):
-            key = name, a, first
-            values = grouped[name, a, source][:, (first - source) * P : (first - source + count) * P, :]
-            words = sbuf("codes_%s%d_%d" % key, [P, count * P], U32)
-            scales = sbuf("code_scales_%s%d_%d" % key, [P, count * P], U8)
-            nc.vector.quantize_mx(
-                out=words[:].bitcast(FP8X4), scales=scales[:], in_=values.rearrange("p n i -> p (n i)")
-            )
-            for n in range(count):
-                codes[name, a, first + n] = words[:, n * P : (n + 1) * P]
-                code_scales[name, a, first + n] = scales[:, n * P : (n + 1) * P]
-
+        grouped_wi = sbuf("grouped_wi", [P, PASSES * 4 * N], BF16)
+        grouped_neg = sbuf("grouped_neg", [P, PASSES * 4 * N], BF16)
         for a in range(PASSES):
-            cast("wi", a)
-        for a in range(PASSES):
-            negate(a)
-        cast("wr", 0)
+            cast(grouped_wi[:, a * 4 * N : (a + 1) * 4 * N], raw["wi", a][:])
+        nc.scalar.activation(grouped_neg[:], grouped_wi[:], COPY, scale=-1.0)
+        grouped_wr0 = sbuf("grouped_wr0_0", [P, 4 * N], BF16)
+        cast(grouped_wr0[:], raw["wr", 0][:])
+        grouped_wr1 = {}
         for first in (0, 2):
-            cast("wr", 1, first, 2)
+            grouped_wr1[first] = sbuf("grouped_wr1_%d" % first, [P, 2 * N], BF16)
+            cast(grouped_wr1[first][:], raw["wr", 1][:, :, first * P : (first + 2) * P])
+        every_part = [(a, n) for a in range(PASSES) for n in range(ROW_TILES)]
 
         picked, parted = {}, {}
 
@@ -197,29 +192,29 @@ def tile_list_cpxtab_gate_kernel(
                 picked[t, c][:].bitcast(U16).rearrange("p (h j d) -> p h d j", h=2, d=2),
             )
 
-        for a in range(PASSES):
-            quantise("wi", a)
-        for t in range(2):
-            for c in range(2):
-                gather_words(t, c)
-            for c in range(2):
-                part_words(t, c)
-            if t == 0:
-                for a in range(PASSES):
-                    quantise("neg", a)
-                gather_words(0, 2)
-        gate_window = [load_gates(n) for n in range(ROW_TILES)]
-        quantise("wr", 0)
+        quantise("wi", grouped_wi[:], every_part)
+        for c in range(2):
+            gather_words(0, c)
+        for c in range(2):
+            part_words(0, c)
+        quantise("neg", grouped_neg[:], every_part)
+        gather_words(0, 2)
+        for c in range(2):
+            gather_words(1, c)
+        part_words(1, 0)
+        quantise("wr", grouped_wr0[:], every_part[:ROW_TILES])
+        part_words(1, 1)
         gather_words(0, 3)
-        quantise("wr", 1, 0, 2)
+        quantise("wr", grouped_wr1[0][:], [(1, 0), (1, 1)])
         part_words(0, 2)
-        quantise("wr", 1, 2, 1, 2)
-        quantise("wr", 1, 3, 1, 2)
+        for n in (2, 3):
+            quantise("wr", grouped_wr1[2][:, (n - 2) * N : (n - 1) * N], [(1, n)])
         part_words(0, 3)
         for c in (2, 3):
             gather_words(1, c)
         for c in (2, 3):
             part_words(1, c)
+        gate_window = [load_gates(n) for n in range(ROW_TILES)]
 
         terms = ((("neg", 1), ("wr", 0)), (("wi", 0), ("wr", 1)))
         pieces = [(n, (2 * h, 2 * h + 1)) for n in range(ROW_TILES) for h in range(HALVES)]
@@ -229,7 +224,7 @@ def tile_list_cpxtab_gate_kernel(
         def on_gpsimd(n, c, o):
             if o == 1:
                 return (n, c) != (ROW_TILES - 1, CHUNKS - 1)
-            return CHUNKS * n + c < REAL_ON_GPSIMD
+            return c < 2 and 2 * n + c < REAL_ON_GPSIMD
 
         banks = {}
 
@@ -275,6 +270,9 @@ def tile_list_cpxtab_gate_kernel(
         for n, c in sorted(opening):
             mx_pass(n, c, 1, 3)
             empty(n, c, 1)
+
+        for n, c in sorted(opening)[:REAL_ON_GPSIMD]:
+            product(n, c, 0)
 
         def gather_gate(u):
             n, chunks = pieces[u]

@@ -51,25 +51,21 @@ def tile_list_cpxtab_gate_kernel(
             "scale_window0": 30,
             "raw_wr0": 32,
             "picked0_3": 32,
-            "parted1_1": 36,
-            "scale_window1": 40,
+            "scale_window1": 72,
             "raw_wr1": 40,
             "picked1_2": 40,
             "gate0": 40,
             "raw_wi0": 48,
             "raw_wi1": 56,
             "gate_window0": 48,
-            "result2_0": 48,
-            "result3_0": 52,
-            "result4_0": 54,
-            "result5_0": 58,
-            "result9_0": 62,
+            "result0_1_0": 48,
+            "result1_1_0": 52,
+            "result2_0_0": 56,
+            "result2_1_0": 60,
             "grouped_wi": 64,
             "gate_window1": 64,
-            "result6_0": 64,
-            "result7_0": 68,
-            "result9_1": 72,
-            "result8_0": 74,
+            "result3_0_0": 64,
+            "result3_1_0": 68,
             "grouped_neg": 80,
             "gate_window2": 80,
             "grouped_wr0_0": 96,
@@ -82,20 +78,21 @@ def tile_list_cpxtab_gate_kernel(
             "picked1_0": 104,
             "picked0_1": 108,
             "picked1_1": 108,
-            "parted0_1": 112,
+            "parted1_1": 112,
             "gate9": 112,
+            "parted1_0": 114,
+            "gate8": 114,
+            "codes_wr1_0": 132,
             "gate6": 132,
-            "codes_wr1_0": 135.5,
+            "codes_wr1_2": 136,
             "gate7": 136,
-            "codes_wr1_2": 140,
-            "gate8": 140,
             "picked0_2": 116,
             "gate_window3": 116,
         }
 
         def sbuf(name, shape, dtype):
             if name in place:
-                return shared.tile(shape, dtype, name=name, align_bytes=64, offset=int(place[name] * KIB))
+                return shared.tile(shape, dtype, name=name, align_bytes=64, offset=place[name] * KIB)
             return held.tile(shape, dtype, name=name, align_bytes=64)
 
         offsets = held.tile([P, J // 16], U16, name="offsets")
@@ -106,7 +103,7 @@ def tile_list_cpxtab_gate_kernel(
 
         scale_window = []
         for t, scales in enumerate((tab_scales, tab2_scales)):
-            window = sbuf("scale_window%d" % t, [P, T // 4], I32)
+            window = sbuf("scale_window%d" % t, [P, (3 - 2 * t) * T // 4], I32)[:, 0 : T // 4]
             nc.sync.dma_start(window[SCALE_ROWS:P, :], scales.bitcast(I32).rearrange("a q t -> q a t"))
             nc.gpsimd.memset(window[0:SCALE_ROWS, :], 0)
             scale_window.append(window)
@@ -146,8 +143,8 @@ def tile_list_cpxtab_gate_kernel(
         pick_scales(0)
         word_window.append(load_words(1, tab2_words))
         load_weight("wr", wr, 0)
-        pick_scales(1)
         load_weight("wr", wr, 1)
+        pick_scales(1)
 
         codes, code_scales = {}, {}
 
@@ -201,9 +198,9 @@ def tile_list_cpxtab_gate_kernel(
         gather_words(0, 2)
         for c in range(2):
             gather_words(1, c)
-        part_words(1, 0)
+        for c in range(2):
+            part_words(1, c)
         quantise("wr", grouped_wr0[:], every_part[:ROW_TILES])
-        part_words(1, 1)
         gather_words(0, 3)
         quantise("wr", grouped_wr1[0][:], [(1, 0), (1, 1)])
         part_words(0, 2)
@@ -216,7 +213,7 @@ def tile_list_cpxtab_gate_kernel(
             part_words(1, c)
         gate_window = [load_gates(n) for n in range(ROW_TILES)]
 
-        terms = ((("neg", 1), ("wr", 0)), (("wi", 0), ("wr", 1)))
+        terms = ((("wr", 0), ("neg", 1)), (("wi", 0), ("wr", 1)))
         pieces = [(n, (2 * h, 2 * h + 1)) for n in range(ROW_TILES) for h in range(HALVES)]
         pieces[:1] = [(0, (c,)) for c in pieces[0][1]]
         pieces[-1:] = [(ROW_TILES - 1, (c,)) for c in pieces[-1][1]]
@@ -274,54 +271,78 @@ def tile_list_cpxtab_gate_kernel(
         for n, c in sorted(opening)[:REAL_ON_GPSIMD]:
             product(n, c, 0)
 
+        gates = {}
+
         def gather_gate(u):
             n, chunks = pieces[u]
-            rows = slice(n * P, (n + 1) * P)
             gate = sbuf("gate%d" % u, [P, len(chunks) * CHUNK], F32)
             nc.vector.tensor_copy(gate[:], gate_window[n][:].indirect(listed(chunks[0] * CHUNK, len(chunks) * CHUNK)))
-            for o in (1, 0):
-                mine = [c for c in chunks if on_gpsimd(n, c, o)]
-                if not mine:
-                    continue
-                tile = sums[n, chunks[0] // 2, o]
-                for c in mine:
-                    cols = slice((c % 2) * CHUNK, (c % 2 + 1) * CHUNK)
-                    gate_cols = slice((c - chunks[0]) * CHUNK, (c - chunks[0] + 1) * CHUNK)
-                    nc.gpsimd.tensor_tensor(tile[:, cols], tile[:, cols], gate[:, gate_cols], MULT)
-                last = mine[-1]
-                if last % 2 == 1 or not on_gpsimd(n, last + 1, o):
-                    nc.sync.dma_start(
-                        outs[o][rows, (last - last % 2) * CHUNK : (last + 1) * CHUNK],
-                        tile[:, 0 : (last % 2 + 1) * CHUNK],
-                    )
-            return gate
+            for k, c in enumerate(chunks):
+                gates[n, c] = gate[:, k * CHUNK : (k + 1) * CHUNK]
 
-        def multiply(u):
+        def store(queue, o, n, first, values):
+            queue.dma_start(outs[o][n * P : (n + 1) * P, first * CHUNK : first * CHUNK + values.shape[1]], values)
+
+        def multiply_sums(u):
             n, chunks = pieces[u]
             for o in range(2):
-                mine = [c for c in chunks if not on_gpsimd(n, c, o)]
-                if not mine:
-                    continue
-                result = sbuf("result%d_%d" % (u, o), [P, len(mine) * CHUNK], F32)
-                for c in mine:
-                    product(n, c, o)
-                    cols = slice((c - mine[0]) * CHUNK, (c - mine[0] + 1) * CHUNK)
-                    gate_cols = slice((c - chunks[0]) * CHUNK, (c - chunks[0] + 1) * CHUNK)
-                    nc.vector.tensor_tensor(result[:, cols], banks[n, c, o][:], gates[u][:, gate_cols], MULT)
-                    if n == ROW_TILES - 1:
-                        nc.scalar.dma_start(outs[o][n * P : (n + 1) * P, c * CHUNK : (c + 1) * CHUNK], result[:, cols])
-                if n < ROW_TILES - 1:
-                    nc.scalar.dma_start(
-                        outs[o][n * P : (n + 1) * P, mine[0] * CHUNK : (mine[-1] + 1) * CHUNK], result[:]
-                    )
-
-        gates = {}
-        for n in range(ROW_TILES):
-            for c in range(CHUNKS):
-                for o in (1, 0):
-                    if on_gpsimd(n, c, o) and (n, c, o) not in banks:
+                for c in chunks:
+                    if not on_gpsimd(n, c, o):
+                        continue
+                    if (n, c, o) not in banks:
                         product(n, c, o)
-            for u in range(len(pieces)):
-                if pieces[u][0] == n:
-                    gates[u] = gather_gate(u)
-                    multiply(u)
+                for c in chunks:
+                    if not on_gpsimd(n, c, o):
+                        continue
+                    tile = sums[n, c // 2, o]
+                    values = tile[:, (c % 2) * CHUNK : (c % 2 + 1) * CHUNK]
+                    nc.gpsimd.tensor_tensor(values, values, gates[n, c], MULT)
+                    if c % 2 == 1:
+                        store(nc.sync, o, n, c - 1, tile[:])
+                    elif u + 2 == len(pieces):
+                        store(nc.sync, o, n, c, values)
+
+        results = {}
+
+        def multiply_bank(n, c, o):
+            key = n, c // 2, o
+            if key not in results:
+                results[key] = sums[key] if key in sums else sbuf("result%d_%d_%d" % key, [P, HALF], F32)
+            values = results[key][:, (c % 2) * CHUNK : (c % 2 + 1) * CHUNK]
+            if (n, c, o) not in banks:
+                product(n, c, o)
+            nc.vector.tensor_tensor(values, banks[n, c, o][:], gates[n, c], MULT)
+            if key[:2] >= (ROW_TILES - 2, 1):
+                store(nc.scalar, o, n, c, values)
+            elif c % 2 == 1:
+                store(nc.scalar, o, n, c - 1, results[key][:])
+
+        for u in range(3):
+            gather_gate(u)
+            multiply_sums(u)
+        for c in (2, 3):
+            multiply_bank(0, c, 0)
+        for u in (3, 4):
+            gather_gate(u)
+        for u in (3, 4):
+            multiply_sums(u)
+        gather_gate(5)
+        multiply_sums(5)
+        for c in (1, 2, 3):
+            multiply_bank(1, c, 0)
+        gather_gate(6)
+        product(2, 2, 1)
+        for c in (0, 1, 2):
+            multiply_bank(2, c, 0)
+        multiply_sums(6)
+        gather_gate(7)
+        multiply_sums(7)
+        multiply_bank(2, 3, 0)
+        multiply_bank(3, 0, 0)
+        gather_gate(8)
+        multiply_sums(8)
+        multiply_bank(3, 1, 0)
+        gather_gate(9)
+        multiply_bank(3, 2, 0)
+        for o in range(2):
+            multiply_bank(3, 3, o)

@@ -22,13 +22,62 @@ K_PASS = K // PASSES
 CHUNK = 512
 CHUNKS = J // CHUNK
 HALF = 2 * CHUNK
-HALVES = J // HALF
 ROW_TILES = N // P
+LAST_ROW_TILE, LAST_CHUNK = ROW_TILES - 1, CHUNKS - 1
+BANKS = 8
 SCALE_ROWS = 96
 REAL_ON_GPSIMD = 3
-QUICK_BANKS = 2
-BANKS = 8
-KIB = 1024
+
+PLACE_KIB = {
+    "word_window0": 0,
+    "scale_window0": 30,
+    "word_window1": 16,
+    "raw_wr0": 32,
+    "raw_wr1": 40,
+    "raw_wi0": 48,
+    "raw_wi1": 56,
+    "gate_window0": 48,
+    "grouped_wi": 64,
+    "scale_window1": 72,
+    "gate_window1": 64,
+    "grouped_neg": 80,
+    "gate_window2": 80,
+    "picked0_2": 116,
+    "gate_window3": 116,
+    "picked0_0": 104,
+    "picked1_0": 104,
+    "picked0_1": 108,
+    "picked1_1": 108,
+    "picked0_3": 32,
+    "grouped_wr0_0": 96,
+    "parted0_2": 96,
+    "picked1_2": 40,
+    "grouped_wr1_0": 100,
+    "grouped_wr1_2": 102,
+    "picked1_3": 102,
+    "gate0": 40,
+    "gate1": 102,
+    "gate2": 16,
+    "gate3": 20,
+    "codes_wr1_0": 132,
+    "gate4": 132,
+    "codes_wr1_1": 136,
+    "gate5": 136,
+    "codes_neg1_0": 140,
+    "gate6": 140,
+    "codes_wr1_2": 144,
+    "gate7": 144,
+    "parted1_0": 114,
+    "gate8": 114,
+    "parted1_1": 112,
+    "gate9": 112,
+    "result0_1_0": 48,
+    "result1_1_0": 52,
+    "result2_0_0": 56,
+    "result2_1_0": 60,
+    "result3_0_0": 64,
+    "result3_1_0": 68,
+}
 
 
 def tile_list_cpxtab_gate_kernel(
@@ -41,58 +90,9 @@ def tile_list_cpxtab_gate_kernel(
         shared = ctx.enter_context(tc.tile_pool(name="shared", bufs=1))
         psum = ctx.enter_context(tc.psum_pool(name="psum", bufs=1))
 
-        place = {
-            "word_window0": 0,
-            "word_window1": 16,
-            "gate2": 16,
-            "gate3": 20,
-            "gate4": 24,
-            "gate5": 28,
-            "scale_window0": 30,
-            "raw_wr0": 32,
-            "picked0_3": 32,
-            "scale_window1": 72,
-            "raw_wr1": 40,
-            "picked1_2": 40,
-            "gate0": 40,
-            "raw_wi0": 48,
-            "raw_wi1": 56,
-            "gate_window0": 48,
-            "result0_1_0": 48,
-            "result1_1_0": 52,
-            "result2_0_0": 56,
-            "result2_1_0": 60,
-            "grouped_wi": 64,
-            "gate_window1": 64,
-            "result3_0_0": 64,
-            "result3_1_0": 68,
-            "grouped_neg": 80,
-            "gate_window2": 80,
-            "grouped_wr0_0": 96,
-            "parted0_2": 96,
-            "grouped_wr1_0": 100,
-            "grouped_wr1_2": 102,
-            "picked1_3": 102,
-            "gate1": 102,
-            "picked0_0": 104,
-            "picked1_0": 104,
-            "picked0_1": 108,
-            "picked1_1": 108,
-            "parted1_1": 112,
-            "gate9": 112,
-            "parted1_0": 114,
-            "gate8": 114,
-            "codes_wr1_0": 132,
-            "gate6": 132,
-            "codes_wr1_2": 136,
-            "gate7": 136,
-            "picked0_2": 116,
-            "gate_window3": 116,
-        }
-
         def sbuf(name, shape, dtype):
-            if name in place:
-                return shared.tile(shape, dtype, name=name, align_bytes=64, offset=place[name] * KIB)
+            if name in PLACE_KIB:
+                return shared.tile(shape, dtype, name=name, align_bytes=64, offset=PLACE_KIB[name] * 1024)
             return held.tile(shape, dtype, name=name, align_bytes=64)
 
         offsets = held.tile([P, J // 16], U16, name="offsets")
@@ -102,8 +102,8 @@ def tile_list_cpxtab_gate_kernel(
             return offsets[:, first // 16 : (first + count) // 16]
 
         scale_window = []
-        for t, scales in enumerate((tab_scales, tab2_scales)):
-            window = sbuf("scale_window%d" % t, [P, (3 - 2 * t) * T // 4], I32)[:, 0 : T // 4]
+        for t, (scales, windows_wide) in enumerate(((tab_scales, 3), (tab2_scales, 1))):
+            window = sbuf("scale_window%d" % t, [P, windows_wide * T // 4], I32)[:, 0 : T // 4]
             nc.sync.dma_start(window[SCALE_ROWS:P, :], scales.bitcast(I32).rearrange("a q t -> q a t"))
             nc.gpsimd.memset(window[0:SCALE_ROWS, :], 0)
             scale_window.append(window)
@@ -131,11 +131,13 @@ def tile_list_cpxtab_gate_kernel(
             return window
 
         def pick_scales(t):
-            picked = sbuf("picked_scales%d" % t, [P, J], U8)
-            nc.vector.tensor_copy(picked[:], scale_window[t][:].bitcast(U8).indirect(offsets[:]))
+            bytes_picked = sbuf("picked_scales%d" % t, [P, J], U8)
+            nc.vector.tensor_copy(bytes_picked[:], scale_window[t][:].bitcast(U8).indirect(offsets[:]))
             for quadrant in (0, 2, 1, 3):
                 row = SCALE_ROWS + 8 * quadrant
-                nc.sync.dma_start(planes[t][32 * quadrant : 32 * quadrant + 4, :], picked[row : row + 8, :].bitcast(I32))
+                nc.sync.dma_start(
+                    planes[t][32 * quadrant : 32 * quadrant + 4, :], bytes_picked[row : row + 8, :].bitcast(I32)
+                )
 
         load_weight("wi", wi, 0)
         load_weight("wi", wi, 1)
@@ -154,27 +156,28 @@ def tile_list_cpxtab_gate_kernel(
             )
 
         def quantise(name, values, parts):
-            width = len(parts) * P
             label = "%s%d_%d" % (name, *parts[0])
-            words = sbuf("codes_" + label, [P, width], U32)
-            scales = sbuf("code_scales_" + label, [P, width], U8)
+            words = sbuf("codes_" + label, [P, len(parts) * P], U32)
+            scales = sbuf("code_scales_" + label, [P, len(parts) * P], U8)
             nc.vector.quantize_mx(out=words[:].bitcast(FP8X4), scales=scales[:], in_=values)
-            for k, (a, n) in enumerate(parts):
-                codes[name, a, n] = words[:, k * P : (k + 1) * P]
-                code_scales[name, a, n] = scales[:, k * P : (k + 1) * P]
+            for place, (a, n) in enumerate(parts):
+                codes[name, a, n] = words[:, place * P : (place + 1) * P]
+                code_scales[name, a, n] = scales[:, place * P : (place + 1) * P]
 
-        grouped_wi = sbuf("grouped_wi", [P, PASSES * 4 * N], BF16)
-        grouped_neg = sbuf("grouped_neg", [P, PASSES * 4 * N], BF16)
+        part_width = 4 * P
+        pass_width = ROW_TILES * part_width
+        every_part = [(a, n) for a in range(PASSES) for n in range(ROW_TILES)]
+        grouped_wi = sbuf("grouped_wi", [P, PASSES * pass_width], BF16)
+        grouped_neg = sbuf("grouped_neg", [P, PASSES * pass_width], BF16)
         for a in range(PASSES):
-            cast(grouped_wi[:, a * 4 * N : (a + 1) * 4 * N], raw["wi", a][:])
+            cast(grouped_wi[:, a * pass_width : (a + 1) * pass_width], raw["wi", a][:])
         nc.scalar.activation(grouped_neg[:], grouped_wi[:], COPY, scale=-1.0)
-        grouped_wr0 = sbuf("grouped_wr0_0", [P, 4 * N], BF16)
+        grouped_wr0 = sbuf("grouped_wr0_0", [P, pass_width], BF16)
         cast(grouped_wr0[:], raw["wr", 0][:])
         grouped_wr1 = {}
         for first in (0, 2):
-            grouped_wr1[first] = sbuf("grouped_wr1_%d" % first, [P, 2 * N], BF16)
+            grouped_wr1[first] = sbuf("grouped_wr1_%d" % first, [P, 2 * part_width], BF16)
             cast(grouped_wr1[first][:], raw["wr", 1][:, :, first * P : (first + 2) * P])
-        every_part = [(a, n) for a in range(PASSES) for n in range(ROW_TILES)]
 
         picked, parted = {}, {}
 
@@ -190,22 +193,25 @@ def tile_list_cpxtab_gate_kernel(
             )
 
         quantise("wi", grouped_wi[:], every_part)
-        for c in range(2):
+        for c in (0, 1):
             gather_words(0, c)
-        for c in range(2):
+        for c in (0, 1):
             part_words(0, c)
-        quantise("neg", grouped_neg[:], every_part)
+        for first, count in ((0, 4), (4, 2), (6, 2)):
+            values = grouped_neg[:, first * part_width : (first + count) * part_width]
+            quantise("neg", values, every_part[first : first + count])
         gather_words(0, 2)
-        for c in range(2):
+        for c in (0, 1):
             gather_words(1, c)
-        for c in range(2):
+        for c in (0, 1):
             part_words(1, c)
         quantise("wr", grouped_wr0[:], every_part[:ROW_TILES])
         gather_words(0, 3)
-        quantise("wr", grouped_wr1[0][:], [(1, 0), (1, 1)])
+        for n in (0, 1):
+            quantise("wr", grouped_wr1[0][:, n * part_width : (n + 1) * part_width], [(1, n)])
         part_words(0, 2)
         for n in (2, 3):
-            quantise("wr", grouped_wr1[2][:, (n - 2) * N : (n - 1) * N], [(1, n)])
+            quantise("wr", grouped_wr1[2][:, (n - 2) * part_width : (n - 1) * part_width], [(1, n)])
         part_words(0, 3)
         for c in (2, 3):
             gather_words(1, c)
@@ -214,24 +220,22 @@ def tile_list_cpxtab_gate_kernel(
         gate_window = [load_gates(n) for n in range(ROW_TILES)]
 
         terms = ((("wr", 0), ("neg", 1)), (("wi", 0), ("wr", 1)))
-        pieces = [(n, (2 * h, 2 * h + 1)) for n in range(ROW_TILES) for h in range(HALVES)]
+
+        pieces = [(n, (first, first + 1)) for n in range(ROW_TILES) for first in (0, 2)]
         pieces[:1] = [(0, (c,)) for c in pieces[0][1]]
-        pieces[-1:] = [(ROW_TILES - 1, (c,)) for c in pieces[-1][1]]
+        pieces[-1:] = [(LAST_ROW_TILE, (c,)) for c in pieces[-1][1]]
 
         def on_gpsimd(n, c, o):
             if o == 1:
-                return (n, c) != (ROW_TILES - 1, CHUNKS - 1)
+                return (n, c) != (LAST_ROW_TILE, LAST_CHUNK)
             return c < 2 and 2 * n + c < REAL_ON_GPSIMD
 
         banks = {}
 
-        def open_bank(n, c, o):
-            number = 2 * n + c if len(banks) < BANKS else len(banks) % BANKS
-            banks[n, c, o] = psum.tile([P, CHUNK], F32, name="acc", tag="bank%d" % number)
-
         def mx_pass(n, c, o, step):
             if step == 0:
-                open_bank(n, c, o)
+                number = 2 * n + c if len(banks) < BANKS else len(banks) % BANKS
+                banks[n, c, o] = psum.tile([P, CHUNK], F32, name="acc", tag="bank%d" % number)
             name, t = terms[o][step // PASSES]
             a = step % PASSES
             first = (J * a + CHUNK * c) // 4
@@ -245,31 +249,33 @@ def tile_list_cpxtab_gate_kernel(
                 stop=(step == 2 * PASSES - 1),
             )
 
+        def in_half(c):
+            return slice((c % 2) * CHUNK, (c % 2 + 1) * CHUNK)
+
         sums = {}
 
         def empty(n, c, o):
             if (n, c // 2, o) not in sums:
                 sums[n, c // 2, o] = sbuf("sums%d_%d_%d" % (n, c // 2, o), [P, HALF], F32)
-            nc.scalar.activation(sums[n, c // 2, o][:, (c % 2) * CHUNK : (c % 2 + 1) * CHUNK], banks[n, c, o][:], COPY)
+            nc.scalar.activation(sums[n, c // 2, o][:, in_half(c)], banks[n, c, o][:], COPY)
 
-        def product(n, c, o):
+        def make_sum(n, c, o):
             for step in range(2 * PASSES):
                 mx_pass(n, c, o, step)
             if on_gpsimd(n, c, o):
                 empty(n, c, o)
 
-        opening = [(n, c) for c in range(2) for n in range(ROW_TILES)]
+        opening = [(n, c) for c in (0, 1) for n in range(ROW_TILES)]
         for n, c in opening:
-            for step in range(PASSES):
+            for step in (0, 1):
                 mx_pass(n, c, 1, step)
         for n, c in opening:
             mx_pass(n, c, 1, 2)
         for n, c in sorted(opening):
             mx_pass(n, c, 1, 3)
             empty(n, c, 1)
-
         for n, c in sorted(opening)[:REAL_ON_GPSIMD]:
-            product(n, c, 0)
+            make_sum(n, c, 0)
 
         gates = {}
 
@@ -277,30 +283,26 @@ def tile_list_cpxtab_gate_kernel(
             n, chunks = pieces[u]
             gate = sbuf("gate%d" % u, [P, len(chunks) * CHUNK], F32)
             nc.vector.tensor_copy(gate[:], gate_window[n][:].indirect(listed(chunks[0] * CHUNK, len(chunks) * CHUNK)))
-            for k, c in enumerate(chunks):
-                gates[n, c] = gate[:, k * CHUNK : (k + 1) * CHUNK]
+            for place, c in enumerate(chunks):
+                gates[n, c] = gate[:, place * CHUNK : (place + 1) * CHUNK]
 
-        def store(queue, o, n, first, values):
-            queue.dma_start(outs[o][n * P : (n + 1) * P, first * CHUNK : first * CHUNK + values.shape[1]], values)
+        def store(queue, o, n, c, values):
+            queue.dma_start(outs[o][n * P : (n + 1) * P, c * CHUNK : c * CHUNK + values.shape[1]], values)
 
         def multiply_sums(u):
             n, chunks = pieces[u]
             for o in range(2):
-                for c in chunks:
-                    if not on_gpsimd(n, c, o):
-                        continue
+                mine = [c for c in chunks if on_gpsimd(n, c, o)]
+                for c in mine:
                     if (n, c, o) not in banks:
-                        product(n, c, o)
-                for c in chunks:
-                    if not on_gpsimd(n, c, o):
-                        continue
+                        make_sum(n, c, o)
+                for c in mine:
                     tile = sums[n, c // 2, o]
-                    values = tile[:, (c % 2) * CHUNK : (c % 2 + 1) * CHUNK]
-                    nc.gpsimd.tensor_tensor(values, values, gates[n, c], MULT)
+                    nc.gpsimd.tensor_tensor(tile[:, in_half(c)], tile[:, in_half(c)], gates[n, c], MULT)
                     if c % 2 == 1:
                         store(nc.sync, o, n, c - 1, tile[:])
-                    elif u + 2 == len(pieces):
-                        store(nc.sync, o, n, c, values)
+                    elif (n, c) == (LAST_ROW_TILE, LAST_CHUNK - 1):
+                        store(nc.sync, o, n, c, tile[:, in_half(c)])
 
         results = {}
 
@@ -308,30 +310,28 @@ def tile_list_cpxtab_gate_kernel(
             key = n, c // 2, o
             if key not in results:
                 results[key] = sums[key] if key in sums else sbuf("result%d_%d_%d" % key, [P, HALF], F32)
-            values = results[key][:, (c % 2) * CHUNK : (c % 2 + 1) * CHUNK]
-            if (n, c, o) not in banks:
-                product(n, c, o)
+            values = results[key][:, in_half(c)]
+            make_sum(n, c, o)
             nc.vector.tensor_tensor(values, banks[n, c, o][:], gates[n, c], MULT)
-            if key[:2] >= (ROW_TILES - 2, 1):
+            if (n, c // 2) >= (LAST_ROW_TILE - 1, 1):
                 store(nc.scalar, o, n, c, values)
             elif c % 2 == 1:
                 store(nc.scalar, o, n, c - 1, results[key][:])
 
-        for u in range(3):
+        for u in range(4):
             gather_gate(u)
             multiply_sums(u)
-        for c in (2, 3):
-            multiply_bank(0, c, 0)
-        for u in (3, 4):
-            gather_gate(u)
-        for u in (3, 4):
-            multiply_sums(u)
+        multiply_bank(0, 2, 0)
+        gather_gate(4)
+        multiply_bank(0, 3, 0)
+        multiply_sums(4)
+        for c in (1, 2):
+            multiply_bank(1, c, 0)
         gather_gate(5)
         multiply_sums(5)
-        for c in (1, 2, 3):
-            multiply_bank(1, c, 0)
+        multiply_bank(1, 3, 0)
         gather_gate(6)
-        product(2, 2, 1)
+        make_sum(2, 2, 1)
         for c in (0, 1, 2):
             multiply_bank(2, c, 0)
         multiply_sums(6)

@@ -26,7 +26,7 @@ ROW_TILES = N // P
 LAST_ROW_TILE, LAST_CHUNK = ROW_TILES - 1, CHUNKS - 1
 BANKS = 8
 SCALE_ROWS = 96
-REAL_ON_GPSIMD = 3
+REAL_ON_GPSIMD = 4
 
 PLACE_KIB = {
     "word_window0": 0,
@@ -40,14 +40,14 @@ PLACE_KIB = {
     "grouped_wi": 64,
     "scale_window1": 72,
     "gate_window1": 64,
-    "grouped_neg": 80,
+    "grouped_neg": 148,
     "gate_window2": 80,
     "picked0_2": 116,
     "gate_window3": 116,
     "picked0_0": 104,
     "picked1_0": 104,
-    "picked0_1": 108,
-    "picked1_1": 108,
+    "picked0_1": 90,
+    "picked1_1": 90,
     "picked0_3": 32,
     "grouped_wr0_0": 96,
     "parted0_2": 96,
@@ -63,8 +63,9 @@ PLACE_KIB = {
     "gate4": 132,
     "codes_wr1_1": 136,
     "gate5": 136,
-    "codes_neg1_0": 140,
-    "gate6": 140,
+    "codes_neg1_0": 44,
+    "gate6": 44,
+    "codes_neg1_2": 42,
     "codes_wr1_2": 144,
     "gate7": 144,
     "parted1_0": 114,
@@ -104,8 +105,10 @@ def tile_list_cpxtab_gate_kernel(
         scale_window = []
         for t, (scales, windows_wide) in enumerate(((tab_scales, 3), (tab2_scales, 1))):
             window = sbuf("scale_window%d" % t, [P, windows_wide * T // 4], I32)[:, 0 : T // 4]
-            nc.sync.dma_start(window[SCALE_ROWS:P, :], scales.bitcast(I32).rearrange("a q t -> q a t"))
-            nc.gpsimd.memset(window[0:SCALE_ROWS, :], 0)
+            first = SCALE_ROWS * (1 - t)
+            nc.sync.dma_start(window[first : first + 32, :], scales.bitcast(I32).rearrange("a q t -> q a t"))
+            for start, stop in (((0, SCALE_ROWS),), ((32, 64), (64, P)))[t]:
+                nc.gpsimd.memset(window[start:stop, :], 0)
             scale_window.append(window)
 
         planes = []
@@ -134,7 +137,7 @@ def tile_list_cpxtab_gate_kernel(
             bytes_picked = sbuf("picked_scales%d" % t, [P, J], U8)
             nc.vector.tensor_copy(bytes_picked[:], scale_window[t][:].bitcast(U8).indirect(offsets[:]))
             for quadrant in (0, 2, 1, 3):
-                row = SCALE_ROWS + 8 * quadrant
+                row = SCALE_ROWS * (1 - t) + 8 * quadrant
                 nc.sync.dma_start(
                     planes[t][32 * quadrant : 32 * quadrant + 4, :], bytes_picked[row : row + 8, :].bitcast(I32)
                 )
@@ -173,7 +176,9 @@ def tile_list_cpxtab_gate_kernel(
             cast(grouped_wi[:, a * pass_width : (a + 1) * pass_width], raw["wi", a][:])
         nc.scalar.activation(grouped_neg[:], grouped_wi[:], COPY, scale=-1.0)
         grouped_wr0 = sbuf("grouped_wr0_0", [P, pass_width], BF16)
-        cast(grouped_wr0[:], raw["wr", 0][:])
+        for first in (0, 2):
+            target = grouped_wr0[:, first * part_width : (first + 2) * part_width]
+            cast(target, raw["wr", 0][:, :, first * P : (first + 2) * P])
         grouped_wr1 = {}
         for first in (0, 2):
             grouped_wr1[first] = sbuf("grouped_wr1_%d" % first, [P, 2 * part_width], BF16)
@@ -197,22 +202,24 @@ def tile_list_cpxtab_gate_kernel(
             gather_words(0, c)
         for c in (0, 1):
             part_words(0, c)
-        for first, count in ((0, 4), (4, 2), (6, 2)):
-            values = grouped_neg[:, first * part_width : (first + count) * part_width]
-            quantise("neg", values, every_part[first : first + count])
+        quantise("neg", grouped_neg[:, :pass_width], every_part[:ROW_TILES])
         gather_words(0, 2)
         for c in (0, 1):
             gather_words(1, c)
         for c in (0, 1):
             part_words(1, c)
-        quantise("wr", grouped_wr0[:], every_part[:ROW_TILES])
+        quantise("wr", grouped_wr0[:, : 2 * part_width], every_part[:2])
         gather_words(0, 3)
+        quantise("wr", grouped_wr0[:, 2 * part_width :], every_part[2:ROW_TILES])
         for n in (0, 1):
             quantise("wr", grouped_wr1[0][:, n * part_width : (n + 1) * part_width], [(1, n)])
         part_words(0, 2)
         for n in (2, 3):
             quantise("wr", grouped_wr1[2][:, (n - 2) * part_width : (n - 1) * part_width], [(1, n)])
         part_words(0, 3)
+        for first in (4, 6):
+            values = grouped_neg[:, first * part_width : (first + 2) * part_width]
+            quantise("neg", values, every_part[first : first + 2])
         for c in (2, 3):
             gather_words(1, c)
         for c in (2, 3):
@@ -283,6 +290,7 @@ def tile_list_cpxtab_gate_kernel(
             n, chunks = pieces[u]
             gate = sbuf("gate%d" % u, [P, len(chunks) * CHUNK], F32)
             nc.vector.tensor_copy(gate[:], gate_window[n][:].indirect(listed(chunks[0] * CHUNK, len(chunks) * CHUNK)))
+            gates[n, chunks] = gate[:]
             for place, c in enumerate(chunks):
                 gates[n, c] = gate[:, place * CHUNK : (place + 1) * CHUNK]
 
@@ -296,13 +304,18 @@ def tile_list_cpxtab_gate_kernel(
                 for c in mine:
                     if (n, c, o) not in banks:
                         make_sum(n, c, o)
+                if len(mine) == 2 and n in (1, 2) and (n, o) != (1, 1):
+                    tile = sums[n, mine[0] // 2, o]
+                    nc.gpsimd.tensor_tensor(tile[:], tile[:], gates[n, chunks], MULT)
+                    store(nc.sync, o, n, mine[0], tile[:])
+                    continue
                 for c in mine:
                     tile = sums[n, c // 2, o]
                     nc.gpsimd.tensor_tensor(tile[:, in_half(c)], tile[:, in_half(c)], gates[n, c], MULT)
-                    if c % 2 == 1:
-                        store(nc.sync, o, n, c - 1, tile[:])
-                    elif (n, c) == (LAST_ROW_TILE, LAST_CHUNK - 1):
+                    if n == LAST_ROW_TILE:
                         store(nc.sync, o, n, c, tile[:, in_half(c)])
+                    elif c % 2 == 1:
+                        store(nc.sync, o, n, c - 1, tile[:])
 
         results = {}
 
@@ -325,8 +338,7 @@ def tile_list_cpxtab_gate_kernel(
         gather_gate(4)
         multiply_bank(0, 3, 0)
         multiply_sums(4)
-        for c in (1, 2):
-            multiply_bank(1, c, 0)
+        multiply_bank(1, 2, 0)
         gather_gate(5)
         multiply_sums(5)
         multiply_bank(1, 3, 0)

@@ -20,64 +20,43 @@ P = 128
 PASSES = 2
 K_PASS = K // PASSES
 CHUNK = 512
-CHUNKS = J // CHUNK
 HALF = 2 * CHUNK
 ROW_TILES = N // P
-LAST_ROW_TILE, LAST_CHUNK = ROW_TILES - 1, CHUNKS - 1
 BANKS = 8
+PART = 4 * P
 SCALE_ROWS = 96
-REAL_ON_GPSIMD = 4
 
 PLACE_KIB = {
-    "word_window0": 0,
-    "scale_window0": 30,
-    "word_window1": 16,
-    "raw_wr0": 32,
-    "raw_wr1": 40,
-    "raw_wi0": 48,
-    "raw_wi1": 56,
-    "gate_window0": 48,
+    "scale_window1": 6,
+    "scale_window0": 10,
+    "raw_wr1": 0,
+    "word_window1": 8,
+    "gate_window3": 8,
+    "picked1_3": 0,
+    "parted1_2": 2,
+    "raw_wi0": 24,
+    "raw_wi1": 32,
+    "gate_window0": 24,
+    "word_window0": 40,
+    "gate_window1": 40,
+    "raw_wr0": 56,
     "grouped_wi": 64,
-    "scale_window1": 72,
-    "gate_window1": 64,
-    "grouped_neg": 148,
-    "gate_window2": 80,
-    "picked0_2": 116,
-    "gate_window3": 116,
-    "picked0_0": 104,
-    "picked1_0": 104,
-    "picked0_1": 90,
-    "picked1_1": 90,
-    "picked0_3": 32,
-    "grouped_wr0_0": 96,
-    "parted0_2": 96,
-    "picked1_2": 40,
-    "grouped_wr1_0": 100,
-    "grouped_wr1_2": 102,
-    "picked1_3": 102,
-    "gate0": 40,
-    "gate1": 102,
-    "gate2": 16,
-    "gate3": 20,
-    "codes_wr1_0": 132,
-    "gate4": 132,
-    "codes_wr1_1": 136,
-    "gate5": 136,
-    "codes_neg1_0": 44,
-    "gate6": 44,
-    "codes_neg1_2": 42,
-    "codes_wr1_2": 144,
-    "gate7": 144,
-    "parted1_0": 114,
-    "gate8": 114,
-    "parted1_1": 112,
-    "gate9": 112,
-    "result0_1_0": 48,
-    "result1_1_0": 52,
-    "result2_0_0": 56,
-    "result2_1_0": 60,
-    "result3_0_0": 64,
-    "result3_1_0": 68,
+    "gate_window2": 56,
+    "picked1_0": 72,
+    "codes_neg0": 72,
+    "gate2_2": 72,
+    "picked1_1": 76,
+    "codes_neg2": 76,
+    "grouped_wr1_0": 78,
+    "picked1_2": 78,
+    "codes_wr1_0": 80,
+    "gate2_0": 80,
+    "codes_wr1_1": 84,
+    "gate3_0": 84,
+    "codes_wr1_2": 88,
+    "gate3_2": 88,
+    "parted1_1": 90,
+    "gate3_3": 90,
 }
 
 
@@ -103,24 +82,14 @@ def tile_list_cpxtab_gate_kernel(
             return offsets[:, first // 16 : (first + count) // 16]
 
         scale_window = []
-        for t, (scales, windows_wide) in enumerate(((tab_scales, 3), (tab2_scales, 1))):
-            window = sbuf("scale_window%d" % t, [P, windows_wide * T // 4], I32)[:, 0 : T // 4]
-            first = SCALE_ROWS * (1 - t)
-            nc.sync.dma_start(window[first : first + 32, :], scales.bitcast(I32).rearrange("a q t -> q a t"))
-            for start, stop in (((0, SCALE_ROWS),), ((32, 64), (64, P)))[t]:
-                nc.gpsimd.memset(window[start:stop, :], 0)
+        for t, scales in enumerate((tab_scales, tab2_scales)):
+            window = sbuf("scale_window%d" % t, [P, T // 4], I32)
+            nc.sync.dma_start(window[SCALE_ROWS:P, :], scales.bitcast(I32).rearrange("a q t -> (a q) t"))
+            nc.gpsimd.memset(window[0:SCALE_ROWS, :], 0)
             scale_window.append(window)
 
-        planes = []
-        for t in range(2):
-            plane = sbuf("planes%d" % t, [P, PASSES * J // 4], I32)
-            nc.gpsimd.memset(plane[:], 0)
-            planes.append(plane)
-
-        def load_words(t, words):
-            window = sbuf("word_window%d" % t, [P, T], I32)
-            nc.sync.dma_start(window[:], words[0].rearrange("p t b -> p (t b)").bitcast(I32))
-            return window
+        planes = sbuf("planes", [P, PASSES * 2 * J // 4], I32)
+        nc.gpsimd.memset(planes[:], 0)
 
         raw = {}
 
@@ -128,28 +97,30 @@ def tile_list_cpxtab_gate_kernel(
             raw[name, a] = sbuf("raw_%s%d" % (name, a), [P, 4, N], F32)
             nc.sync.dma_start(raw[name, a][:], w[K_PASS * a : K_PASS * (a + 1), :].rearrange("(p i) n -> p i n", i=4))
 
-        def load_gates(n):
-            window = sbuf("gate_window%d" % n, [P, T], F32)
-            nc.sync.dma_start(window[:], gT[n * P : (n + 1) * P, :])
+        def load_words(t, words):
+            window = sbuf("word_window%d" % t, [P, T], I32)
+            nc.sync.dma_start(window[:], words[0].rearrange("p t b -> p (t b)").bitcast(I32))
             return window
-
-        def pick_scales(t):
-            bytes_picked = sbuf("picked_scales%d" % t, [P, J], U8)
-            nc.vector.tensor_copy(bytes_picked[:], scale_window[t][:].bitcast(U8).indirect(offsets[:]))
-            for quadrant in (0, 2, 1, 3):
-                row = SCALE_ROWS * (1 - t) + 8 * quadrant
-                nc.sync.dma_start(
-                    planes[t][32 * quadrant : 32 * quadrant + 4, :], bytes_picked[row : row + 8, :].bitcast(I32)
-                )
 
         load_weight("wi", wi, 0)
         load_weight("wi", wi, 1)
         word_window = [load_words(0, tab_words)]
-        pick_scales(0)
-        word_window.append(load_words(1, tab2_words))
         load_weight("wr", wr, 0)
+
+        picked_scales = sbuf("picked_scales", [P, 2 * J], U8)
+        for t in range(2):
+            nc.vector.tensor_copy(
+                picked_scales[:, t * J : (t + 1) * J], scale_window[t][:].bitcast(U8).indirect(offsets[:])
+            )
+        for a in range(PASSES):
+            for r in range(4):
+                row = SCALE_ROWS + 16 * a
+                nc.sync.dma_start(
+                    planes[r:P:32, a * 2 * J // 4 : (a + 1) * 2 * J // 4],
+                    picked_scales[row + r : row + 16 : 4, :].bitcast(I32),
+                )
+        word_window.append(load_words(1, tab2_words))
         load_weight("wr", wr, 1)
-        pick_scales(1)
 
         codes, code_scales = {}, {}
 
@@ -158,8 +129,7 @@ def tile_list_cpxtab_gate_kernel(
                 target.rearrange("p (c m i) -> p c i m", m=4, i=4), source.rearrange("p i (c m) -> p c i m", m=4), COPY
             )
 
-        def quantise(name, values, parts):
-            label = "%s%d_%d" % (name, *parts[0])
+        def quantise(label, name, values, parts):
             words = sbuf("codes_" + label, [P, len(parts) * P], U32)
             scales = sbuf("code_scales_" + label, [P, len(parts) * P], U8)
             nc.vector.quantize_mx(out=words[:].bitcast(FP8X4), scales=scales[:], in_=values)
@@ -167,76 +137,74 @@ def tile_list_cpxtab_gate_kernel(
                 codes[name, a, n] = words[:, place * P : (place + 1) * P]
                 code_scales[name, a, n] = scales[:, place * P : (place + 1) * P]
 
-        part_width = 4 * P
-        pass_width = ROW_TILES * part_width
-        every_part = [(a, n) for a in range(PASSES) for n in range(ROW_TILES)]
+        pass_width = ROW_TILES * PART
         grouped_wi = sbuf("grouped_wi", [P, PASSES * pass_width], BF16)
-        grouped_neg = sbuf("grouped_neg", [P, PASSES * pass_width], BF16)
         for a in range(PASSES):
             cast(grouped_wi[:, a * pass_width : (a + 1) * pass_width], raw["wi", a][:])
-        nc.scalar.activation(grouped_neg[:], grouped_wi[:], COPY, scale=-1.0)
-        grouped_wr0 = sbuf("grouped_wr0_0", [P, pass_width], BF16)
-        for first in (0, 2):
-            target = grouped_wr0[:, first * part_width : (first + 2) * part_width]
-            cast(target, raw["wr", 0][:, :, first * P : (first + 2) * P])
+        grouped_neg = sbuf("grouped_neg", [P, PASSES * pass_width], BF16)
+        nc.scalar.activation(
+            grouped_neg[:].rearrange("p (h a x) -> p h a x", h=2, a=PASSES),
+            grouped_wi[:].rearrange("p (a h x) -> p h a x", h=2, a=PASSES),
+            COPY,
+            scale=-1.0,
+        )
+        grouped_wr0 = sbuf("grouped_wr0", [P, pass_width], BF16)
+        cast(grouped_wr0[:], raw["wr", 0][:])
         grouped_wr1 = {}
-        for first in (0, 2):
-            grouped_wr1[first] = sbuf("grouped_wr1_%d" % first, [P, 2 * part_width], BF16)
-            cast(grouped_wr1[first][:], raw["wr", 1][:, :, first * P : (first + 2) * P])
+        for first, count in ((0, 1), (1, 1), (2, 2)):
+            tile = sbuf("grouped_wr1_%d" % first, [P, count * PART], BF16)
+            cast(tile[:], raw["wr", 1][:, :, first * P : (first + count) * P])
+            for place in range(count):
+                grouped_wr1[first + place] = tile[:, place * PART : (place + 1) * PART]
 
         picked, parted = {}, {}
 
-        def gather_words(t, c):
-            picked[t, c] = sbuf("picked%d_%d" % (t, c), [P, CHUNK], U32)
-            nc.vector.tensor_copy(picked[t, c][:], word_window[t][:].bitcast(U32).indirect(listed(c * CHUNK, CHUNK)))
-
-        def part_words(t, c):
-            parted[t, c] = sbuf("parted%d_%d" % (t, c), [P, PASSES, CHUNK], U16)
+        def gather_words(t, c, chunks=1):
+            picked[t, c] = sbuf("picked%d_%d" % (t, c), [P, chunks * CHUNK], U32)
             nc.vector.tensor_copy(
-                parted[t, c][:].rearrange("p d (h j) -> p h d j", h=2),
-                picked[t, c][:].bitcast(U16).rearrange("p (h j d) -> p h d j", h=2, d=2),
+                picked[t, c][:], word_window[t][:].bitcast(U32).indirect(listed(c * CHUNK, chunks * CHUNK))
             )
 
-        quantise("wi", grouped_wi[:], every_part)
-        for c in (0, 1):
-            gather_words(0, c)
-        for c in (0, 1):
-            part_words(0, c)
-        quantise("neg", grouped_neg[:, :pass_width], every_part[:ROW_TILES])
-        gather_words(0, 2)
+        def part_words(t, c, chunks=1):
+            tile = sbuf("parted%d_%d" % (t, c), [P, PASSES, chunks * CHUNK], U16)
+            nc.vector.tensor_copy(
+                tile[:].rearrange("p d (h j) -> p h d j", h=2),
+                picked[t, c][:].bitcast(U16).rearrange("p (h j d) -> p h d j", h=2, d=2),
+            )
+            for place in range(chunks):
+                for a in range(PASSES):
+                    parted[t, c + place, a] = tile[:, a, place * CHUNK : (place + 1) * CHUNK]
+
+        quantise("wi", "wi", grouped_wi[:], [(a, n) for a in range(PASSES) for n in range(ROW_TILES)])
+        gather_words(0, 0)
+        gather_words(0, 1)
+        part_words(0, 0)
+        gather_words(0, 2, 2)
+        part_words(0, 1)
+        part_words(0, 2, 2)
+        quantise("wr0", "wr", grouped_wr0[:], [(0, n) for n in range(ROW_TILES)])
         for c in (0, 1):
             gather_words(1, c)
         for c in (0, 1):
             part_words(1, c)
-        quantise("wr", grouped_wr0[:, : 2 * part_width], every_part[:2])
-        gather_words(0, 3)
-        quantise("wr", grouped_wr0[:, 2 * part_width :], every_part[2:ROW_TILES])
+        for first in (0, 2):
+            values = grouped_neg[:, first * PASSES * PART : (first + 2) * PASSES * PART]
+            quantise("neg%d" % first, "neg", values, [(a, n) for a in range(PASSES) for n in (first, first + 1)])
         for n in (0, 1):
-            quantise("wr", grouped_wr1[0][:, n * part_width : (n + 1) * part_width], [(1, n)])
-        part_words(0, 2)
+            quantise("wr1_%d" % n, "wr", grouped_wr1[n], [(1, n)])
+        gather_words(1, 2)
         for n in (2, 3):
-            quantise("wr", grouped_wr1[2][:, (n - 2) * part_width : (n - 1) * part_width], [(1, n)])
-        part_words(0, 3)
-        for first in (4, 6):
-            values = grouped_neg[:, first * part_width : (first + 2) * part_width]
-            quantise("neg", values, every_part[first : first + 2])
-        for c in (2, 3):
-            gather_words(1, c)
+            quantise("wr1_%d" % n, "wr", grouped_wr1[n], [(1, n)])
+        gather_words(1, 3)
         for c in (2, 3):
             part_words(1, c)
-        gate_window = [load_gates(n) for n in range(ROW_TILES)]
+
+        gate_window = []
+        for n in range(ROW_TILES):
+            gate_window.append(sbuf("gate_window%d" % n, [P, T], F32))
+            nc.sync.dma_start(gate_window[n][:], gT[n * P : (n + 1) * P, :])
 
         terms = ((("wr", 0), ("neg", 1)), (("wi", 0), ("wr", 1)))
-
-        pieces = [(n, (first, first + 1)) for n in range(ROW_TILES) for first in (0, 2)]
-        pieces[:1] = [(0, (c,)) for c in pieces[0][1]]
-        pieces[-1:] = [(LAST_ROW_TILE, (c,)) for c in pieces[-1][1]]
-
-        def on_gpsimd(n, c, o):
-            if o == 1:
-                return (n, c) != (LAST_ROW_TILE, LAST_CHUNK)
-            return c < 2 and 2 * n + c < REAL_ON_GPSIMD
-
         banks = {}
 
         def mx_pass(n, c, o, step):
@@ -245,32 +213,51 @@ def tile_list_cpxtab_gate_kernel(
                 banks[n, c, o] = psum.tile([P, CHUNK], F32, name="acc", tag="bank%d" % number)
             name, t = terms[o][step // PASSES]
             a = step % PASSES
-            first = (J * a + CHUNK * c) // 4
+            first = (J * (2 * a + t) + CHUNK * c) // 4
             nc.tensor.matmul_mx(
                 out=banks[n, c, o][:],
                 lhsT=codes[name, a, n].bitcast(FP8X4),
                 lhsT_scale=code_scales[name, a, n],
-                rhs=parted[t, c][:, a, :].bitcast(FP4X4),
-                rhs_scale=planes[t][:, first : first + CHUNK // 4].bitcast(U8),
+                rhs=parted[t, c, a].bitcast(FP4X4),
+                rhs_scale=planes[:, first : first + CHUNK // 4].bitcast(U8),
                 start=(step == 0),
                 stop=(step == 2 * PASSES - 1),
             )
 
-        def in_half(c):
-            return slice((c % 2) * CHUNK, (c % 2 + 1) * CHUNK)
+        results = {(n, o): sbuf("result%d_%d" % (n, o), [P, J], F32) for n in range(ROW_TILES) for o in range(2)}
 
-        sums = {}
+        def columns(c, chunks=1):
+            return slice(c * CHUNK, (c + chunks) * CHUNK)
 
         def empty(n, c, o):
-            if (n, c // 2, o) not in sums:
-                sums[n, c // 2, o] = sbuf("sums%d_%d_%d" % (n, c // 2, o), [P, HALF], F32)
-            nc.scalar.activation(sums[n, c // 2, o][:, in_half(c)], banks[n, c, o][:], COPY)
+            nc.scalar.activation(results[n, o][:, columns(c)], banks[n, c, o][:], COPY)
 
         def make_sum(n, c, o):
             for step in range(2 * PASSES):
                 mx_pass(n, c, o, step)
-            if on_gpsimd(n, c, o):
-                empty(n, c, o)
+
+        def sum_for_gpsimd(n, c, o):
+            make_sum(n, c, o)
+            empty(n, c, o)
+
+        gates = {}
+
+        def gather_gate(n, c, chunks=1):
+            gate = sbuf("gate%d_%d" % (n, c), [P, chunks * CHUNK], F32)
+            nc.vector.tensor_copy(gate[:], gate_window[n][:].indirect(listed(c * CHUNK, chunks * CHUNK)))
+            gates[n, c, chunks] = gate[:]
+            for place in range(chunks):
+                gates[n, c + place, 1] = gate[:, columns(place)]
+
+        def on_gpsimd(n, c, o, chunks=1):
+            values = results[n, o][:, columns(c, chunks)]
+            nc.gpsimd.tensor_tensor(values, values, gates[n, c, chunks], MULT)
+
+        def on_vector(n, c, o):
+            nc.vector.tensor_tensor(results[n, o][:, columns(c)], banks[n, c, o][:], gates[n, c, 1], MULT)
+
+        def store(n, c, o, chunks):
+            nc.sync.dma_start(outs[o][n * P : (n + 1) * P, columns(c, chunks)], results[n, o][:, columns(c, chunks)])
 
         opening = [(n, c) for c in (0, 1) for n in range(ROW_TILES)]
         for n, c in opening:
@@ -281,80 +268,67 @@ def tile_list_cpxtab_gate_kernel(
         for n, c in sorted(opening):
             mx_pass(n, c, 1, 3)
             empty(n, c, 1)
-        for n, c in sorted(opening)[:REAL_ON_GPSIMD]:
-            make_sum(n, c, 0)
 
-        gates = {}
-
-        def gather_gate(u):
-            n, chunks = pieces[u]
-            gate = sbuf("gate%d" % u, [P, len(chunks) * CHUNK], F32)
-            nc.vector.tensor_copy(gate[:], gate_window[n][:].indirect(listed(chunks[0] * CHUNK, len(chunks) * CHUNK)))
-            gates[n, chunks] = gate[:]
-            for place, c in enumerate(chunks):
-                gates[n, c] = gate[:, place * CHUNK : (place + 1) * CHUNK]
-
-        def store(queue, o, n, c, values):
-            queue.dma_start(outs[o][n * P : (n + 1) * P, c * CHUNK : c * CHUNK + values.shape[1]], values)
-
-        def multiply_sums(u):
-            n, chunks = pieces[u]
-            for o in range(2):
-                mine = [c for c in chunks if on_gpsimd(n, c, o)]
-                for c in mine:
-                    if (n, c, o) not in banks:
-                        make_sum(n, c, o)
-                if len(mine) == 2 and n in (1, 2) and (n, o) != (1, 1):
-                    tile = sums[n, mine[0] // 2, o]
-                    nc.gpsimd.tensor_tensor(tile[:], tile[:], gates[n, chunks], MULT)
-                    store(nc.sync, o, n, mine[0], tile[:])
-                    continue
-                for c in mine:
-                    tile = sums[n, c // 2, o]
-                    nc.gpsimd.tensor_tensor(tile[:, in_half(c)], tile[:, in_half(c)], gates[n, c], MULT)
-                    if n == LAST_ROW_TILE:
-                        store(nc.sync, o, n, c, tile[:, in_half(c)])
-                    elif c % 2 == 1:
-                        store(nc.sync, o, n, c - 1, tile[:])
-
-        results = {}
-
-        def multiply_bank(n, c, o):
-            key = n, c // 2, o
-            if key not in results:
-                results[key] = sums[key] if key in sums else sbuf("result%d_%d_%d" % key, [P, HALF], F32)
-            values = results[key][:, in_half(c)]
+        def sum_for_vector(n, c, o):
             make_sum(n, c, o)
-            nc.vector.tensor_tensor(values, banks[n, c, o][:], gates[n, c], MULT)
-            if (n, c // 2) >= (LAST_ROW_TILE - 1, 1):
-                store(nc.scalar, o, n, c, values)
-            elif c % 2 == 1:
-                store(nc.scalar, o, n, c - 1, results[key][:])
+            on_vector(n, c, o)
 
-        for u in range(4):
-            gather_gate(u)
-            multiply_sums(u)
-        multiply_bank(0, 2, 0)
-        gather_gate(4)
-        multiply_bank(0, 3, 0)
-        multiply_sums(4)
-        multiply_bank(1, 2, 0)
-        gather_gate(5)
-        multiply_sums(5)
-        multiply_bank(1, 3, 0)
-        gather_gate(6)
-        make_sum(2, 2, 1)
-        for c in (0, 1, 2):
-            multiply_bank(2, c, 0)
-        multiply_sums(6)
-        gather_gate(7)
-        multiply_sums(7)
-        multiply_bank(2, 3, 0)
-        multiply_bank(3, 0, 0)
-        gather_gate(8)
-        multiply_sums(8)
-        multiply_bank(3, 1, 0)
-        gather_gate(9)
-        multiply_bank(3, 2, 0)
-        for o in range(2):
-            multiply_bank(3, 3, o)
+        gather_gate(0, 0)
+        gather_gate(0, 1)
+        gather_gate(0, 2, 2)
+        gather_gate(1, 0, 2)
+        gather_gate(1, 2, 2)
+        for c in (0, 1):
+            sum_for_gpsimd(0, c, 0)
+        for o in (1, 0):
+            for c in (0, 1):
+                on_gpsimd(0, c, o)
+        for o in (1, 0):
+            for c in (2, 3):
+                sum_for_gpsimd(0, c, o)
+        on_gpsimd(0, 2, 1, 2)
+        store(0, 0, 1, 4)
+        on_gpsimd(1, 0, 1, 2)
+        for c in (0, 1):
+            sum_for_vector(1, c, 0)
+        for o in (0, 1):
+            store(1, 0, o, 2)
+        gather_gate(2, 0, 2)
+        on_gpsimd(0, 2, 0, 2)
+        store(0, 0, 0, 4)
+        for c in (2, 3):
+            sum_for_gpsimd(1, c, 1)
+        on_gpsimd(1, 2, 1, 2)
+        store(1, 2, 1, 2)
+        sum_for_vector(1, 2, 0)
+        gather_gate(3, 0, 2)
+        sum_for_vector(1, 3, 0)
+        store(1, 2, 0, 2)
+        gather_gate(2, 2, 2)
+        on_gpsimd(2, 0, 1, 2)
+        store(2, 0, 1, 2)
+        for c in (0, 1):
+            sum_for_vector(2, c, 0)
+        store(2, 0, 0, 2)
+        on_gpsimd(3, 0, 1, 2)
+        store(3, 0, 1, 2)
+        for c in (2, 3):
+            sum_for_gpsimd(2, c, 1)
+        on_gpsimd(2, 2, 1, 2)
+        sum_for_vector(2, 2, 0)
+        gather_gate(3, 2)
+        sum_for_vector(2, 3, 0)
+        store(2, 2, 0, 2)
+        for c in (0, 1):
+            sum_for_vector(3, c, 0)
+        store(3, 0, 0, 2)
+        store(2, 2, 1, 2)
+        gather_gate(3, 3)
+        sum_for_gpsimd(3, 2, 1)
+        on_gpsimd(3, 2, 1)
+        for c in (2, 3):
+            sum_for_vector(3, c, 0)
+            store(3, c, 0, 1)
+        sum_for_vector(3, 3, 1)
+        for c in (2, 3):
+            store(3, c, 1, 1)

@@ -26,37 +26,36 @@ BANKS = 8
 PART = 4 * P
 SCALE_ROWS = 96
 
+LATER_BANKS = (0, 1, 4, 5, 6, 7) + (2, 3, 4, 5, 0, 1) + (6, 7, 2, 3, 4, 5) + (6, 7, 0, 1, 2, 3)
+
 PLACE_KIB = {
-    "scale_window1": 6,
-    "scale_window0": 10,
-    "raw_wr1": 0,
-    "word_window1": 8,
-    "gate_window3": 8,
-    "picked1_3": 0,
-    "parted1_2": 2,
-    "raw_wi0": 24,
-    "raw_wi1": 32,
-    "gate_window0": 24,
-    "word_window0": 40,
-    "gate_window1": 40,
-    "raw_wr0": 56,
-    "grouped_wi": 64,
-    "gate_window2": 56,
-    "picked1_0": 72,
-    "codes_neg0": 72,
-    "gate2_2": 72,
-    "picked1_1": 76,
-    "codes_neg2": 76,
-    "grouped_wr1_0": 78,
-    "picked1_2": 78,
-    "codes_wr1_0": 80,
-    "gate2_0": 80,
-    "codes_wr1_1": 84,
-    "gate3_0": 84,
-    "codes_wr1_2": 88,
+    "scale_window0": 14,
+    "word_window1": 0,
+    "gate_window3": 0,
+    "raw_wr0": 16,
+    "codes_neg0": 16,
+    "codes_neg2": 20,
+    "parted0_2": 22,
+    "scale_window1": 30,
+    "raw_wr1": 26,
+    "picked1_2": 26,
+    "picked1_3": 28,
+    "raw_wi0": 40,
+    "raw_wi1": 48,
+    "gate_window0": 36,
+    "planes1": 52,
+    "gate2_0": 36,
+    "gate2_2": 40,
+    "codes_wr1_2": 92,
+    "gate3_0": 92,
+    "parted0_1": 88,
     "gate3_2": 88,
     "parted1_1": 90,
     "gate3_3": 90,
+    "word_window0": 56,
+    "gate_window1": 56,
+    "grouped_wi": 72,
+    "gate_window2": 72,
 }
 
 
@@ -84,12 +83,17 @@ def tile_list_cpxtab_gate_kernel(
         scale_window = []
         for t, scales in enumerate((tab_scales, tab2_scales)):
             window = sbuf("scale_window%d" % t, [P, T // 4], I32)
-            nc.sync.dma_start(window[SCALE_ROWS:P, :], scales.bitcast(I32).rearrange("a q t -> (a q) t"))
+            nc.sync.dma_start(window[SCALE_ROWS:P, :], scales.bitcast(I32).rearrange("a q t -> q a t"))
             nc.gpsimd.memset(window[0:SCALE_ROWS, :], 0)
             scale_window.append(window)
 
-        planes = sbuf("planes", [P, PASSES * 2 * J // 4], I32)
-        nc.gpsimd.memset(planes[:], 0)
+        planes = {}
+
+        def clear_planes(h):
+            planes[h] = sbuf("planes%d" % h, [P, PASSES * 2 * HALF // 4], I32)
+            nc.gpsimd.memset(planes[h][:], 0)
+
+        clear_planes(0)
 
         raw = {}
 
@@ -105,21 +109,26 @@ def tile_list_cpxtab_gate_kernel(
         load_weight("wi", wi, 0)
         load_weight("wi", wi, 1)
         word_window = [load_words(0, tab_words)]
-        load_weight("wr", wr, 0)
 
-        picked_scales = sbuf("picked_scales", [P, 2 * J], U8)
-        for t in range(2):
-            nc.vector.tensor_copy(
-                picked_scales[:, t * J : (t + 1) * J], scale_window[t][:].bitcast(U8).indirect(offsets[:])
-            )
-        for a in range(PASSES):
-            for r in range(4):
-                row = SCALE_ROWS + 16 * a
-                nc.sync.dma_start(
-                    planes[r:P:32, a * 2 * J // 4 : (a + 1) * 2 * J // 4],
-                    picked_scales[row + r : row + 16 : 4, :].bitcast(I32),
+        picked_scales = {}
+        for h in range(2):
+            picked_scales[h] = sbuf("picked_scales%d" % h, [P, 2 * HALF], U8)
+            for t in range(2):
+                nc.vector.tensor_copy(
+                    picked_scales[h][:, t * HALF : (t + 1) * HALF],
+                    scale_window[t][:].bitcast(U8).indirect(listed(h * HALF, HALF)),
                 )
+
+        def move_scales(h):
+            for quadrant in (0, 2, 1, 3):
+                row = SCALE_ROWS + 8 * quadrant
+                nc.sync.dma_start(
+                    planes[h][32 * quadrant : 32 * quadrant + 4, :], picked_scales[h][row : row + 8, :].bitcast(I32)
+                )
+
+        move_scales(0)
         word_window.append(load_words(1, tab2_words))
+        load_weight("wr", wr, 0)
         load_weight("wr", wr, 1)
 
         codes, code_scales = {}, {}
@@ -149,7 +158,8 @@ def tile_list_cpxtab_gate_kernel(
             scale=-1.0,
         )
         grouped_wr0 = sbuf("grouped_wr0", [P, pass_width], BF16)
-        cast(grouped_wr0[:], raw["wr", 0][:])
+        for first in (0, 2):
+            cast(grouped_wr0[:, first * PART : (first + 2) * PART], raw["wr", 0][:, :, first * P : (first + 2) * P])
         grouped_wr1 = {}
         for first, count in ((0, 1), (1, 1), (2, 2)):
             tile = sbuf("grouped_wr1_%d" % first, [P, count * PART], BF16)
@@ -181,21 +191,23 @@ def tile_list_cpxtab_gate_kernel(
         part_words(0, 0)
         gather_words(0, 2, 2)
         part_words(0, 1)
-        part_words(0, 2, 2)
-        quantise("wr0", "wr", grouped_wr0[:], [(0, n) for n in range(ROW_TILES)])
         for c in (0, 1):
             gather_words(1, c)
         for c in (0, 1):
             part_words(1, c)
         for first in (0, 2):
+            values = grouped_wr0[:, first * PART : (first + 2) * PART]
+            quantise("wr0_%d" % first, "wr", values, [(0, first), (0, first + 1)])
+        for first in (0, 2):
             values = grouped_neg[:, first * PASSES * PART : (first + 2) * PASSES * PART]
             quantise("neg%d" % first, "neg", values, [(a, n) for a in range(PASSES) for n in (first, first + 1)])
         for n in (0, 1):
             quantise("wr1_%d" % n, "wr", grouped_wr1[n], [(1, n)])
-        gather_words(1, 2)
+        part_words(0, 2, 2)
         for n in (2, 3):
             quantise("wr1_%d" % n, "wr", grouped_wr1[n], [(1, n)])
-        gather_words(1, 3)
+        for c in (2, 3):
+            gather_words(1, c)
         for c in (2, 3):
             part_words(1, c)
 
@@ -203,23 +215,26 @@ def tile_list_cpxtab_gate_kernel(
         for n in range(ROW_TILES):
             gate_window.append(sbuf("gate_window%d" % n, [P, T], F32))
             nc.sync.dma_start(gate_window[n][:], gT[n * P : (n + 1) * P, :])
+            if n == 0:
+                clear_planes(1)
+                move_scales(1)
 
         terms = ((("wr", 0), ("neg", 1)), (("wi", 0), ("wr", 1)))
         banks = {}
 
         def mx_pass(n, c, o, step):
             if step == 0:
-                number = 2 * n + c if len(banks) < BANKS else len(banks) % BANKS
+                number = 2 * n + c if len(banks) < BANKS else LATER_BANKS[len(banks) - BANKS]
                 banks[n, c, o] = psum.tile([P, CHUNK], F32, name="acc", tag="bank%d" % number)
             name, t = terms[o][step // PASSES]
             a = step % PASSES
-            first = (J * (2 * a + t) + CHUNK * c) // 4
+            first = (HALF * (2 * a + t) + CHUNK * (c % 2)) // 4
             nc.tensor.matmul_mx(
                 out=banks[n, c, o][:],
                 lhsT=codes[name, a, n].bitcast(FP8X4),
                 lhsT_scale=code_scales[name, a, n],
                 rhs=parted[t, c, a].bitcast(FP4X4),
-                rhs_scale=planes[:, first : first + CHUNK // 4].bitcast(U8),
+                rhs_scale=planes[c // 2][:, first : first + CHUNK // 4].bitcast(U8),
                 start=(step == 0),
                 stop=(step == 2 * PASSES - 1),
             )
@@ -263,7 +278,7 @@ def tile_list_cpxtab_gate_kernel(
         for n, c in opening:
             for step in (0, 1):
                 mx_pass(n, c, 1, step)
-        for n, c in opening:
+        for n, c in sorted(opening, key=lambda s: s[0] // 2):
             mx_pass(n, c, 1, 2)
         for n, c in sorted(opening):
             mx_pass(n, c, 1, 3)
@@ -276,59 +291,49 @@ def tile_list_cpxtab_gate_kernel(
         gather_gate(0, 0)
         gather_gate(0, 1)
         gather_gate(0, 2, 2)
-        gather_gate(1, 0, 2)
-        gather_gate(1, 2, 2)
         for c in (0, 1):
             sum_for_gpsimd(0, c, 0)
         for o in (1, 0):
             for c in (0, 1):
                 on_gpsimd(0, c, o)
+            store(0, 0, o, 2)
         for o in (1, 0):
             for c in (2, 3):
                 sum_for_gpsimd(0, c, o)
-        on_gpsimd(0, 2, 1, 2)
-        store(0, 0, 1, 4)
-        on_gpsimd(1, 0, 1, 2)
-        for c in (0, 1):
-            sum_for_vector(1, c, 0)
-        for o in (0, 1):
-            store(1, 0, o, 2)
-        gather_gate(2, 0, 2)
-        on_gpsimd(0, 2, 0, 2)
-        store(0, 0, 0, 4)
+            on_gpsimd(0, 2, o, 2)
+        for c in (0, 2):
+            gather_gate(1, c, 2)
         for c in (2, 3):
             sum_for_gpsimd(1, c, 1)
-        on_gpsimd(1, 2, 1, 2)
-        store(1, 2, 1, 2)
-        sum_for_vector(1, 2, 0)
-        gather_gate(3, 0, 2)
-        sum_for_vector(1, 3, 0)
-        store(1, 2, 0, 2)
-        gather_gate(2, 2, 2)
-        on_gpsimd(2, 0, 1, 2)
-        store(2, 0, 1, 2)
-        for c in (0, 1):
-            sum_for_vector(2, c, 0)
-        store(2, 0, 0, 2)
-        on_gpsimd(3, 0, 1, 2)
-        store(3, 0, 1, 2)
+        for c in range(4):
+            sum_for_vector(1, c, 0)
+        for c in (0, 2):
+            on_gpsimd(1, c, 1, 2)
+        for n, c, o in ((0, 2, 1), (1, 0, 0), (0, 2, 0), (1, 0, 1), (1, 2, 1), (1, 2, 0)):
+            store(n, c, o, 2)
+        for c in (0, 2):
+            gather_gate(2, c, 2)
         for c in (2, 3):
             sum_for_gpsimd(2, c, 1)
-        on_gpsimd(2, 2, 1, 2)
-        sum_for_vector(2, 2, 0)
+        for c in range(4):
+            sum_for_vector(2, c, 0)
+        on_gpsimd(2, 0, 1, 2)
+        for c in (2, 3):
+            on_gpsimd(2, c, 1)
+        for c, o, chunks in ((0, 0, 2), (2, 0, 1), (0, 1, 2), (2, 1, 1), (3, 0, 1), (3, 1, 1)):
+            store(2, c, o, chunks)
+        gather_gate(3, 0, 2)
+        sum_for_vector(3, 0, 0)
         gather_gate(3, 2)
-        sum_for_vector(2, 3, 0)
-        store(2, 2, 0, 2)
+        sum_for_vector(3, 1, 0)
         for c in (0, 1):
-            sum_for_vector(3, c, 0)
-        store(3, 0, 0, 2)
-        store(2, 2, 1, 2)
+            on_gpsimd(3, c, 1)
+        for c, o in ((0, 0), (0, 1), (1, 0), (1, 1)):
+            store(3, c, o, 1)
         gather_gate(3, 3)
         sum_for_gpsimd(3, 2, 1)
         on_gpsimd(3, 2, 1)
-        for c in (2, 3):
-            sum_for_vector(3, c, 0)
-            store(3, c, 0, 1)
-        sum_for_vector(3, 3, 1)
-        for c in (2, 3):
-            store(3, c, 1, 1)
+        for c, o in ((2, 0), (3, 0), (3, 1)):
+            sum_for_vector(3, c, o)
+        for c, o in ((2, 0), (2, 1), (3, 0), (3, 1)):
+            store(3, c, o, 1)

@@ -296,7 +296,6 @@ def tile_list_cpxtab_gate_kernel(
         for o in (1, 0):
             for c in (0, 1):
                 on_gpsimd(0, c, o)
-            store(0, 0, o, 2)
         for o in (1, 0):
             for c in (2, 3):
                 sum_for_gpsimd(0, c, o)
@@ -309,31 +308,31 @@ def tile_list_cpxtab_gate_kernel(
             sum_for_vector(1, c, 0)
         for c in (0, 2):
             on_gpsimd(1, c, 1, 2)
-        for n, c, o in ((0, 2, 1), (1, 0, 0), (0, 2, 0), (1, 0, 1), (1, 2, 1), (1, 2, 0)):
-            store(n, c, o, 2)
+        for o in (1, 0):
+            store(0, 0, o, 4)
+        for c, o in ((0, 0), (0, 1), (2, 1), (2, 0)):
+            store(1, c, o, 2)
         for c in (0, 2):
             gather_gate(2, c, 2)
         for c in (2, 3):
             sum_for_gpsimd(2, c, 1)
         for c in range(4):
             sum_for_vector(2, c, 0)
-        on_gpsimd(2, 0, 1, 2)
-        for c in (2, 3):
-            on_gpsimd(2, c, 1)
-        for c, o, chunks in ((0, 0, 2), (2, 0, 1), (0, 1, 2), (2, 1, 1), (3, 0, 1), (3, 1, 1)):
-            store(2, c, o, chunks)
+        for c in (0, 2):
+            on_gpsimd(2, c, 1, 2)
+        for c, o in ((0, 0), (0, 1), (2, 1), (2, 0)):
+            store(2, c, o, 2)
         gather_gate(3, 0, 2)
         sum_for_vector(3, 0, 0)
         gather_gate(3, 2)
         sum_for_vector(3, 1, 0)
-        for c in (0, 1):
-            on_gpsimd(3, c, 1)
-        for c, o in ((0, 0), (0, 1), (1, 0), (1, 1)):
-            store(3, c, o, 1)
+        on_gpsimd(3, 0, 1, 2)
+        for o in (1, 0):
+            store(3, 0, o, 2)
         gather_gate(3, 3)
         sum_for_gpsimd(3, 2, 1)
         on_gpsimd(3, 2, 1)
         for c, o in ((2, 0), (3, 0), (3, 1)):
             sum_for_vector(3, c, o)
-        for c, o in ((2, 0), (2, 1), (3, 0), (3, 1)):
+        for c, o in ((2, 1), (2, 0), (3, 0), (3, 1)):
             store(3, c, o, 1)

@@ -26,36 +26,35 @@ BANKS = 8
 PART = 4 * P
 SCALE_ROWS = 96
 
-LATER_BANKS = (0, 1, 4, 5, 6, 7) + (2, 3, 4, 5, 0, 1) + (6, 7, 2, 3, 4, 5) + (6, 7, 0, 1, 2, 3)
+LATER_BANKS = (0, 1, 4, 5, 6, 7) + (4, 5, 0, 2, 3, 1) + (6, 7, 2, 3, 4, 5) + (6, 7, 0, 1, 2, 3)
 
 PLACE_KIB = {
-    "scale_window0": 14,
+    "scale_window0": 15,
     "word_window1": 0,
     "gate_window3": 0,
-    "raw_wr0": 16,
-    "codes_neg0": 16,
+    "raw_wr0": 18,
+    "codes_neg0": 18,
+    "gate2_2": 16,
     "codes_neg2": 20,
-    "parted0_2": 22,
-    "scale_window1": 30,
-    "raw_wr1": 26,
-    "picked1_2": 26,
-    "picked1_3": 28,
-    "raw_wi0": 40,
-    "raw_wi1": 48,
-    "gate_window0": 36,
-    "planes1": 52,
-    "gate2_0": 36,
-    "gate2_2": 40,
-    "codes_wr1_2": 92,
-    "gate3_0": 92,
-    "parted0_1": 88,
-    "gate3_2": 88,
-    "parted1_1": 90,
-    "gate3_3": 90,
-    "word_window0": 56,
-    "gate_window1": 56,
-    "grouped_wi": 72,
-    "gate_window2": 72,
+    "parted0_2": 25,
+    "scale_window1": 33,
+    "raw_wr1": 29,
+    "picked1_2": 29,
+    "picked1_3": 31,
+    "raw_wi0": 41,
+    "raw_wi1": 49,
+    "gate_window0": 37,
+    "planes1": 53,
+    "word_window0": 57,
+    "gate_window1": 57,
+    "grouped_wi": 73,
+    "gate_window2": 73,
+    "parted1_1": 89,
+    "gate3_2": 89,
+    "codes_wr1_1": 93,
+    "gate2_0": 93,
+    "codes_wr1_2": 97,
+    "gate3_0": 97,
 }
 
 
@@ -152,8 +151,8 @@ def tile_list_cpxtab_gate_kernel(
             cast(grouped_wi[:, a * pass_width : (a + 1) * pass_width], raw["wi", a][:])
         grouped_neg = sbuf("grouped_neg", [P, PASSES * pass_width], BF16)
         nc.scalar.activation(
-            grouped_neg[:].rearrange("p (h a x) -> p h a x", h=2, a=PASSES),
-            grouped_wi[:].rearrange("p (a h x) -> p h a x", h=2, a=PASSES),
+            grouped_neg[:].rearrange("p (n a x) -> p n a x", n=ROW_TILES, a=PASSES),
+            grouped_wi[:].rearrange("p (a n x) -> p n a x", n=ROW_TILES, a=PASSES),
             COPY,
             scale=-1.0,
         )
@@ -198,9 +197,10 @@ def tile_list_cpxtab_gate_kernel(
         for first in (0, 2):
             values = grouped_wr0[:, first * PART : (first + 2) * PART]
             quantise("wr0_%d" % first, "wr", values, [(0, first), (0, first + 1)])
-        for first in (0, 2):
-            values = grouped_neg[:, first * PASSES * PART : (first + 2) * PASSES * PART]
-            quantise("neg%d" % first, "neg", values, [(a, n) for a in range(PASSES) for n in (first, first + 1)])
+        for first, count in ((0, 2), (2, 2)):
+            values = grouped_neg[:, first * PASSES * PART : (first + count) * PASSES * PART]
+            parts = [(a, n) for n in range(first, first + count) for a in range(PASSES)]
+            quantise("neg%d" % first, "neg", values, parts)
         for n in (0, 1):
             quantise("wr1_%d" % n, "wr", grouped_wr1[n], [(1, n)])
         part_words(0, 2, 2)
@@ -255,14 +255,19 @@ def tile_list_cpxtab_gate_kernel(
             make_sum(n, c, o)
             empty(n, c, o)
 
-        gates = {}
+        gates, gate_tiles = {}, {}
 
         def gather_gate(n, c, chunks=1):
-            gate = sbuf("gate%d_%d" % (n, c), [P, chunks * CHUNK], F32)
-            nc.vector.tensor_copy(gate[:], gate_window[n][:].indirect(listed(c * CHUNK, chunks * CHUNK)))
-            gates[n, c, chunks] = gate[:]
-            for place in range(chunks):
-                gates[n, c + place, 1] = gate[:, columns(place)]
+            if (n, c) not in gate_tiles:
+                width = 2 if (n, c) in ((0, 0), (3, 2)) else chunks
+                tile = sbuf("gate%d_%d" % (n, c), [P, width * CHUNK], F32)
+                for place in range(width):
+                    gate_tiles[n, c + place] = tile
+                    for count in range(1, width - place + 1):
+                        gates[n, c + place, count] = tile[:, columns(place, count)]
+            nc.vector.tensor_copy(
+                gates[n, c, chunks], gate_window[n][:].indirect(listed(c * CHUNK, chunks * CHUNK))
+            )
 
         def on_gpsimd(n, c, o, chunks=1):
             values = results[n, o][:, columns(c, chunks)]
@@ -293,43 +298,43 @@ def tile_list_cpxtab_gate_kernel(
         gather_gate(0, 2, 2)
         for c in (0, 1):
             sum_for_gpsimd(0, c, 0)
-        for o in (1, 0):
-            for c in (0, 1):
-                on_gpsimd(0, c, o)
+        for c in (0, 1):
+            on_gpsimd(0, c, 1)
+        on_gpsimd(0, 0, 0, 2)
         for o in (1, 0):
             for c in (2, 3):
                 sum_for_gpsimd(0, c, o)
             on_gpsimd(0, 2, o, 2)
+            store(0, 0, o, 4)
         for c in (0, 2):
             gather_gate(1, c, 2)
+        for c in (0, 1, 2):
+            sum_for_vector(1, c, 0)
         for c in (2, 3):
             sum_for_gpsimd(1, c, 1)
-        for c in range(4):
-            sum_for_vector(1, c, 0)
         for c in (0, 2):
             on_gpsimd(1, c, 1, 2)
-        for o in (1, 0):
-            store(0, 0, o, 4)
-        for c, o in ((0, 0), (0, 1), (2, 1), (2, 0)):
-            store(1, c, o, 2)
-        for c in (0, 2):
-            gather_gate(2, c, 2)
+        gather_gate(2, 0, 2)
+        sum_for_vector(1, 3, 0)
+        gather_gate(2, 2, 2)
+        for o in (0, 1):
+            store(1, 0, o, 4)
         for c in (2, 3):
             sum_for_gpsimd(2, c, 1)
         for c in range(4):
             sum_for_vector(2, c, 0)
         for c in (0, 2):
             on_gpsimd(2, c, 1, 2)
-        for c, o in ((0, 0), (0, 1), (2, 1), (2, 0)):
-            store(2, c, o, 2)
+        for c, o, chunks in ((0, 0, 3), (0, 1, 2), (2, 1, 2), (3, 0, 1)):
+            store(2, c, o, chunks)
         gather_gate(3, 0, 2)
-        sum_for_vector(3, 0, 0)
-        gather_gate(3, 2)
-        sum_for_vector(3, 1, 0)
+        for c in (0, 1):
+            sum_for_vector(3, c, 0)
         on_gpsimd(3, 0, 1, 2)
-        for o in (1, 0):
+        for o in (0, 1):
             store(3, 0, o, 2)
-        gather_gate(3, 3)
+        for c in (2, 3):
+            gather_gate(3, c)
         sum_for_gpsimd(3, 2, 1)
         on_gpsimd(3, 2, 1)
         for c, o in ((2, 0), (3, 0), (3, 1)):

@@ -26,35 +26,32 @@ BANKS = 8
 PART = 4 * P
 SCALE_ROWS = 96
 
-LATER_BANKS = (0, 1, 4, 5, 6, 7) + (4, 5, 0, 2, 3, 1) + (6, 7, 2, 3, 4, 5) + (6, 7, 0, 1, 2, 3)
+LATER_BANKS = (0, 1, 4, 5, 6, 7) + (4, 5, 0, 1, 2, 3) + (6, 7, 2, 3, 4, 5) + (6, 7, 0, 1, 2, 3)
 
 PLACE_KIB = {
-    "scale_window0": 15,
-    "word_window1": 0,
-    "gate_window3": 0,
-    "raw_wr0": 18,
-    "codes_neg0": 18,
-    "gate2_2": 16,
-    "codes_neg2": 20,
-    "parted0_2": 25,
-    "scale_window1": 33,
-    "raw_wr1": 29,
-    "picked1_2": 29,
-    "picked1_3": 31,
-    "raw_wi0": 41,
-    "raw_wi1": 49,
-    "gate_window0": 37,
-    "planes1": 53,
-    "word_window0": 57,
-    "gate_window1": 57,
-    "grouped_wi": 73,
-    "gate_window2": 73,
-    "parted1_1": 89,
-    "gate3_2": 89,
-    "codes_wr1_1": 93,
-    "gate2_0": 93,
-    "codes_wr1_2": 97,
-    "gate3_0": 97,
+    "grouped_wi": 0,
+    "gate_window2": 0,
+    "word_window1": 16,
+    "scale_window0": 30,
+    "raw_wr0": 32,
+    "codes_neg": 32,
+    "parted0_2": 36,
+    "scale_window1": 44,
+    "raw_wr1": 40,
+    "picked1_2": 40,
+    "picked1_3": 42,
+    "gate_window0": 48,
+    "raw_wi0": 52,
+    "raw_wi1": 60,
+    "planes1": 64,
+    "word_window0": 68,
+    "gate_window1": 68,
+    "parted1_1": 84,
+    "gate3_2": 84,
+    "codes_wr1_2": 88,
+    "gate3_0": 88,
+    "gate2_0": 48,
+    "gate2_2": 52,
 }
 
 
@@ -150,12 +147,7 @@ def tile_list_cpxtab_gate_kernel(
         for a in range(PASSES):
             cast(grouped_wi[:, a * pass_width : (a + 1) * pass_width], raw["wi", a][:])
         grouped_neg = sbuf("grouped_neg", [P, PASSES * pass_width], BF16)
-        nc.scalar.activation(
-            grouped_neg[:].rearrange("p (n a x) -> p n a x", n=ROW_TILES, a=PASSES),
-            grouped_wi[:].rearrange("p (a n x) -> p n a x", n=ROW_TILES, a=PASSES),
-            COPY,
-            scale=-1.0,
-        )
+        nc.scalar.activation(grouped_neg[:], grouped_wi[:], COPY, scale=-1.0)
         grouped_wr0 = sbuf("grouped_wr0", [P, pass_width], BF16)
         for first in (0, 2):
             cast(grouped_wr0[:, first * PART : (first + 2) * PART], raw["wr", 0][:, :, first * P : (first + 2) * P])
@@ -197,10 +189,7 @@ def tile_list_cpxtab_gate_kernel(
         for first in (0, 2):
             values = grouped_wr0[:, first * PART : (first + 2) * PART]
             quantise("wr0_%d" % first, "wr", values, [(0, first), (0, first + 1)])
-        for first, count in ((0, 2), (2, 2)):
-            values = grouped_neg[:, first * PASSES * PART : (first + count) * PASSES * PART]
-            parts = [(a, n) for n in range(first, first + count) for a in range(PASSES)]
-            quantise("neg%d" % first, "neg", values, parts)
+        quantise("neg", "neg", grouped_neg[:], [(a, n) for a in range(PASSES) for n in range(ROW_TILES)])
         for n in (0, 1):
             quantise("wr1_%d" % n, "wr", grouped_wr1[n], [(1, n)])
         part_words(0, 2, 2)
@@ -212,10 +201,12 @@ def tile_list_cpxtab_gate_kernel(
             part_words(1, c)
 
         gate_window = []
-        for n in range(ROW_TILES):
-            gate_window.append(sbuf("gate_window%d" % n, [P, T], F32))
-            nc.sync.dma_start(gate_window[n][:], gT[n * P : (n + 1) * P, :])
-            if n == 0:
+        for first, count in ((0, 1), (1, 1), (2, 2)):
+            tile = sbuf("gate_window%d" % first, [P, count, T], F32)
+            rows = gT[first * P : (first + count) * P, :]
+            nc.sync.dma_start(tile[:], rows.rearrange("(n p) t -> p n t", p=P))
+            gate_window.extend(tile[:, place, :] for place in range(count))
+            if first == 0:
                 clear_planes(1)
                 move_scales(1)
 
@@ -266,7 +257,7 @@ def tile_list_cpxtab_gate_kernel(
                     for count in range(1, width - place + 1):
                         gates[n, c + place, count] = tile[:, columns(place, count)]
             nc.vector.tensor_copy(
-                gates[n, c, chunks], gate_window[n][:].indirect(listed(c * CHUNK, chunks * CHUNK))
+                gates[n, c, chunks], gate_window[n].indirect(listed(c * CHUNK, chunks * CHUNK))
             )
 
         def on_gpsimd(n, c, o, chunks=1):
@@ -308,17 +299,16 @@ def tile_list_cpxtab_gate_kernel(
             store(0, 0, o, 4)
         for c in (0, 2):
             gather_gate(1, c, 2)
-        for c in (0, 1, 2):
+        for c in range(4):
             sum_for_vector(1, c, 0)
+        store(1, 0, 0, 4)
         for c in (2, 3):
             sum_for_gpsimd(1, c, 1)
         for c in (0, 2):
             on_gpsimd(1, c, 1, 2)
-        gather_gate(2, 0, 2)
-        sum_for_vector(1, 3, 0)
-        gather_gate(2, 2, 2)
-        for o in (0, 1):
-            store(1, 0, o, 4)
+            store(1, c, 1, 2)
+        for c in (0, 2):
+            gather_gate(2, c, 2)
         for c in (2, 3):
             sum_for_gpsimd(2, c, 1)
         for c in range(4):
@@ -339,5 +329,5 @@ def tile_list_cpxtab_gate_kernel(
         on_gpsimd(3, 2, 1)
         for c, o in ((2, 0), (3, 0), (3, 1)):
             sum_for_vector(3, c, o)
-        for c, o in ((2, 1), (2, 0), (3, 0), (3, 1)):
-            store(3, c, o, 1)
+        for c, o, chunks in ((2, 1, 1), (2, 0, 2), (3, 1, 1)):
+            store(3, c, o, chunks)

@@ -26,7 +26,7 @@ BANKS = 8
 PART = 4 * P
 SCALE_ROWS = 96
 
-LATER_BANKS = (0, 1, 4, 5, 6, 7) + (4, 5, 0, 1, 2, 3) + (6, 7, 2, 3, 4, 5) + (6, 7, 0, 1, 2, 3)
+LATER_BANKS = (0, 1, 2, 3, 4, 5, 6, 7, 0, 1, 4, 5) + (6, 7, 4, 5, 2, 3) + (6, 7, 0, 1, 4, 5)
 
 PLACE_KIB = {
     "grouped_wi": 0,
@@ -35,21 +35,21 @@ PLACE_KIB = {
     "scale_window0": 30,
     "raw_wr0": 32,
     "codes_neg": 32,
-    "parted0_2": 36,
+    "picked0_3": 36,
     "scale_window1": 44,
     "raw_wr1": 40,
     "picked1_2": 40,
-    "picked1_3": 42,
+    "parted0_2": 44,
+    "parted0_3": 46,
     "gate_window0": 48,
-    "raw_wi0": 52,
-    "raw_wi1": 60,
-    "planes1": 64,
-    "word_window0": 68,
-    "gate_window1": 68,
-    "parted1_1": 84,
-    "gate3_2": 84,
-    "codes_wr1_2": 88,
-    "gate3_0": 88,
+    "raw_wi0": 48,
+    "raw_wi1": 56,
+    "word_window0": 64,
+    "gate_window1": 64,
+    "parted1_1": 80,
+    "gate3_2": 80,
+    "codes_wr1_2": 84,
+    "gate3_0": 84,
     "gate2_0": 48,
     "gate2_2": 52,
 }
@@ -89,7 +89,8 @@ def tile_list_cpxtab_gate_kernel(
             planes[h] = sbuf("planes%d" % h, [P, PASSES * 2 * HALF // 4], I32)
             nc.gpsimd.memset(planes[h][:], 0)
 
-        clear_planes(0)
+        for h in range(2):
+            clear_planes(h)
 
         raw = {}
 
@@ -103,8 +104,8 @@ def tile_list_cpxtab_gate_kernel(
             return window
 
         load_weight("wi", wi, 0)
-        load_weight("wi", wi, 1)
         word_window = [load_words(0, tab_words)]
+        load_weight("wi", wi, 1)
 
         picked_scales = {}
         for h in range(2):
@@ -176,12 +177,17 @@ def tile_list_cpxtab_gate_kernel(
                 for a in range(PASSES):
                     parted[t, c + place, a] = tile[:, a, place * CHUNK : (place + 1) * CHUNK]
 
-        quantise("wi", "wi", grouped_wi[:], [(a, n) for a in range(PASSES) for n in range(ROW_TILES)])
-        gather_words(0, 0)
-        gather_words(0, 1)
-        part_words(0, 0)
-        gather_words(0, 2, 2)
-        part_words(0, 1)
+        def quantise_wi(a):
+            values = grouped_wi[:, a * pass_width : (a + 1) * pass_width]
+            quantise("wi%d" % a, "wi", values, [(a, n) for n in range(ROW_TILES)])
+
+        quantise_wi(0)
+        for c in (0, 1):
+            gather_words(0, c)
+        for c in (0, 1):
+            part_words(0, c)
+        gather_words(0, 2)
+        quantise_wi(1)
         for c in (0, 1):
             gather_words(1, c)
         for c in (0, 1):
@@ -192,13 +198,13 @@ def tile_list_cpxtab_gate_kernel(
         quantise("neg", "neg", grouped_neg[:], [(a, n) for a in range(PASSES) for n in range(ROW_TILES)])
         for n in (0, 1):
             quantise("wr1_%d" % n, "wr", grouped_wr1[n], [(1, n)])
-        part_words(0, 2, 2)
+        gather_words(0, 3)
         for n in (2, 3):
             quantise("wr1_%d" % n, "wr", grouped_wr1[n], [(1, n)])
+        gather_words(1, 2, 2)
         for c in (2, 3):
-            gather_words(1, c)
-        for c in (2, 3):
-            part_words(1, c)
+            part_words(0, c)
+        part_words(1, 2, 2)
 
         gate_window = []
         for first, count in ((0, 1), (1, 1), (2, 2)):
@@ -207,10 +213,9 @@ def tile_list_cpxtab_gate_kernel(
             nc.sync.dma_start(tile[:], rows.rearrange("(n p) t -> p n t", p=P))
             gate_window.extend(tile[:, place, :] for place in range(count))
             if first == 0:
-                clear_planes(1)
                 move_scales(1)
 
-        terms = ((("wr", 0), ("neg", 1)), (("wi", 0), ("wr", 1)))
+        terms = ((("neg", 1), ("wr", 0)), (("wi", 0), ("wr", 1)))
         banks = {}
 
         def mx_pass(n, c, o, step):
@@ -271,8 +276,8 @@ def tile_list_cpxtab_gate_kernel(
             nc.sync.dma_start(outs[o][n * P : (n + 1) * P, columns(c, chunks)], results[n, o][:, columns(c, chunks)])
 
         opening = [(n, c) for c in (0, 1) for n in range(ROW_TILES)]
-        for n, c in opening:
-            for step in (0, 1):
+        for step in (0, 1):
+            for n, c in opening:
                 mx_pass(n, c, 1, step)
         for n, c in sorted(opening, key=lambda s: s[0] // 2):
             mx_pass(n, c, 1, 2)
@@ -290,6 +295,8 @@ def tile_list_cpxtab_gate_kernel(
         for c in (0, 1):
             sum_for_gpsimd(0, c, 0)
         for c in (0, 1):
+            make_sum(1, c, 0)
+        for c in (0, 1):
             on_gpsimd(0, c, 1)
         on_gpsimd(0, 0, 0, 2)
         for o in (1, 0):
@@ -299,14 +306,16 @@ def tile_list_cpxtab_gate_kernel(
             store(0, 0, o, 4)
         for c in (0, 2):
             gather_gate(1, c, 2)
-        for c in range(4):
+        for c in (0, 1):
+            on_vector(1, c, 0)
+        for c in (2, 3):
             sum_for_vector(1, c, 0)
-        store(1, 0, 0, 4)
         for c in (2, 3):
             sum_for_gpsimd(1, c, 1)
         for c in (0, 2):
             on_gpsimd(1, c, 1, 2)
-            store(1, c, 1, 2)
+        for o in (0, 1):
+            store(1, 0, o, 4)
         for c in (0, 2):
             gather_gate(2, c, 2)
         for c in (2, 3):
@@ -315,7 +324,7 @@ def tile_list_cpxtab_gate_kernel(
             sum_for_vector(2, c, 0)
         for c in (0, 2):
             on_gpsimd(2, c, 1, 2)
-        for c, o, chunks in ((0, 0, 3), (0, 1, 2), (2, 1, 2), (3, 0, 1)):
+        for c, o, chunks in ((0, 1, 2), (0, 0, 4), (2, 1, 2)):
             store(2, c, o, chunks)
         gather_gate(3, 0, 2)
         for c in (0, 1):

@@ -26,12 +26,13 @@ BANKS = 8
 PART = 4 * P
 SCALE_ROWS = 96
 
-LATER_BANKS = (0, 1, 2, 3, 4, 5, 6, 7, 0, 1, 4, 5) + (6, 7, 4, 5, 2, 3) + (6, 7, 0, 1, 4, 5)
+LATER_BANKS = (0, 1, 2, 3, 4, 5, 6, 7, 0, 1, 4, 5) + (6, 7, 4, 5, 2, 3) + (4, 5, 0, 1, 6, 7)
 
 PLACE_KIB = {
-    "grouped_wi": 0,
+    "word_window0": 0,
     "gate_window2": 0,
     "word_window1": 16,
+    "gate_window3": 16,
     "scale_window0": 30,
     "raw_wr0": 32,
     "codes_neg": 32,
@@ -42,15 +43,16 @@ PLACE_KIB = {
     "parted0_2": 44,
     "parted0_3": 46,
     "gate_window0": 48,
-    "raw_wi0": 48,
-    "raw_wi1": 56,
-    "word_window0": 64,
-    "gate_window1": 64,
-    "parted1_1": 80,
-    "gate3_2": 80,
-    "codes_wr1_2": 84,
-    "gate3_0": 84,
+    "raw_wi0": 60,
+    "planes1": 64,
     "gate2_0": 48,
+    "gate_window1": 68,
+    "raw_wi1": 68,
+    "grouped_wi": 76,
+    "parted0_1": 84,
+    "gate3_2": 84,
+    "codes_wr1_2": 88,
+    "gate3_0": 88,
     "gate2_2": 52,
 }
 
@@ -89,8 +91,7 @@ def tile_list_cpxtab_gate_kernel(
             planes[h] = sbuf("planes%d" % h, [P, PASSES * 2 * HALF // 4], I32)
             nc.gpsimd.memset(planes[h][:], 0)
 
-        for h in range(2):
-            clear_planes(h)
+        clear_planes(0)
 
         raw = {}
 
@@ -177,17 +178,17 @@ def tile_list_cpxtab_gate_kernel(
                 for a in range(PASSES):
                     parted[t, c + place, a] = tile[:, a, place * CHUNK : (place + 1) * CHUNK]
 
-        def quantise_wi(a):
-            values = grouped_wi[:, a * pass_width : (a + 1) * pass_width]
-            quantise("wi%d" % a, "wi", values, [(a, n) for n in range(ROW_TILES)])
+        def quantise_wi(a, first, count):
+            values = grouped_wi[:, a * pass_width + first * PART : a * pass_width + (first + count) * PART]
+            quantise("wi%d_%d" % (a, first), "wi", values, [(a, n) for n in range(first, first + count)])
 
-        quantise_wi(0)
+        quantise_wi(0, 0, ROW_TILES)
         for c in (0, 1):
             gather_words(0, c)
         for c in (0, 1):
             part_words(0, c)
         gather_words(0, 2)
-        quantise_wi(1)
+        quantise_wi(1, 0, ROW_TILES)
         for c in (0, 1):
             gather_words(1, c)
         for c in (0, 1):
@@ -207,12 +208,11 @@ def tile_list_cpxtab_gate_kernel(
         part_words(1, 2, 2)
 
         gate_window = []
-        for first, count in ((0, 1), (1, 1), (2, 2)):
-            tile = sbuf("gate_window%d" % first, [P, count, T], F32)
-            rows = gT[first * P : (first + count) * P, :]
-            nc.sync.dma_start(tile[:], rows.rearrange("(n p) t -> p n t", p=P))
-            gate_window.extend(tile[:, place, :] for place in range(count))
-            if first == 0:
+        for n in range(ROW_TILES):
+            gate_window.append(sbuf("gate_window%d" % n, [P, T], F32))
+            nc.sync.dma_start(gate_window[n][:], gT[n * P : (n + 1) * P, :])
+            if n == 0:
+                clear_planes(1)
                 move_scales(1)
 
         terms = ((("neg", 1), ("wr", 0)), (("wi", 0), ("wr", 1)))
@@ -255,14 +255,14 @@ def tile_list_cpxtab_gate_kernel(
 
         def gather_gate(n, c, chunks=1):
             if (n, c) not in gate_tiles:
-                width = 2 if (n, c) in ((0, 0), (3, 2)) else chunks
+                width = 2 if (n, c) in ((0, 0), (3, 0), (3, 2)) else chunks
                 tile = sbuf("gate%d_%d" % (n, c), [P, width * CHUNK], F32)
                 for place in range(width):
                     gate_tiles[n, c + place] = tile
                     for count in range(1, width - place + 1):
                         gates[n, c + place, count] = tile[:, columns(place, count)]
             nc.vector.tensor_copy(
-                gates[n, c, chunks], gate_window[n].indirect(listed(c * CHUNK, chunks * CHUNK))
+                gates[n, c, chunks], gate_window[n][:].indirect(listed(c * CHUNK, chunks * CHUNK))
             )
 
         def on_gpsimd(n, c, o, chunks=1):
@@ -314,19 +314,22 @@ def tile_list_cpxtab_gate_kernel(
             sum_for_gpsimd(1, c, 1)
         for c in (0, 2):
             on_gpsimd(1, c, 1, 2)
-        for o in (0, 1):
-            store(1, 0, o, 4)
+        for c, o, chunks in ((0, 0, 4), (0, 1, 2)):
+            store(1, c, o, chunks)
         for c in (0, 2):
             gather_gate(2, c, 2)
+        for c in (0, 1):
+            sum_for_vector(2, c, 0)
         for c in (2, 3):
             sum_for_gpsimd(2, c, 1)
-        for c in range(4):
+        for c in (2, 3):
             sum_for_vector(2, c, 0)
         for c in (0, 2):
             on_gpsimd(2, c, 1, 2)
-        for c, o, chunks in ((0, 1, 2), (0, 0, 4), (2, 1, 2)):
-            store(2, c, o, chunks)
-        gather_gate(3, 0, 2)
+        for n, c, o in ((1, 2, 1), (2, 0, 0), (2, 0, 1), (2, 2, 0), (2, 2, 1)):
+            store(n, c, o, 2)
+        for c in (0, 1):
+            gather_gate(3, c)
         for c in (0, 1):
             sum_for_vector(3, c, 0)
         on_gpsimd(3, 0, 1, 2)
@@ -338,5 +341,5 @@ def tile_list_cpxtab_gate_kernel(
         on_gpsimd(3, 2, 1)
         for c, o in ((2, 0), (3, 0), (3, 1)):
             sum_for_vector(3, c, o)
-        for c, o, chunks in ((2, 1, 1), (2, 0, 2), (3, 1, 1)):
-            store(3, c, o, chunks)
+        for c, o in ((2, 1), (2, 0), (3, 0), (3, 1)):
+            store(3, c, o, 1)

@@ -26,7 +26,7 @@ BANKS = 8
 PART = 4 * P
 SCALE_ROWS = 96
 
-LATER_BANKS = (0, 1, 2, 3, 4, 5, 6, 7, 0, 1, 4, 5) + (6, 7, 4, 5, 2, 3) + (4, 5, 0, 1, 6, 7)
+LATER_BANKS = (0, 1, 2, 3, 4, 5, 6, 7, 0, 1, 4, 5) + (6, 7, 4, 2, 3, 5) + (4, 5, 0, 1, 6, 7)
 
 PLACE_KIB = {
     "word_window0": 0,
@@ -35,12 +35,11 @@ PLACE_KIB = {
     "gate_window3": 16,
     "scale_window0": 30,
     "raw_wr0": 32,
-    "codes_neg": 32,
-    "picked0_3": 36,
+    "picked0_3": 32,
+    "parted0_2": 36,
     "scale_window1": 44,
     "raw_wr1": 40,
     "picked1_2": 40,
-    "parted0_2": 44,
     "parted0_3": 46,
     "gate_window0": 48,
     "raw_wi0": 60,
@@ -54,6 +53,8 @@ PLACE_KIB = {
     "codes_wr1_2": 88,
     "gate3_0": 88,
     "gate2_2": 52,
+    "picked1_0": 92,
+    "codes_neg": 92,
 }
 
 
@@ -193,18 +194,16 @@ def tile_list_cpxtab_gate_kernel(
             gather_words(1, c)
         for c in (0, 1):
             part_words(1, c)
+        quantise("neg", "neg", grouped_neg[:], [(a, n) for a in range(PASSES) for n in range(ROW_TILES)])
         for first in (0, 2):
             values = grouped_wr0[:, first * PART : (first + 2) * PART]
             quantise("wr0_%d" % first, "wr", values, [(0, first), (0, first + 1)])
-        quantise("neg", "neg", grouped_neg[:], [(a, n) for a in range(PASSES) for n in range(ROW_TILES)])
-        for n in (0, 1):
-            quantise("wr1_%d" % n, "wr", grouped_wr1[n], [(1, n)])
         gather_words(0, 3)
-        for n in (2, 3):
+        part_words(0, 2)
+        for n in range(ROW_TILES):
             quantise("wr1_%d" % n, "wr", grouped_wr1[n], [(1, n)])
         gather_words(1, 2, 2)
-        for c in (2, 3):
-            part_words(0, c)
+        part_words(0, 3)
         part_words(1, 2, 2)
 
         gate_window = []
@@ -320,12 +319,13 @@ def tile_list_cpxtab_gate_kernel(
             gather_gate(2, c, 2)
         for c in (0, 1):
             sum_for_vector(2, c, 0)
-        for c in (2, 3):
-            sum_for_gpsimd(2, c, 1)
+        sum_for_gpsimd(2, 2, 1)
         for c in (2, 3):
             sum_for_vector(2, c, 0)
-        for c in (0, 2):
-            on_gpsimd(2, c, 1, 2)
+        sum_for_gpsimd(2, 3, 1)
+        on_gpsimd(2, 0, 1, 2)
+        for c in (2, 3):
+            on_gpsimd(2, c, 1)
         for n, c, o in ((1, 2, 1), (2, 0, 0), (2, 0, 1), (2, 2, 0), (2, 2, 1)):
             store(n, c, o, 2)
         for c in (0, 1):

from contextlib import ExitStack

import concourse.mybir as mybir

K, N, T, J = 1024, 512, 4096, 2048
FLOPS = 4 * 2 * K * N * J

F32 = mybir.dt.float32
BF16 = mybir.dt.bfloat16
I32 = mybir.dt.int32
U32 = mybir.dt.uint32
U16 = mybir.dt.uint16
U8 = mybir.dt.uint8
FP8X4 = mybir.dt.float8_e4m3fn_x4
FP4X4 = mybir.dt.float4_e2m1fn_x4
COPY = mybir.ActivationFunctionType.Copy
MULT = mybir.AluOpType.mult

P = 128
PASSES = 2
K_PASS = K // PASSES
CHUNK = 512
HALF = 2 * CHUNK
ROW_TILES = N // P
BANKS = 8
PART = 4 * P
SCALE_ROWS = 96

LATER_BANKS = (0, 1, 2, 3, 4, 5, 6, 7, 0, 1, 4, 5) + (6, 7, 4, 2, 3, 5) + (4, 5, 0, 1, 6, 7)

PLACE_KIB = {
    "word_window0": 0,
    "gate_window2": 0,
    "word_window1": 16,
    "gate_window3": 16,
    "scale_window0": 30,
    "raw_wr0": 32,
    "picked0_3": 32,
    "parted0_2": 36,
    "scale_window1": 44,
    "raw_wr1": 40,
    "picked1_2": 40,
    "parted0_3": 46,
    "gate_window0": 48,
    "raw_wi0": 60,
    "planes1": 64,
    "gate2_0": 48,
    "gate_window1": 68,
    "raw_wi1": 68,
    "grouped_wi": 76,
    "parted0_1": 84,
    "gate3_2": 84,
    "codes_wr1_2": 88,
    "gate3_0": 88,
    "gate2_2": 52,
    "picked1_0": 92,
    "codes_neg": 92,
}


def tile_list_cpxtab_gate_kernel(
    tc, tab_words, tab_scales, tab2_words, tab2_scales, wr, wi, gT, offs, out_0, out_1
):
    nc = tc.nc
    outs = (out_0, out_1)
    with ExitStack() as ctx:
        held = ctx.enter_context(tc.tile_pool(name="held", bufs=1))
        shared = ctx.enter_context(tc.tile_pool(name="shared", bufs=1))
        psum = ctx.enter_context(tc.psum_pool(name="psum", bufs=1))

        def sbuf(name, shape, dtype):
            if name in PLACE_KIB:
                return shared.tile(shape, dtype, name=name, align_bytes=64, offset=PLACE_KIB[name] * 1024)
            return held.tile(shape, dtype, name=name, align_bytes=64)

        offsets = held.tile([P, J // 16], U16, name="offsets")
        nc.sync.dma_start(offsets[:], offs)

        def listed(first, count):
            return offsets[:, first // 16 : (first + count) // 16]

        scale_window = []
        for t, scales in enumerate((tab_scales, tab2_scales)):
            window = sbuf("scale_window%d" % t, [P, T // 4], I32)
            nc.sync.dma_start(window[SCALE_ROWS:P, :], scales.bitcast(I32).rearrange("a q t -> q a t"))
            nc.gpsimd.memset(window[0:SCALE_ROWS, :], 0)
            scale_window.append(window)

        planes = {}

        def clear_planes(h):
            planes[h] = sbuf("planes%d" % h, [P, PASSES * 2 * HALF // 4], I32)
            nc.gpsimd.memset(planes[h][:], 0)

        clear_planes(0)

        raw = {}

        def load_weight(name, w, a):
            raw[name, a] = sbuf("raw_%s%d" % (name, a), [P, 4, N], F32)
            nc.sync.dma_start(raw[name, a][:], w[K_PASS * a : K_PASS * (a + 1), :].rearrange("(p i) n -> p i n", i=4))

        def load_words(t, words):
            window = sbuf("word_window%d" % t, [P, T], I32)
            nc.sync.dma_start(window[:], words[0].rearrange("p t b -> p (t b)").bitcast(I32))
            return window

        load_weight("wi", wi, 0)
        word_window = [load_words(0, tab_words)]
        load_weight("wi", wi, 1)

        picked_scales = {}
        for h in range(2):
            picked_scales[h] = sbuf("picked_scales%d" % h, [P, 2 * HALF], U8)
            for t in range(2):
                nc.vector.tensor_copy(
                    picked_scales[h][:, t * HALF : (t + 1) * HALF],
                    scale_window[t][:].bitcast(U8).indirect(listed(h * HALF, HALF)),
                )

        def move_scales(h):
            for quadrant in (0, 2, 1, 3):
                row = SCALE_ROWS + 8 * quadrant
                nc.sync.dma_start(
                    planes[h][32 * quadrant : 32 * quadrant + 4, :], picked_scales[h][row : row + 8, :].bitcast(I32)
                )

        move_scales(0)
        word_window.append(load_words(1, tab2_words))
        load_weight("wr", wr, 0)
        load_weight("wr", wr, 1)

        codes, code_scales = {}, {}

        def cast(target, source):
            nc.scalar.activation(
                target.rearrange("p (c m i) -> p c i m", m=4, i=4), source.rearrange("p i (c m) -> p c i m", m=4), COPY
            )

        def quantise(label, name, values, parts):
            words = sbuf("codes_" + label, [P, len(parts) * P], U32)
            scales = sbuf("code_scales_" + label, [P, len(parts) * P], U8)
            nc.vector.quantize_mx(out=words[:].bitcast(FP8X4), scales=scales[:], in_=values)
            for place, (a, n) in enumerate(parts):
                codes[name, a, n] = words[:, place * P : (place + 1) * P]
                code_scales[name, a, n] = scales[:, place * P : (place + 1) * P]

        pass_width = ROW_TILES * PART
        grouped_wi = sbuf("grouped_wi", [P, PASSES * pass_width], BF16)
        for a in range(PASSES):
            cast(grouped_wi[:, a * pass_width : (a + 1) * pass_width], raw["wi", a][:])
        grouped_neg = sbuf("grouped_neg", [P, PASSES * pass_width], BF16)
        nc.scalar.activation(grouped_neg[:], grouped_wi[:], COPY, scale=-1.0)
        grouped_wr0 = sbuf("grouped_wr0", [P, pass_width], BF16)
        for first in (0, 2):
            cast(grouped_wr0[:, first * PART : (first + 2) * PART], raw["wr", 0][:, :, first * P : (first + 2) * P])
        grouped_wr1 = {}
        for first, count in ((0, 1), (1, 1), (2, 2)):
            tile = sbuf("grouped_wr1_%d" % first, [P, count * PART], BF16)
            cast(tile[:], raw["wr", 1][:, :, first * P : (first + count) * P])
            for place in range(count):
                grouped_wr1[first + place] = tile[:, place * PART : (place + 1) * PART]

        picked, parted = {}, {}

        def gather_words(t, c, chunks=1):
            picked[t, c] = sbuf("picked%d_%d" % (t, c), [P, chunks * CHUNK], U32)
            nc.vector.tensor_copy(
                picked[t, c][:], word_window[t][:].bitcast(U32).indirect(listed(c * CHUNK, chunks * CHUNK))
            )

        def part_words(t, c, chunks=1):
            tile = sbuf("parted%d_%d" % (t, c), [P, PASSES, chunks * CHUNK], U16)
            nc.vector.tensor_copy(
                tile[:].rearrange("p d (h j) -> p h d j", h=2),
                picked[t, c][:].bitcast(U16).rearrange("p (h j d) -> p h d j", h=2, d=2),
            )
            for place in range(chunks):
                for a in range(PASSES):
                    parted[t, c + place, a] = tile[:, a, place * CHUNK : (place + 1) * CHUNK]

        def quantise_wi(a, first, count):
            values = grouped_wi[:, a * pass_width + first * PART : a * pass_width + (first + count) * PART]
            quantise("wi%d_%d" % (a, first), "wi", values, [(a, n) for n in range(first, first + count)])

        quantise_wi(0, 0, ROW_TILES)
        for c in (0, 1):
            gather_words(0, c)
        for c in (0, 1):
            part_words(0, c)
        gather_words(0, 2)
        quantise_wi(1, 0, ROW_TILES)
        for c in (0, 1):
            gather_words(1, c)
        for c in (0, 1):
            part_words(1, c)
        quantise("neg", "neg", grouped_neg[:], [(a, n) for a in range(PASSES) for n in range(ROW_TILES)])
        for first in (0, 2):
            values = grouped_wr0[:, first * PART : (first + 2) * PART]
            quantise("wr0_%d" % first, "wr", values, [(0, first), (0, first + 1)])
        gather_words(0, 3)
        part_words(0, 2)
        for n in range(ROW_TILES):
            quantise("wr1_%d" % n, "wr", grouped_wr1[n], [(1, n)])
        gather_words(1, 2, 2)
        part_words(0, 3)
        part_words(1, 2, 2)

        gate_window = []
        for n in range(ROW_TILES):
            gate_window.append(sbuf("gate_window%d" % n, [P, T], F32))
            nc.sync.dma_start(gate_window[n][:], gT[n * P : (n + 1) * P, :])
            if n == 0:
                clear_planes(1)
                move_scales(1)

        terms = ((("neg", 1), ("wr", 0)), (("wi", 0), ("wr", 1)))
        banks = {}

        def mx_pass(n, c, o, step):
            if step == 0:
                number = 2 * n + c if len(banks) < BANKS else LATER_BANKS[len(banks) - BANKS]
                banks[n, c, o] = psum.tile([P, CHUNK], F32, name="acc", tag="bank%d" % number)
            name, t = terms[o][step // PASSES]
            a = step % PASSES
            first = (HALF * (2 * a + t) + CHUNK * (c % 2)) // 4
            nc.tensor.matmul_mx(
                out=banks[n, c, o][:],
                lhsT=codes[name, a, n].bitcast(FP8X4),
                lhsT_scale=code_scales[name, a, n],
                rhs=parted[t, c, a].bitcast(FP4X4),
                rhs_scale=planes[c // 2][:, first : first + CHUNK // 4].bitcast(U8),
                start=(step == 0),
                stop=(step == 2 * PASSES - 1),
            )

        results = {(n, o): sbuf("result%d_%d" % (n, o), [P, J], F32) for n in range(ROW_TILES) for o in range(2)}

        def columns(c, chunks=1):
            return slice(c * CHUNK, (c + chunks) * CHUNK)

        def empty(n, c, o):
            nc.scalar.activation(results[n, o][:, columns(c)], banks[n, c, o][:], COPY)

        def make_sum(n, c, o):
            for step in range(2 * PASSES):
                mx_pass(n, c, o, step)

        def sum_for_gpsimd(n, c, o):
            make_sum(n, c, o)
            empty(n, c, o)

        gates, gate_tiles = {}, {}

        def gather_gate(n, c, chunks=1):
            if (n, c) not in gate_tiles:
                width = 2 if (n, c) in ((0, 0), (3, 0), (3, 2)) else chunks
                tile = sbuf("gate%d_%d" % (n, c), [P, width * CHUNK], F32)
                for place in range(width):
                    gate_tiles[n, c + place] = tile
                    for count in range(1, width - place + 1):
                        gates[n, c + place, count] = tile[:, columns(place, count)]
            nc.vector.tensor_copy(
                gates[n, c, chunks], gate_window[n][:].indirect(listed(c * CHUNK, chunks * CHUNK))
            )

        def on_gpsimd(n, c, o, chunks=1):
            values = results[n, o][:, columns(c, chunks)]
            nc.gpsimd.tensor_tensor(values, values, gates[n, c, chunks], MULT)

        def on_vector(n, c, o):
            nc.vector.tensor_tensor(results[n, o][:, columns(c)], banks[n, c, o][:], gates[n, c, 1], MULT)

        def store(n, c, o, chunks):
            nc.sync.dma_start(outs[o][n * P : (n + 1) * P, columns(c, chunks)], results[n, o][:, columns(c, chunks)])

        opening = [(n, c) for c in (0, 1) for n in range(ROW_TILES)]
        for step in (0, 1):
            for n, c in opening:
                mx_pass(n, c, 1, step)
        for n, c in sorted(opening, key=lambda s: s[0] // 2):
            mx_pass(n, c, 1, 2)
        for n, c in sorted(opening):
            mx_pass(n, c, 1, 3)
            empty(n, c, 1)

        def sum_for_vector(n, c, o):
            make_sum(n, c, o)
            on_vector(n, c, o)

        gather_gate(0, 0)
        gather_gate(0, 1)
        gather_gate(0, 2, 2)
        for c in (0, 1):
            sum_for_gpsimd(0, c, 0)
        for c in (0, 1):
            make_sum(1, c, 0)
        for c in (0, 1):
            on_gpsimd(0, c, 1)
        on_gpsimd(0, 0, 0, 2)
        for o in (1, 0):
            for c in (2, 3):
                sum_for_gpsimd(0, c, o)
            on_gpsimd(0, 2, o, 2)
            store(0, 0, o, 4)
        for c in (0, 2):
            gather_gate(1, c, 2)
        for c in (0, 1):
            on_vector(1, c, 0)
        for c in (2, 3):
            sum_for_vector(1, c, 0)
        for c in (2, 3):
            sum_for_gpsimd(1, c, 1)
        for c in (0, 2):
            on_gpsimd(1, c, 1, 2)
        for c, o, chunks in ((0, 0, 4), (0, 1, 2)):
            store(1, c, o, chunks)
        for c in (0, 2):
            gather_gate(2, c, 2)
        for c in (0, 1):
            sum_for_vector(2, c, 0)
        sum_for_gpsimd(2, 2, 1)
        for c in (2, 3):
            sum_for_vector(2, c, 0)
        sum_for_gpsimd(2, 3, 1)
        on_gpsimd(2, 0, 1, 2)
        for c in (2, 3):
            on_gpsimd(2, c, 1)
        for n, c, o in ((1, 2, 1), (2, 0, 0), (2, 0, 1), (2, 2, 0), (2, 2, 1)):
            store(n, c, o, 2)
        for c in (0, 1):
            gather_gate(3, c)
        for c in (0, 1):
            sum_for_vector(3, c, 0)
        on_gpsimd(3, 0, 1, 2)
        for o in (0, 1):
            store(3, 0, o, 2)
        for c in (2, 3):
            gather_gate(3, c)
        sum_for_gpsimd(3, 2, 1)
        on_gpsimd(3, 2, 1)
        for c, o in ((2, 0), (3, 0), (3, 1)):
            sum_for_vector(3, c, o)
        for c, o in ((2, 1), (2, 0), (3, 0), (3, 1)):
            store(3, c, o, 1)
